import numpy as np, ml_dtypes
CORES = [40,42,43,45,46]
N = 5
BF = ml_dtypes.bfloat16
def gentries(a):
    return np.ascontiguousarray(a.reshape(8, 16, -1).transpose(0, 2, 1)).reshape(8, -1)
def gtable(e):
    e = np.asarray(e); return np.ascontiguousarray(e.reshape(8, -1, 16).transpose(0, 2, 1)).reshape(128, -1).astype(np.int32)
NL, H, L, K, S, RO = 4096, 2048, 128, 8, 2, 6
MT = [32, 24, 40, 28, 48, 20]
AT = [8, 10, 7, 9, 6, 11]
def own(rng, c):
    return np.take_along_axis(c, rng.integers(0, K, (N, 8, 1, L)), 2)[:, :, 0]
def parts(rng):
    v = rng.integers(0, 256, (N, 8, 16, NL))
    g = 2 * np.argsort(rng.random((N, 8, 16, H)), axis=-1) + rng.integers(0, 2, (N, 8, 16, H))
    c = rng.integers(0, NL, (N, 8, K, L)); d = rng.integers(0, NL, (N, 8, K, L))
    return v, g, c, d, own(rng, c)
def pack(v, g, c, d, l):
    return {"val": np.ascontiguousarray(v.reshape(N, 128, NL)).astype(np.float32).astype(BF), "gen": np.ascontiguousarray(g.reshape(N, 128, H)).astype(np.int32),
            "cla": np.stack([gtable(a.reshape(8, -1)) for a in c]), "par": np.stack([gtable(a.reshape(8, -1)) for a in d]), "lit": np.stack([gtable(a) for a in l])}
def setup_inputs(rng):
    return pack(*parts(rng))
def setup_inputs_corners(rng):
    v, g, c, d, l = parts(rng)
    top = rng.random((N, 8, 1, NL)) < 1.0 / K
    v = np.where(top, rng.choice(np.array([222, 223, 224, 240, 255]), v.shape), rng.choice(np.array([0, 1, 31, 32, 33, 100]), v.shape))
    v[0, 6] = 0; v[1, 6] = 255
    g[:, 0, 3] = 2 * np.arange(H); g[:, 0, 15] = 2 * np.arange(H) + 1
    g[:, 1] = g[:, 1, :1].copy(); g[:, 2, ::4] = 0; g[:, 2, 1::4] = NL - 1
    c[..., 0::5] = d[..., 0::5]
    c[..., 1::5] = c[:, :, :1, 1::5].copy()
    c[:, :, 1::2, 2::5] = c[:, :, 0::2, 2::5] ^ 1
    e = c[..., 3::5]; c[..., 3::5] = rng.choice(np.array([0, 1, NL - 2, NL - 1]), e.shape)
    l[..., 0::3] = 0; l[..., 1::3] = NL - 1; l[..., 2::3] = c[:, :, K - 1, 2::3]
    return pack(v, g, c, d, l)
def setup_inputs_crowd(rng):
    v, g, c, d, l = parts(rng)
    for q in range(N):
        for s in range(8):
            w = 2 * rng.permutation(H)[:2 * K] + rng.integers(0, 2, 2 * K); c[q, s] = w[:K, None]; d[q, s] = w[K:, None]
            j = 15 if s == 7 else int(rng.integers(0, 16)); k = K - 1 if s == 0 else int(rng.integers(0, K))
            im = g[q, s, j, w[:K] >> 1] ^ (w[:K] & 1); both = np.concatenate([im, im ^ 1])
            v[q, s][:, both] = np.minimum(v[q, s][:, both], 100); v[q, s][:, im[k]] = 255; l[q, s] = im[k]
            if s in (2, 5):
                turn = rng.random(L) < 0.5; c[q, s] = np.where(turn, c[q, s] ^ 1, c[q, s]); v[q, s][:, im[k] ^ 1] = 255
            if s & 1:
                o = 0 if s == 1 else L - 1 if s == 7 else int(rng.integers(0, L))
                c[q, s, :, o] = int(c[q, s, 0, o]); d[q, s, :, o] = int(d[q, s, 0, o])
    return pack(v, g, c, d, l)
def endclauses(rng):
    E = np.array([0, NL - 1]); sh = (N, 8, 1, L); b = rng.integers(0, 2, sh); x = E[b]; y = E[1 - b]; kind = rng.integers(0, 4, sh)
    k1 = rng.integers(0, K, sh); k2 = (k1 + rng.integers(1, K, sh)) % K; k = np.arange(K).reshape(1, 1, K, 1)
    c = np.where(k == k1, y, x); c = np.where((kind == 2) & (k == k2), x ^ 1, c)
    return np.where(kind == 3, E[rng.integers(0, 2, (N, 8, K, L))], c)
def setup_inputs_ends(rng):
    E = np.array([0, NL - 1]); v = 255 * rng.integers(0, 2, (N, 8, 16, NL)); g = E[rng.integers(0, 2, (N, 8, 16, H))]
    c = endclauses(rng); d = endclauses(rng); l = E[rng.integers(0, 2, (N, 8, L))]
    for o, k in ((0, 0), (L - 1, K - 1)):
        c[:, :, :, o] = NL - 1; c[:, :, k, o] = 0
    h = (np.arange(16) < 8).astype(np.int64); on = np.ones(16, np.int64); no = 0 * on
    for q in range(N):
        for s in range(8):
            ty = (3 * q + s) % 6
            if q == N - 1 and s == 7: ty = 0
            if q in (0, 2) and s == 6: ty = 6
            four = [[on, no, no, on], [no, on, on, no], [h, no, no, 1 - h], [no, h, 1 - h, no], list(rng.integers(0, 2, (4, 16))), [on, no, no, on], [on, no, no, no]][ty]
            four = np.stack(four)
            if ty == 5: four[:, 13:] = rng.integers(0, 2, (4, 3))
            if ty == 6: g[q, s, :2, 0] = NL - 1; g[q, s, 2:, 0] = 0
            v[q, s][:, [0, 1, NL - 2, NL - 1]] = 255 * four.T
    return pack(v, g, c, d, l)
def setup_inputs_spread(rng):
    v, g, c, d, l = parts(rng)
    v = np.minimum((1.1 * np.exp2(8 * rng.random((N, 8, 1, NL))) * rng.random((N, 8, 16, NL))).astype(np.int64), 255)
    v[:, 1::2] = np.minimum((256 * rng.random((N, 4, 16, NL)) ** np.exp2(rng.integers(-1, 3, (N, 4, 16, 1)))).astype(np.int64), 255)
    g[:, :, ::2] = 2 * np.minimum((H * rng.random((N, 8, 8, H)) ** 3).astype(np.int64), H - 1) + rng.integers(0, 2, (N, 8, 8, H))
    p = rng.choice(np.array([1, 2, 4]), (N, 8, 1, 1))
    c = np.minimum((NL * rng.random((N, 8, K, L)) ** p).astype(np.int64), NL - 1); d = NL - 1 - np.minimum((NL * rng.random((N, 8, K, L)) ** p).astype(np.int64), NL - 1)
    l = np.where(rng.random((N, 8, L)) < 0.5, own(rng, c), own(rng, d))
    return pack(v, g, c, d, l)
def apart(rng, v, g, c, d, l, s, one):
    w = rng.permutation(H); z = 2 * w[:L] + rng.integers(0, 2, L); r = w[L:]; m = np.zeros(H, np.int64)
    m[z >> 1] = np.roll(z, -1) ^ (z & 1); m[r] = 2 * rng.permutation(r) + rng.integers(0, 2, H - L); g[:, s, 0] = m
    v[:, s] = np.minimum(v[:, s], 100); v[:, s][:, :, z] = 255; v[:, s][:, :, z ^ 1] = rng.integers(200, 256, (N, 16, L))
    c[:, s] = 2 * r[rng.integers(0, H - L, (N, K, L))] + rng.integers(0, 2, (N, K, L))
    for q in range(N):
        y = rng.permutation(z); c[q, s, rng.integers(0, K, L), np.arange(L)] = y; l[q, s] = y
        if one:
            o = L - 1 if q == N - 1 else int(rng.integers(0, L))
            c[q, s, :, o] = int(c[q, s, 0, o]); d[q, s, :, o] = int(d[q, s, 0, o])
def setup_inputs_ties(rng):
    v, g, c, d, l = parts(rng); m = np.array(MT)[np.arange(8) % RO].reshape(1, 8, 1, 1); u = K * rng.random((N, 8, 1, NL))
    low = (rng.random(v.shape) * (255 - m)).astype(np.int64)
    w = np.where(u < 1, 255, np.where(u < 1.3, 255 - m, np.where(u < 4, 254 - m, low)))
    v = np.where(rng.random(v.shape) < 0.02, v, w)
    h = (np.arange(16) < 8).astype(np.int64).reshape(16, 1); x = u[:, [2, 5]]
    v[:, [2, 5]] = np.where(x < 1, 255 * h, np.where(x < 2, 255 * (1 - h), np.minimum(low[:, [2, 5]], 100)))
    eq = rng.random((N, 8, 1, H)) < 0.25; v[..., 1::2] = np.where(eq, v[..., 0::2], v[..., 1::2])
    apart(rng, v, g, c, d, l, 6, False); apart(rng, v, g, c, d, l, 7, True)
    return pack(v, g, c, d, l)
def check_inputs(d):
    bad = []
    for k, lo, hi in (("val", 0, 255), ("gen", 0, NL - 1), ("cla", 0, NL - 1), ("par", 0, NL - 1), ("lit", 0, NL - 1)):
        a = np.asarray(d[k]).astype(np.float64)
        if not (np.min(a) >= lo and np.max(a) <= hi): bad.append("range of " + k)
        elif np.any(a != np.floor(a)): bad.append("whole numbers of " + k)
    return bad
def reference(val, gen, cla, par, lit):
    V = val.astype(np.float32).astype(np.int16).reshape(N, 8, 16, NL)
    e = gen.astype(np.int64).reshape(N, 8, 16, H); P = np.stack([e, e ^ 1], axis=-1).reshape(N, 8, 16, NL)
    C = np.stack([gentries(a) for a in cla]).astype(np.int64).reshape(N, 8, K, L); D = np.stack([gentries(a) for a in par]).astype(np.int64).reshape(N, 8, K, L)
    l = np.stack([gentries(a) for a in lit]).astype(np.int64); A = np.zeros((N, 8), np.int64)
    for t in range(RO):
        if t: C = np.roll(C, S, axis=0); D = np.roll(D, S, axis=0); l = np.roll(l, S, axis=0)
        for a in range(N):
            v = V[a]; x = l[a][:, None, :]
            less = np.take_along_axis(v, x, 2) < np.take_along_axis(v, x ^ 1, 2)
            c = np.where((np.add.reduce(less.astype(np.int64), axis=1) >= 9)[:, None, :], D[a], C[a])
            img = np.take_along_axis(P[a], c.reshape(8, 1, K * L), 2)
            w = np.take_along_axis(v, img.reshape(8, 1, 16 * K * L), 2).reshape(8, 16, 16, K, L)
            near = w >= np.max(w, axis=3)[:, :, :, None] - MT[t]
            unit = np.add.reduce(near, axis=3, dtype=np.int16) == 1
            votes = np.add.reduce(unit.astype(np.int64), axis=1); js = np.argmax(votes, axis=1)
            pro = np.max(votes, axis=1) >= (AT[t] + (A[a] & 1))[:, None]
            new = np.take_along_axis(img.reshape(8, 16, K, L), js[:, None, None, :], 1)[:, 0]
            un = np.take_along_axis(unit, js[:, None, None, :], 2)[:, :, 0]
            vn = np.take_along_axis(v, new.reshape(8, 1, K * L), 2).reshape(8, 16, K, L).astype(np.int64)
            ks = np.argmax(np.add.reduce(np.where(un[:, :, None, :], vn, 0), axis=1), axis=1)
            nl = np.take_along_axis(new, ks[:, None, :], 1)[:, 0]
            C[a] = np.where(pro[:, None, :], new, D[a]); D[a] = c; l[a] = np.where(pro, nl, l[a])
            for g in range(8):
                z = nl[g, np.flatnonzero(pro[g])]
                z = z[np.unique(z >> 1, return_index=True)[1]]
                up = np.minimum(v[g][:, z] + 32, 255); down = np.maximum(v[g][:, z ^ 1] - 32, 0)
                v[g][:, z] = up; v[g][:, z ^ 1] = down
            A[a] = np.add.reduce(pro.astype(np.int64), axis=1)
    return {"yv": V.reshape(N, 128, NL).astype(np.float32).astype(BF), "yc": np.stack([gtable(a.reshape(8, -1)) for a in C]).astype(np.float32),
            "yd": np.stack([gtable(a.reshape(8, -1)) for a in D]).astype(np.float32), "yl": np.stack([gtable(a) for a in l]).astype(np.float32)}

@@ -1,0 +1,699 @@
+import numpy as np
+from concourse.mybir import AluOpType as ALU, ActivationFunctionType as AF
+
+RO, STEP = 6, 2
+MT = [32, 24, 40, 28, 48, 20]
+AT = [8, 10, 7, 9, 6, 11]
+PAR = {
+    "chs": [[1024] * 4, [1024] * 4],
+    "last": [[1024] * 4, [1024] * 3, [512, 512]],
+    "dveg": ((0, 0, 2), (0, 0, 5), (5, 1, 4)),
+    "head": 128,
+    "hot": 2,
+    "g1": "act",
+    "up": "act",
+    "seed": 1,
+    "steps": 2800,
+}
+CW = 1024
+ENG = 16
+BIG = 100
+F, B, I, U = "float32", "bfloat16", "int32", "uint16"
+MW = 112
+
+SCRATCH = {
+    "cin": ("sbuf", [128, 136], I), "cinf": ("sbuf", [128, 136], F),
+    "pidx": ("sbuf", [128, 16], I), "pf": ("sbuf", [128, 16], F),
+    "ones": ("sbuf", [128, 160], F), "If": ("sbuf", [128, 128], F), "nIf": ("sbuf", [128, 128], F),
+    "nBig": ("sbuf", [128, 128], F), "pBig": ("sbuf", [128, 128], F), "Ib": ("sbuf", [128, 128], B), "nIb": ("sbuf", [128, 128], B),
+    "SW0": ("sbuf", [128, 160], F), "SW1": ("sbuf", [128, 160], F), "Z0": ("sbuf", [128, 130], F), "Z1": ("sbuf", [128, 130], F),
+    "In0": ("sbuf", [128, 160], F), "In1": ("sbuf", [128, 160], F), "Out": ("sbuf", [128, 128], F), "Hs": ("sbuf", [128, 256], F),
+    "rows": ("sbuf", [128, 800], F), "WW": ("sbuf", [128, 144], B), "VB": ("sbuf", [128, 144], B),
+    "S10": ("sbuf", [128, 160], B), "S11": ("sbuf", [128, 160], B), "B32": ("sbuf", [128, 128], F), "dl": ("sbuf", [128, 128], F),
+    "o64": ("sbuf", [128, 128], B), "CK": ("sbuf", [128, 512], B), "TB": ("sbuf", [128, 32], B),
+    "m8": ("sbuf", [128, CW], B), "zb": ("sbuf", [128, 128], B), "m8s": ("sbuf", [128, 32], B), "m16": ("sbuf", [128, 512], B), "m128": ("sbuf", [128, 512], B),
+    "sm": ("sbuf", [128, 160], F), "su": ("sbuf", [128, 16], U), "Hb": ("sbuf", [128, 256], B),
+    "w": ("sbuf", [128, 8192], B), "Q": ("sbuf", [128, 8192 + 512], B), "z": ("sbuf", [128, 8192], B),
+}
+for _s in "01":
+    SCRATCH.update({
+        "V" + _s: ("sbuf", [128, 4352], B), "G" + _s: ("sbuf", [128, 2048], I), "P" + _s: ("sbuf", [128, 4096], F),
+        "tmp" + _s: ("sbuf", [128, 1024], F),
+        "lo" + _s: ("sbuf", [128, 16], B), "g2" + _s: ("sbuf", [128, 64], B),
+        "usg" + _s: ("sbuf", [128, 1024], B), "img" + _s: ("sbuf", [128, 512], F), "imT" + _s: ("sbuf", [128, 512], F),
+        "of" + _s: ("sbuf", [128, 512], U), "ks" + _s: ("sbuf", [128, 512], F),
+        "um" + _s: ("sbuf", [128, 512], B), "pr" + _s: ("sbuf", [128, 512], B),
+        "ab" + _s: ("sbuf", [128, 512], B), "mn" + _s: ("sbuf", [128, 512], B),
+        "X" + _s: ("sbuf", [128, 128], F), "nv" + _s: ("sbuf", [128, 256], B), "g1" + _s: ("sbuf", [128, 128], B),
+        "f" + _s: ("sbuf", [128, 640], F), "n" + _s: ("sbuf", [128, 128], I), "u" + _s: ("sbuf", [128, 160], U),
+        "land" + _s: ("sbuf", [128, RO * MW], F), "msg" + _s: ("sbuf", [128, RO * MW], F),
+        "pa" + _s: ("psum", [128, 512], F), "pb" + _s: ("psum", [128, 512], F),
+        "pc" + _s: ("psum", [128, 512], F), "pd" + _s: ("psum", [128, 512], F),
+    })
+SEMAPHORES = (["act", "dve", "pe", "pool", "sent", "ldc", "fin"] + ["ld%s%d" % (k, s) for k in "ghv" for s in range(2)]
+              + ["arr%d_%d" % (t, s) for t in range(1, RO) for s in range(2)])
+
+HALF = 21.0
+ROUND = ("97c 180 76a 121 142c 1a 135 161d 86a 164d 166 168 170d 221 70b 194 372c 244d 339c 459a 156c 135c 106c 251b 130a 218b 232b 156 242b "
+         "153c 232 138d 279 282a 127b 266 278 376 267 233 65c 402 324d 294 445c 327 340d 354d 368 241 493 233a 179d 182d 245 268b 288d 396b "
+         "305a 346 351a 319 332b 330 303b 265a 337a 322d 339d 332b 334 375a 387b 336c 193 345c 353b 492b 395d 447d 364c 452 346d 369 519 358 "
+         "333c 381 367b 449b 308 369d 482c 228d 363d 433d 457d 431 386b 480a 350a 328b 451 398 473d 632c 451a 440 506d 328b 496b 559c 520 490 "
+         "526d 291c 484d 488d 513c 527 460 533a 523 565c 567a 696c 662b")
+DUE = {(p, q): (int(x.rstrip("abcd")) / 10.0, {"a": 0.1, "b": 0.2, "c": 0.4, "d": 0.8}.get(x[-1], 0.0))
+       for p in "abmy" for q, x in enumerate(ROUND.split())}
+SPREAD = [(1.25, 1.56, 3.8, .06, .08, 2.6), (1.25, 1.56, 3.8, .02, .15, 3.5), (1.1, 1.2, 5, .04, .1, 2.5), (1.4, 1.9, 2.5, .05, .06, 4.5),
+          (1.1, 1.9, 4.5, .03, .2, 3.0), (1.4, 1.2, 3, .0, .05, 2.0), (1.25, 1.56, 3.8, .045, .11, 3.3)]
+CYC = 0.00083 * 1.25
+COST = {"cyc": CYC, "gat": 1.56, "sca": 3.8, "fix": 0.06, "lat": 0.08, "rem": 2.6, "dma": 2.0, "bw": 200e3}
+
+
+def build(g, core, T, topo):
+    rank = T.rank_of(core)
+    n = len(T.cores)
+    dst = T.cores[(rank + STEP) % n]
+    ops = []
+    ctx = {"pri": (0, 0, 0), "ts": None, "seen": [0], "all": [0]}
+
+    def R(name, a=None, b=None, st=1, p0=0, p1=128):
+        shp = SCRATCH[name][1]
+        if a is None:
+            a, b = 0, shp[1]
+        return (T[name][p0:p1, a:b:st] if st != 1 else T[name][p0:p1, a:b], name, a, b, (b - a + st - 1) // st)
+
+    def two(*v):
+        return all(SCRATCH[x[1]][2] in (B, U) for x in v)
+
+    def ps(v):
+        return SCRATCH[v[1]][0] == "psum"
+
+    def op(eng, fn, rd, wr, kind, amt, sem=None, cnt=0, after=None):
+        ops.append({"e": eng, "fn": fn, "rd": [x[1:4] for x in rd], "wr": [x[1:4] for x in wr], "k": kind, "n": amt,
+                    "sem": sem, "cnt": cnt, "pri": ctx["pri"], "ts": ctx["ts"], "key": None, "i": len(ops)})
+        part = {None: "x", (0, 0): "a", (0, 1): "b", (RO - 1, 0): "y", (RO - 1, 1): "z"}.get(ctx["ts"], "m")
+        seen = ctx["all"] if part == "x" else ctx["seen"]
+        seen[0] += 1
+        ops[-1]["key"] = (part, seen[0] - 1)
+        return ops[-1]
+
+    def ind(win, off):
+        return (win[0].indirect(off[0]), win[1], win[2], win[3], off[4] * 16, off)
+
+    def rds(*v):
+        out = []
+        for x in v:
+            if isinstance(x, tuple):
+                out.append(x)
+                if len(x) > 5:
+                    out.append(x[5])
+        return out
+
+    def ap(x):
+        return x[0] if isinstance(x, tuple) else x
+
+    def vcost(o, i, rate):
+        if len(i) > 5:
+            return "gat", i[4]
+        if len(o) > 5:
+            return "sca", o[4]
+        return "cyc", max(64, rate * i[4])
+
+    def copy(o, i):
+        k, a = vcost(o, i, 0.5 if two(o, i) else 1)
+        op("dve", lambda: g.vector.tensor_copy(o[0], i[0]), rds(i) + rds(o)[1:], [o], k, a)
+
+    def tt(o, a, b, alu):
+        k, c = vcost(o, a, 1 if ps(a) or ps(b) else 2)
+        op("dve", lambda: g.vector.tensor_tensor(o[0], a[0], b[0], alu), rds(a, b), [o], k, c)
+
+    def ts(o, a, s1, s2, o0, o1=None):
+        k, c = vcost(o, a, 0.5 if two(o, a) else 1)
+        if o1 is None:
+            op("dve", lambda: g.vector.tensor_scalar(o[0], a[0], ap(s1), None, o0), rds(a, s1), [o], k, c)
+        else:
+            op("dve", lambda: g.vector.tensor_scalar(o[0], a[0], ap(s1), ap(s2), o0, o1), rds(a, s1, s2), [o], k, c)
+
+    def scan(o, d0, d1, o0, o1):
+        op("dve", lambda: g.vector.tensor_tensor_scan(o[0], d0[0], d1[0], 0.0, o0, o1), rds(d0, d1), [o], "cyc",
+           max(64, (0.5 if two(o, d0, d1) else 1) * o[4]))
+
+    def tr(o, i):
+        op("dve", lambda: g.vector.transpose(o[0], i[0]), [i], [o], "cyc", max(64, i[4]))
+
+    def mset(o, v):
+        op("dve", lambda: g.vector.memset(o[0], v), [], [o], "cyc", max(64, (0.5 if two(o) else 1) * o[4]))
+
+    def act(o, i, fn, bias=0.0, scale=1.0):
+        k, c = vcost(o, i, 1)
+        op("act", lambda: g.scalar.activation(o[0], i[0], fn, bias=ap(bias), scale=scale), rds(i, bias), [o], k, c)
+
+    def mm(*terms, start=True, stop=True):
+        def fn():
+            last = None
+            for q, (o, l, r) in enumerate(terms):
+                last = g.tensor.matmul(o[0], l[0], r[0], start and q == 0, stop and q == len(terms) - 1)
+            return last
+        c = sum(max(64, r[4]) * (1 if two(l) else 4) for o, l, r in terms)
+        op("pe", fn, [x for t in terms for x in t[1:]], [t[0] for t in terms], "pe", c)
+
+    def iota(o, pat, base, cm=0):
+        if SCRATCH[o[1]][2] == I:
+            op("pool", lambda: g.iota(o[0], pat, base, cm), [], [o], "cyc", 130 + 2 * o[4])
+        else:
+            op("pool", lambda: g.iota(o[0], pat, base, cm, allow_small_or_imprecise_dtypes=True), [], [o], "cyc", 130 + 2 * o[4])
+
+    def perm(o, pat, base):
+        i = R("ones", 0, o[4])
+        op("pool", lambda: g.affine_select(o[0], i[0], [[-a, c] for a, c in pat], ALU.is_equal, 0.0, -base, 1), [i], [o], "cyc", 170 + 2 * o[4])
+
+    def dmas(eng, pairs, rd, wr, sem, nbytes):
+        q = {"sp": g.sync, "act": g.scalar}[eng]
+
+        def fn():
+            for o, i in pairs:
+                q.dma_start(o, i).then_inc(T.sem[sem], 16)
+        return op(eng, fn, rd, wr, "dma", (len(pairs), nbytes), sem=sem, cnt=16 * len(pairs))
+
+    dmas("sp", [(T.cin[:, 0:64], T.cla[:]), (T.cin[:, 64:128], T.par[:]), (T.cin[:, 128:136], T.lit[:])], [], [R("cin")], "ldc", 70e3)
+    for s in range(2):
+        S = str(s)
+        hv = [(32 * G + 16 * h, 64 * s + 16 * G) for G in range(4) for h in range(2)]
+        for q in range(2):
+            dmas("act" if s == 0 and q == 0 else "sp", [(T["G" + S][a:a + 16, 1024 * q:1024 * q + 1024], T.gen[b:b + 16, 1024 * q:1024 * q + 1024]) for a, b in hv],
+                 [], [R("G" + S, 1024 * q, 1024 * q + 1024)], "ld%s%d" % ("gh"[q], s), 1 << 19)
+        dmas("act" if s == 0 else "sp", [(T["V" + S][a:a + 16, 0:4096], T.val[b:b + 16, :]) for a, b in hv], [], [R("V" + S, 0, 4096)], "ldv" + S, 1 << 20)
+
+    ctx["pri"] = (0, -1, 0)
+    mset(R("ones"), 1.0)
+    iota(R("pidx", 0, 1), [[0, 1]], 0, 1)
+    perm(R("In0"), [[16, 5], [-1000, 2], [1, 16]], 1000)
+    iota(R("rows", 0, 160), [[2, 5], [-BIG, 4], [0, 8]], 3 * BIG)
+    perm(R("If"), [[1, 128]], 0)
+    fld = {"blk": (4, 7), "G": (5, 3), "p31": (0, 31), "r15": (0, 15), "ht": (4, 1), "y0": (0, 1), "k7": (0, 7), "b": (3, 1), "p3": (0, 3)}
+    col = {}
+    for q, (nm, (sh, ms)) in enumerate(fld.items()):
+        ts(R("pidx", q + 1, q + 2), R("pidx", 0, 1), sh, ms, ALU.logical_shift_right, ALU.bitwise_and)
+        col[nm] = R("pf", q + 1, q + 2)
+    copy(R("pf", 0, 10), R("pidx", 0, 10))
+    copy(R("cinf"), R("cin"))
+    for bt in range(2):
+        ts(R("S1%d" % bt), R("rows", 0, 160), float(bt), col["blk"], ALU.add, ALU.is_equal)
+    ts(R("nIf"), R("If"), -1.0, None, ALU.mult)
+    for s in range(2):
+        mset(R("V%d" % s, 4096, 4352), 0.0)
+    ctx["pri"] = (0, 0, 5)
+    perm(R("SW0"), [[32, 5], [-1000, 2], [1, 16]], 1000)
+    perm(R("SW1"), [[32, 5], [1000, 2], [1, 16]], -16)
+    perm(R("In1"), [[16, 5], [-1000, 2], [1, 16]], 1064)
+    mset(R("m8"), 1.0)
+    mset(R("m8", 0, CW, 8), 0.0)
+    mset(R("zb"), 0.0)
+    def cut(chs):
+        out, at = [], 0
+        for grp in chs:
+            out.append([])
+            for cw in grp:
+                out[-1].append((sum(map(len, out)), at, cw, at + at // 16 + 16))
+                at += cw
+        return out
+    zeros = [x[3] - 1 for grp in cut(PAR["chs"]) for x in grp]
+    mset(R("Q", 15, 8192 + 512, 272), 0.0)
+    turn = [0]
+    copy(R("Ib"), R("If"))
+    copy(R("nIb"), R("nIf"))
+    ctx["pri"] = (1, 0, 0)
+    iota(R("rows", 160, 304), [[1, 9], [-BIG, 2], [0, 8]], BIG)
+    ts(R("VB"), R("rows", 160, 304), col["blk"], 65536.0, ALU.is_equal, ALU.mult)
+    iota(R("CK", p1=64), [[0, 32], [-4096, 16]], 15 * 4096)
+    mset(R("CK", p0=64), float(1 << 20))
+    mset(R("o64"), 1.0 / 64)
+    mset(R("m16"), 1.0)
+    mset(R("m16", 0, 512, 16), 0.0)
+    iota(R("rows", 304, 448), [[1, 9], [-BIG, 16]], 15 * BIG)
+    ts(R("WW"), R("rows", 304, 448), col["blk"], None, ALU.is_equal)
+    iota(R("rows", 704, 736), [[32, 32]], 30)
+    ubase = R("sm", 0, 32)
+    ts(ubase, R("rows", 704, 736), col["b"], None, ALU.add)
+    ts(R("pf", 10, 11), col["k7"], -0.125, 0.875, ALU.mult, ALU.add)
+    ts(R("TB"), R("ones", 0, 32), R("pf", 10, 11), None, ALU.mult)
+    mset(R("m8s"), 1.0)
+    mset(R("m8s", 0, 32, 8), 0.0)
+    perm(R("Z0"), [[2, 65], [-1000, 2]], 1000)
+    perm(R("Z1"), [[2, 65], [1000, 2]], -1)
+    act(R("nBig"), R("If"), AF.Identity, 0.0, -8192.0)
+    act(R("pBig"), R("If"), AF.Identity, 0.0, 8192.0)
+    iota(R("rows", 448, 576), [[1, 4], [0, 32]], 0)
+    ts(R("B32"), R("rows", 448, 576), col["G"], None, ALU.is_equal)
+    iota(R("rows", 576, 704), [[0, 4], [1, 32]], 0)
+    ts(R("dl"), R("rows", 576, 704), col["p31"], None, ALU.is_equal)
+    for ht in range(2):
+        perm(R("Hs", 128 * ht, 128 * ht + 128), [[32, 4], [0, 2], [1, 16]], 16 * ht)
+    mset(R("m128"), 0.0)
+    mset(R("m128", 0, 512, 128), float(1 << 23))
+    iota(R("rows", 736, 752), [[0, 4], [1, 2], [16, 2]], 0)
+    iota(R("rows", 752, 768), [[0, 4], [32, 2], [16, 2]], 0)
+    iota(R("rows", 768, 776), [[1, 4], [0, 2]], 0)
+    ts(R("pf", 11, 12), col["ht"], 64.0, col["r15"], ALU.mult, ALU.add)
+    ts(R("pf", 12, 13), col["y0"], 31.0, R("pf", 11, 12), ALU.mult, ALU.add)
+    lane = []
+    for par in range(2):
+        lane.append(R("sm", 32 + 32 * par, 48 + 32 * par))
+        ts(lane[par], R("rows", 736 + 16 * par, 752 + 16 * par), R("pf", 12 - par, 13 - par), 1.0 / 64, ALU.add, ALU.mult)
+    iota(R("rows", 776, 792), [[16, 16]], 4096)
+    dum = R("sm", 96, 112)
+    ts(dum, R("rows", 776, 792), col["r15"], None, ALU.add)
+    copy(R("Hb"), R("Hs"))
+    for c in range(2):
+        ts(R("su", c, c + 1), col["b"], 8.0, 16.0 * c + 7, ALU.mult, ALU.add)
+    ts(R("su", 2, 3), col["p3"], 128.0, 127.0, ALU.mult, ALU.add)
+    copy(R("su", 4, 12), R("rows", 768, 776))
+    for u in range(2):
+        perm(R("Out", 64 * u, 64 * u + 64), [[32, 4], [1, 16]], 16 * u)
+
+    def other(lv, lo, t1, t2):
+        ts(t1, lv, 2.0 - 2.0 ** -12, 2.0 ** 25, ALU.mult, ALU.add)
+        ts(t2, t1, -2.0 ** 25, 1.0, ALU.add, ALU.add)
+        tt(lo, t2, lv, ALU.subtract)
+
+    def stream(s):
+        S = str(s)
+
+        def r(name, *a, **k):
+            return R(name + S, *a, **k)
+        Vw = r("V")
+        ctx["pri"] = (0, 0, 0) if s == 0 else (1, 0, 8)
+        for q in range(4):
+            ev = r("P", 1024 * q, 1024 * q + 1024, 2)
+            ts(ev, r("G", 512 * q, 512 * q + 512), -0.5, None, ALU.add)
+            tm = r("tmp", 512 * (q % 2), 512 * (q % 2) + 512)
+            act(tm, ev, AF.Identity, 2.0 ** 25, 2.0)
+            pu = r("pb") if q % 2 else R("pa0") if s == 0 else r("pc")
+            act(pu, tm, AF.Identity, -2.0 ** 25)
+            tt(r("P", 1024 * q + 1, 1024 * q + 1024, 2), pu, ev, ALU.subtract)
+        ctx["pri"] = (0, 0, s)
+        for w in range(2):
+            for yb in range(4):
+                mm(*[(r("pc", 32 * w + 8 * yb, 32 * w + 8 * yb + 8), R("In" + S, 16 - 16 * u, 144 - 16 * u),
+                      R("cinf", 64 * w + 4 * u + yb, 64 * w + 64, 8)) for u in range(2)])
+        tr(r("land", 0, 64), r("pc", 0, 64))
+        mm(*[(r("pd", 0, 4), R("In" + S, 16 - 16 * u, 144 - 16 * u), R("cinf", 128 + 4 * u, 132 + 4 * u)) for u in range(2)])
+        copy(r("land", 64, 68), r("pd", 0, 4))
+        other(r("land", 64, 68), r("land", 68, 72), r("f", 400, 404), r("f", 408, 412))
+        thr = r("f", 416, 417)
+        mset(thr, float(((AT[0] - 1) * 32 + 16) * 4096))
+
+        for t in range(RO):
+            par = t % 2
+            chain = (0, t, s)
+            ctx["pri"] = chain
+            ctx["ts"], ctx["seen"] = (t, s), [0]
+            L0, M0 = t * MW, t * MW + 32
+            C, D = r("land", L0, L0 + 32), r("land", L0 + 32, L0 + 64)
+            copy(r("u", 0, 8), r("land", L0 + 64, L0 + 72))
+            mm((r("pc", 0, 32), R("If"), D), (r("pc", 0, 32), R("nIf"), C))
+            if PAR["g1"] == "act":
+                act(r("g1", 0, 64), ind(Vw, r("u", 4, 8)), AF.Identity)
+            else:
+                copy(r("g1", 0, 64), ind(Vw, r("u", 4, 8)))
+            tt(r("g2"), ind(Vw, r("u", 0, 4)), r("g1", 0, 64), ALU.is_lt)
+            for bt in range(2):
+                mm(*[(r("pc", 32 + 16 * bt, 48 + 16 * bt), R("S1%d" % bt, 24 - 8 * yb, 152 - 8 * yb),
+                      r("g2", 16 * yb, 16 + 16 * yb)) for yb in range(4)])
+            ts(r("f", 0, 32), r("pc", 32, 64), 8.5, None, ALU.is_ge)
+            tt(r("f", 32, 64), r("f", 0, 32), r("pc", 0, 32), ALU.mult)
+            tt(C, r("f", 32, 64), C, ALU.add)
+            copy(r("u", 16, 48), C)
+            for a, b in ((0, PAR["head"]), (PAR["head"], 512)):
+                act(r("img", a, b), ind(r("P"), r("u", 16 + a // 16, 16 + b // 16)), AF.Identity, 0.5)
+                tr(r("imT", a, b), r("img", a, b))
+                copy(r("of", a, b), r("imT", a, b))
+            ctx["pri"] = (1, t, s, -1)
+            for y in range(2):
+                mm(*[(r("pd", y, 64, 2), R("SW%d" % y, 16 - 16 * (x - y), 144 - 16 * (x - y)), r("land", L0 + x, L0 + 64, 2)) for x in range(2)])
+            act(r("f", 96, 128), r("pd", 32, 64), AF.Identity, thr)
+            act(r("msg", M0 + 32, M0 + 64), r("pd", 0, 32), AF.Identity)
+            chunks = cut(PAR["last"] if (t, s) == (RO - 1, 1) else PAR["chs"])
+            nch = sum(map(len, chunks))
+            for grp in chunks:
+                ctx["pri"] = (1, t, s, grp[0][0])
+                u0, u1 = grp[0][1] // 8, (grp[-1][1] + grp[-1][2]) // 8
+                pa = "pa%d" % (turn[0] % 2)
+                turn[0] += 1
+                mm((R(pa, 0, u1 - u0), R("zb"), R("m16", 0, u1 - u0)), stop=False)
+                kv = r("pb", u0 // 2, u1 // 2)
+                mm((kv, R("If"), r("imT", u0 // 2, u1 // 2)), (kv, R("o64"), R("CK", u0 // 2, u1 // 2)), stop=False)
+
+                def second(c, a, cw, q):
+                    scan(R("z", a, a + cw), R("w", a, a + cw), R("Q", q - 1, q - 1 + cw), ALU.max, ALU.min)
+                    mm((R(pa, a // 8 - u0, (a + cw) // 8 - u0), R("nIb"), R("z", a + 7, a + cw, 8)), start=False, stop=c == grp[-1][0])
+                for q0, (c, a, cw, q) in enumerate(grp):
+                    ctx["pri"] = (1, t, s, c)
+                    wv = R("w", a, a + cw)
+                    src = ind(Vw, r("of", a // 16, (a + cw) // 16))
+                    if (t, s, c) in PAR["dveg"]:
+                        copy(wv, src)
+                    else:
+                        act(wv, src, AF.Identity)
+                    if c >= nch - PAR["hot"]:
+                        ctx["pri"] = chain
+                    if q - 1 not in zeros:
+                        iota(R("Q", q - 1, q), [[0, 1]], 0)
+                    scan(R("Q", q, q + cw), R("m8", 0, cw), wv, ALU.mult, ALU.max)
+                    top = R("Q", q + 7, q + cw, 8)
+                    mm((R(pa, a // 8 - u0, (a + cw) // 8 - u0), R("Ib"), top), start=False, stop=False)
+                    if c == nch - 1:
+                        mset(top, 0.0)
+                    else:
+                        iota(top, [[0, cw // 8]], 0)
+                    if q0:
+                        second(*grp[q0 - 1])
+                second(*grp[-1])
+                act(r("usg", u0, u1), R(pa, 0, u1 - u0), AF.Sign, -MT[t] - 0.5)
+                mm(*[(kv, R("VB", 8 - 8 * b, 136 - 8 * b), r("usg", u0 + b, u1, 2)) for b in range(2)], start=False)
+                scan(r("ks", u0 // 2, u1 // 2), R("m16", u0 // 2, u1 // 2), kv, ALU.mult, ALU.max)
+            ctx["pri"] = chain
+            km, nC = r("n", 0, 32), r("n", 32, 64)
+            tt(km, r("ks", 15, 512, 16), r("f", 96, 128), ALU.max)
+            ts(r("n", 96, 128), km, 11, 30, ALU.logical_shift_right, ALU.bitwise_and)
+            ts(nC, km, 4095, None, ALU.bitwise_and)
+            tt(r("n", 64, 96), ubase, r("n", 96, 128), ALU.subtract)
+            copy(r("u", 48, 112), r("n", 32, 96))
+            act(r("um"), ind(r("usg"), r("u", 80, 112)), AF.Relu)
+            tt(r("pr"), ind(Vw, r("u", 48, 80)), r("um"), ALU.mult)
+            copy(r("msg", M0, M0 + 32), nC)
+            stay = r("msg", M0 - 32, M0)
+            ts(stay, km, -4096.0, thr, ALU.add, ALU.is_lt)
+            tr(r("f", 192, 256), r("msg", M0 - 32, M0 + 32))
+            st3 = r("f", 192, 224, 8)
+            mm((r("pc", 64, 96), R("Ib"), R("TB")), (r("pc", 64, 96), R("nBig"), stay), stop=False)
+            mm(*([(r("pd", 64, 68), R("pBig"), st3), (r("pd", 64, 68), R("nBig"), R("ones", 0, 4))]
+                 + [(r("pd", 64 + 2 * x, 66 + 2 * x), R("Z%d" % x, 1 - (y - x), 129 - (y - x)), r("land", L0 + 64 + 2 * y, L0 + 66 + 2 * y))
+                    for x in range(2) for y in range(2)]))
+            mm((r("pd", 72, 76), R("pBig"), st3), (r("pd", 72, 76), R("If"), R("sm", 32 + 32 * par, 36 + 32 * par)))
+            mm(*[(r("pc", 64, 96), R("WW", 15 - p, 143 - p), r("pr", p, 512, 16)) for p in range(16)], start=False)
+            tr(r("f", 256, 288), r("pc", 64, 96))
+            scan(r("f", 288, 320), R("m8s"), r("f", 256, 288), ALU.mult, ALU.max)
+            tt(r("f", 320, 352), ind(r("f", 288, 320), R("su", 0, 2)), r("f", 256, 288), ALU.is_equal)
+            tt(r("f", 352, 384), r("f", 320, 352), r("f", 224, 256), ALU.mult)
+            scan(r("f", 256, 288), R("m8s"), r("f", 352, 384), ALU.mult, ALU.add)
+            lv, lo, ll = r("msg", M0 + 64, M0 + 68), r("msg", M0 + 68, M0 + 72), r("msg", M0 + 64, M0 + 72)
+            tt(lv, r("f", 263, 288, 8), r("pd", 64, 68), ALU.max)
+            other(lv, lo, r("f", 400, 404), r("f", 408, 412))
+            if t + 1 < RO:
+                src, la = r("msg", M0, M0 + 72), r("land", L0 + MW, L0 + MW + 72)
+                rid, pid, _ = topo.addr(dst)
+                en = topo.engines(core, dst)[:ENG]
+                mask = sum(1 << e for e in en)
+                sem = "arr%d_%d" % (t + 1, s)
+
+                def send(src=src, la=la, sem=sem, mask=mask, rid=rid, pid=pid):
+                    g.remote_dma(la[0], src[0], T.sem[sem], T.sem.sent, pid, rid, mask)
+                op("pool", send, [src], [la], "rem", len(en), sem=sem, cnt=len(en))
+            kk = r("f", 448, 452)
+            tt(kk, r("f", 408, 412), r("pd", 72, 76), ALU.add)
+            tt(r("X"), ind(kk, R("su", 4, 12)), R("dl"), ALU.mult)
+            mm((r("pc", 128, 256), R("B32"), r("X")))
+            for ht in range(2):
+                mm((r("pd", 80 + ht, 96, 2), R("Hs", 128 * ht, 128 * ht + 128), ll))
+            for c in range(4):
+                act(r("ab", 128 * c, 128 * c + 128), r("pc", 128, 256), AF.Abs, r("f", 408 + c, 409 + c), -1.0)
+            copy(r("u", 112, 128), r("pd", 80, 96))
+            if PAR["up"] == "dve" or (t, s) == (RO - 1, 1):
+                ts(r("nv", 0, 128), ind(Vw, r("u", 112, 120)), 32.0, 255.0, ALU.add, ALU.min)
+            else:
+                act(r("g1"), ind(Vw, r("u", 112, 120)), AF.Relu, 223.0, -1.0)
+                act(r("nv", 0, 128), r("g1"), AF.Identity, 255.0, -1.0)
+            act(r("nv", 128, 256), ind(Vw, r("u", 120, 128)), AF.Relu, -32.0)
+            scan(r("mn"), R("m128"), r("ab"), ALU.add, ALU.min)
+            tt(r("lo"), ind(r("mn"), R("su", 2, 3)), lane[par], ALU.not_equal)
+            for ht in range(2):
+                mm((r("pc", 256 + ht, 272, 2), R("Hb", 128 * ht, 128 * ht + 128), r("lo", 0, 8)))
+            tt(r("f", 472, 488), r("pc", 256, 272), dum, ALU.mult)
+            tt(r("f", 456, 472), r("f", 472, 488), r("pd", 80, 96), ALU.max)
+            copy(r("u", 128, 144), r("f", 456, 472))
+            copy(ind(Vw, r("u", 128, 144)), r("nv"))
+            if t + 1 < RO:
+                ctx["pri"] = (1, t + 1, s, -2)
+                mm(*[(r("pd", 112, 113), R("B32"), r("f", 192 + 8 * c, 193 + 8 * c)) for c in range(4)])
+                copy(r("n", 96, 97), r("pd", 112, 113))
+                ts(r("n", 100, 101), r("n", 96, 97), 1, None, ALU.bitwise_and)
+                ts(thr, r("n", 100, 101), 2.0 ** 17, float(((AT[t + 1] - 1) * 32 + 16) * 4096), ALU.mult, ALU.add)
+                ctx["ts"] = None
+                yield
+        ctx["ts"] = None
+        ctx["pri"] = (0, RO, s)
+        M0 = (RO - 1) * MW + 32
+        tr(r("f", 496, 560), r("msg", M0, M0 + 64))
+        for w in range(2):
+            for u in range(2):
+                for yb in range(4):
+                    mm((r("pb", 64 * w + 4 * u + yb, 64 * w + 64, 8, 0, 64), R("Out", 64 * u, 64 * u + 64),
+                        r("f", 496 + 32 * w + 8 * yb, 504 + 32 * w + 8 * yb)))
+        for u in range(2):
+            mm((r("pb", 128 + 4 * u, 132 + 4 * u, 1, 0, 64), R("Out", 64 * u, 64 * u + 64), r("msg", M0 + 64, M0 + 68)))
+        act(r("ks", 0, 136, 1, 0, 64), r("pb", 0, 136, 1, 0, 64), AF.Identity)
+        ks = T["ks" + S]
+        dmas("sp", [(T.yc[64 * s:64 * s + 64, :], ks[0:64, 0:64]), (T.yd[64 * s:64 * s + 64, :], ks[0:64, 64:128]),
+                    (T.yl[64 * s:64 * s + 64, :], ks[0:64, 128:136])], [r("ks", 0, 136)], [], "fin", 35e3)
+        V = T["V" + S]
+        for h in range(2):
+            dmas("sp" if h == 0 else "act",
+                 [(T.yv[64 * s + 16 * G:64 * s + 16 * G + 16, 2048 * h:2048 * h + 2048],
+                   V[32 * G + 16 * h:32 * G + 16 * h + 16, 2048 * h:2048 * h + 2048]) for G in range(4)], [Vw], [], "fin", 1 << 18)
+
+    both = [stream(0), stream(1)]
+    for t in range(RO):
+        for s in range(2):
+            next(both[s], None)
+    last = {}
+    for o in ops:
+        dep = set()
+        acc = [(x, False) for x in o["rd"]] + [(x, True) for x in o["wr"]]
+        for (nm, a, b), w in acc:
+            bank = SCRATCH[nm][0] == "psum"
+            if bank:
+                a, b = 0, 512
+            for a2, b2, w2, j in last.get(nm, []):
+                if (w or w2 or (bank and ops[j]["e"] != o["e"])) and a < b2 and a2 < b and j != o["i"]:
+                    dep.add(j)
+        for (nm, a, b), w in acc:
+            if SCRATCH[nm][0] == "psum":
+                a, b = 0, 512
+            lst = last.setdefault(nm, [])
+            if w:
+                lst[:] = [e for e in lst if not (a <= e[0] and e[1] <= b)]
+            lst.append((a, b, w, o["i"]))
+        o["dep"] = sorted(dep)
+    return ops
+
+
+def times(o, start, c, st):
+    k, a = o["k"], o["n"]
+    if k == "dma":
+        free = start + 0.06 * a[0]
+        st["dma"] = max(st["dma"], start + c["dma"]) + a[1] / c["bw"]
+        return free, st["dma"]
+    if k == "rem":
+        return start + 0.5, start + c["rem"]
+    if k == "pe":
+        d = a * c["cyc"]
+        return start + d, start + d + c["fix"]
+    d = c["fix"] + a * c["cyc"] * (c[k] if k != "cyc" else 1)
+    return start + d, start + d
+
+
+def dues(ops, c):
+    out = [None] * len(ops)
+    for o in ops:
+        if o["key"][0] == "z":
+            out[o["i"]] = (HALF * (2 * RO - 1) + 10 + 0.3 * o["key"][1], 0.0)
+        elif o["key"] in DUE:
+            d, w = DUE[o["key"]]
+            out[o["i"]] = (d + (HALF * (2 * o["ts"][0] + o["ts"][1]) if o["ts"] else 0.0), w)
+    need = [1e9] * len(ops)
+    for o in reversed(ops):
+        i = o["i"]
+        if out[i] is None and need[i] < 1e9:
+            out[i] = (need[i] - times(o, 0.0, c, {"dma": 0.0})[1] - 0.3, 0.0)
+        if out[i] is not None:
+            for j in o["dep"]:
+                need[j] = min(need[j], out[i][0])
+    for o in ops:
+        if out[o["i"]] is None:
+            out[o["i"]] = (max([out[j][0] for j in o["dep"]] + [-100.0]) + 0.1, 0.0)
+        if o["k"] == "dma" and not o["dep"]:
+            out[o["i"]] = (-1000.0 + o["i"], 0.0)
+    return out
+
+
+def plan(ops, c=COST):
+    due = dues(ops, c)
+    free = {e: 0.0 for e in ("act", "dve", "pe", "pool", "sp")}
+    st = {"dma": 0.0}
+    users = [[] for o in ops]
+    left = [len(o["dep"]) for o in ops]
+    for o in ops:
+        for j in o["dep"]:
+            users[j].append(o["i"])
+    rdy = {o["i"]: 0.0 for o in ops if not o["dep"]}
+    at = [0.0] * len(ops)
+    order = []
+    while rdy:
+        est = {i: max(v, free[ops[i]["e"]]) for i, v in rdy.items()}
+        i0 = min(est, key=est.get)
+        e = ops[i0]["e"]
+        i = min((i for i in est if ops[i]["e"] == e and est[i] <= est[i0] + due[i][1]), key=lambda i: (due[i][0], i))
+        free[e], done = times(ops[i], est[i], c, st)
+        del rdy[i]
+        order.append(i)
+        for j in users[i]:
+            at[j] = max(at[j], done + (0 if e == "pe" and ops[j]["e"] == "pe" else c["lat"]))
+            left[j] -= 1
+            if left[j] == 0:
+                rdy[j] = at[j]
+    return order
+
+
+def in_order(order, pre):
+    seen, out = [False] * len(order), []
+    for i in order:
+        st = [i]
+        while st:
+            x = st[-1]
+            m = [j for j in pre[x] if not seen[j]]
+            if m:
+                st.extend(m)
+            else:
+                st.pop()
+                if not seen[x]:
+                    seen[x] = True
+                    out.append(x)
+    return out
+
+
+def table(ops, c):
+    out = []
+    for o in ops:
+        dep = [(j, 0.0 if o["e"] == "pe" and ops[j]["e"] == "pe" else c["lat"]) for j in o["dep"]]
+        if o["k"] == "dma":
+            out.append((o["e"], 0.06 * o["n"][0], c["dma"], o["n"][1] / c["bw"], dep))
+        else:
+            out.append((o["e"],) + times(o, 0.0, c, None) + (0.0, dep))
+    return out
+
+
+def run_through(tab, order):
+    free, done, start, dma = {}, [0.0] * len(tab), [0.0] * len(tab), 0.0
+    for i in order:
+        e, hold, rdy, wire, dep = tab[i]
+        t = free.get(e, 0.0)
+        for j, l in dep:
+            if done[j] + l > t:
+                t = done[j] + l
+        start[i] = t
+        free[e] = t + hold
+        if wire:
+            dma = max(dma, t + rdy) + wire
+            done[i] = dma
+        else:
+            done[i] = t + rdy
+    return start, max(done)
+
+
+def place(line, t, h):
+    a, b = line
+    lo, hi = 0, len(b)
+    while lo < hi:
+        mid = (lo + hi) // 2
+        if b[mid] <= t:
+            lo = mid + 1
+        else:
+            hi = mid
+    while lo < len(a) and a[lo] < t + h - 1e-9:
+        t = max(t, b[lo])
+        lo += 1
+    a.insert(lo, t)
+    b.insert(lo, t + h)
+    return t
+
+
+def tighten(ops, order):
+    n = len(ops)
+    tabs = [table(ops, dict(COST, cyc=0.00083 * m[0], gat=m[1], sca=m[2], fix=m[3], lat=m[4], rem=m[5])) for m in SPREAD]
+    tab = tabs.pop()
+    res = ["dma" if x[3] else x[0] for x in tab]
+    hold = [x[3] or x[1] for x in tab]
+    lead = [x[2] if x[3] else 0.0 for x in tab]
+    done = [x[3] or x[2] for x in tab]
+    pre = [[(j, done[j] + lead[i] + l) for j, l in tab[i][4]] for i in range(n)]
+    suc = [[] for i in range(n)]
+    for i in range(n):
+        for j, d in pre[i]:
+            suc[j].append((i, d))
+    pre0, suc0 = [[j for j, d in p] for p in pre], [[j for j, d in p] for p in suc]
+    loads = sum(o["k"] == "dma" and not o["dep"] for o in ops)
+    seed = [PAR["seed"]]
+
+    def draw():
+        seed[0] = (seed[0] * 1103515245 + 12345) % 2147483648
+        return seed[0] / 2147483648.0
+    best = sum(run_through(x, order)[1] for x in tabs) / len(tabs)
+    start, span = run_through(tab, order)
+    for step in range(PAR["steps"]):
+        a, w, j = draw() * (span + 10) - 10, (3, 8, 20)[int(draw() * 3)], (0.2, 0.6, 1.6)[int(draw() * 3)]
+        st = [x + j * (draw() + draw() + draw() - 1.5) if a < x < a + w else x for x in start]
+        back, lines = [0.0] * n, {}
+        for i in in_order(sorted(range(n), key=lambda i: (-(st[i] + hold[i]), -i)), suc0):
+            t = max([0.0, done[i] - hold[i]] + [back[k] + hold[k] + d - hold[i] for k, d in suc[i]])
+            back[i] = place(lines.setdefault(res[i], ([], [])), t, hold[i])
+        lines = {}
+        for i in in_order(sorted(range(n), key=lambda i: (i >= loads, -(back[i] + hold[i]) if i >= loads else 0, i)), pre0):
+            st[i] = place(lines.setdefault(res[i], ([], [])), max([lead[i]] + [st[j] + d for j, d in pre[i]]), hold[i])
+        new = in_order(sorted(range(n), key=lambda i: (i >= loads, st[i] - lead[i] if i >= loads else 0, i)), pre0)
+        v = sum(run_through(x, new)[1] for x in tabs) / len(tabs)
+        if v <= best + 0.05:
+            best, start, order = v, st, new
+    return order
+
+
+ORDER = []
+
+
+def rank_program(g, core, T, topo):
+    if T.rank_of(core) is None:
+        return
+    ops = build(g, core, T, topo)
+    if not ORDER:
+        ORDER.extend(tighten(ops, plan(ops)))
+    order = ORDER
+    queue = {"act": g.scalar, "dve": g.vector, "pe": g.tensor, "pool": g, "sp": g.sync}
+    need = set()
+    for o in ops:
+        for j in o["dep"]:
+            if not (o["e"] == "pe" and ops[j]["e"] == "pe"):
+                need.add(j)
+    mark, count, seen, total = {}, {}, {}, {"fin": 0, "sent": 0}
+    for i in order:
+        o = ops[i]
+        e = o["e"]
+        want = {}
+        for j in o["dep"]:
+            if not (e == "pe" and ops[j]["e"] == "pe"):
+                sem, v = mark[j]
+                want[sem] = max(want.get(sem, 0), v)
+        for sem, v in want.items():
+            if seen.get((e, sem), 0) < v:
+                queue[e].wait_ge(T.sem[sem], v)
+                seen[(e, sem)] = v
+        ins = o["fn"]()
+        if o["sem"] is not None:
+            mark[i] = (o["sem"], o["cnt"])
+            if o["k"] == "rem":
+                total["sent"] += o["cnt"]
+            elif o["sem"] == "fin":
+                total["fin"] += o["cnt"]
+        elif i in need:
+            count[e] = count.get(e, 0) + 1
+            ins.then_inc(T.sem[e], 1)
+            mark[i] = (e, count[e])
+    g.wait_ge(T.sem.sent, total["sent"])
+    g.sync.wait_ge(T.sem.fin, total["fin"])

@@ -1,70 +1,71 @@
-import numpy as np
+import math
 from concourse.mybir import AluOpType as ALU, ActivationFunctionType as AF
 
 RO, STEP = 6, 2
 MT = [32, 24, 40, 28, 48, 20]
 AT = [8, 10, 7, 9, 6, 11]
 PAR = {
-    "chs": [[1024] * 4, [1024] * 4],
-    "last": [[1024] * 4, [1024] * 3, [512, 512]],
-    "dveg": ((0, 0, 2), (0, 0, 5), (5, 1, 4)),
-    "head": 128,
-    "hot": 2,
-    "g1": "act",
-    "up": "act",
-    "seed": 1,
-    "steps": 2800,
+    "chs": [[1024, 512, 1024, 1024], [1024, 1024, 1024, 512], [512, 512]],
+    "dve": (1,),
+    "dveg": ((5, 1, 4),),
+    "turn": (0, 96, 224, 352, 512),
+    "piece": 64,
+    "gcut": [[(0, 512), (512, 1024), (1024, 1536), (1536, 2048)], [(0, 1024), (1024, 2048)]],
+    "pcut": [[(0, 512), (512, 1024), (1024, 1536), (1536, 1792), (1792, 2048)], [(0, 512), (512, 1024), (1024, 1536), (1536, 2048)]],
+    "starts": ((0.2, 2), (0.25, 6), (0.17, 4), (0.22, 3)),
+    "steps": (100, 1200, 20000),
+    "heat": 0.0001,
 }
 CW = 1024
 ENG = 16
 BIG = 100
 F, B, I, U = "float32", "bfloat16", "int32", "uint16"
-MW = 112
+MW, LW = 72, 104
+V0, VW = 16, 4368
+SEG = 130
+OFF = V0 - 0.5
 
 SCRATCH = {
     "cin": ("sbuf", [128, 136], I), "cinf": ("sbuf", [128, 136], F),
-    "pidx": ("sbuf", [128, 16], I), "pf": ("sbuf", [128, 16], F),
-    "ones": ("sbuf", [128, 160], F), "If": ("sbuf", [128, 128], F), "nIf": ("sbuf", [128, 128], F),
-    "nBig": ("sbuf", [128, 128], F), "pBig": ("sbuf", [128, 128], F), "Ib": ("sbuf", [128, 128], B), "nIb": ("sbuf", [128, 128], B),
-    "SW0": ("sbuf", [128, 160], F), "SW1": ("sbuf", [128, 160], F), "Z0": ("sbuf", [128, 130], F), "Z1": ("sbuf", [128, 130], F),
-    "In0": ("sbuf", [128, 160], F), "In1": ("sbuf", [128, 160], F), "Out": ("sbuf", [128, 128], F), "Hs": ("sbuf", [128, 256], F),
-    "rows": ("sbuf", [128, 800], F), "WW": ("sbuf", [128, 144], B), "VB": ("sbuf", [128, 144], B),
-    "S10": ("sbuf", [128, 160], B), "S11": ("sbuf", [128, 160], B), "B32": ("sbuf", [128, 128], F), "dl": ("sbuf", [128, 128], F),
-    "o64": ("sbuf", [128, 128], B), "CK": ("sbuf", [128, 512], B), "TB": ("sbuf", [128, 32], B),
-    "m8": ("sbuf", [128, CW], B), "zb": ("sbuf", [128, 128], B), "m8s": ("sbuf", [128, 32], B), "m16": ("sbuf", [128, 512], B), "m128": ("sbuf", [128, 512], B),
-    "sm": ("sbuf", [128, 160], F), "su": ("sbuf", [128, 16], U), "Hb": ("sbuf", [128, 256], B),
-    "w": ("sbuf", [128, 8192], B), "Q": ("sbuf", [128, 8192 + 512], B), "z": ("sbuf", [128, 8192], B),
+    "pidx": ("sbuf", [128, 16], I), "pf": ("sbuf", [128, 24], F),
+    "ones": ("sbuf", [128, 264], F), "If": ("sbuf", [128, 128], F), "nIf": ("sbuf", [128, 128], F),
+    "Ib": ("sbuf", [128, 128], B), "nIb": ("sbuf", [128, 128], B),
+    "SW0": ("sbuf", [128, 160], F), "SW1": ("sbuf", [128, 160], F), "Z0": ("sbuf", [128, 132], F), "Z1": ("sbuf", [128, 132], F),
+    "In0": ("sbuf", [128, 160], F), "In1": ("sbuf", [128, 160], F), "Out": ("sbuf", [128, 256], F), "Hs": ("sbuf", [128, 256], F),
+    "J": ("sbuf", [128, 258], F), "Mp": ("sbuf", [128, 288], F), "Md": ("sbuf", [128, 256], F), "Nb": ("sbuf", [128, 256], B),
+    "rows": ("sbuf", [128, 800], F), "WW": ("sbuf", [128, 144], B), "VB": ("sbuf", [128, 144], B), "nVB": ("sbuf", [128, 144], B),
+    "Bn": ("sbuf", [128, 128], F), "Row": ("sbuf", [128, 256], F), "cb": ("sbuf", [128, 384], B), "Dup": ("sbuf", [128, 128], B),
+    "o64": ("sbuf", [128, 128], B), "CK": ("sbuf", [128, 512], B), "TB": ("sbuf", [128, 64], B), "YC": ("sbuf", [128, 64], B),
+    "m8": ("sbuf", [128, CW], B), "m2": ("sbuf", [128, 64], B),
+    "m16": ("sbuf", [128, 512], B), "mseg": ("sbuf", [128, 4 * SEG], B), "LR": ("sbuf", [128, 2 * SEG + 12], B), "LK": ("sbuf", [128, 32], B),
+    "sm": ("sbuf", [128, 64], F), "su": ("sbuf", [128, 16], U), "Hb": ("sbuf", [128, 256], B),
+    "w": ("sbuf", [128, 8192], B), "Q": ("sbuf", [128, 8192 + 16], B), "z": ("sbuf", [128, 8192], B),
 }
 for _s in "01":
     SCRATCH.update({
-        "V" + _s: ("sbuf", [128, 4352], B), "G" + _s: ("sbuf", [128, 2048], I), "P" + _s: ("sbuf", [128, 4096], F),
-        "tmp" + _s: ("sbuf", [128, 1024], F),
-        "lo" + _s: ("sbuf", [128, 16], B), "g2" + _s: ("sbuf", [128, 64], B),
+        "V" + _s: ("sbuf", [128, VW], B), "G" + _s: ("sbuf", [128, 2048], I), "P" + _s: ("sbuf", [128, 4096], F),
+        "tmp" + _s: ("sbuf", [128, 1024], F), "g2" + _s: ("sbuf", [128, 64], B), "sg" + _s: ("sbuf", [128, 48], B),
         "usg" + _s: ("sbuf", [128, 1024], B), "img" + _s: ("sbuf", [128, 512], F), "imT" + _s: ("sbuf", [128, 512], F),
         "of" + _s: ("sbuf", [128, 512], U), "ks" + _s: ("sbuf", [128, 512], F),
         "um" + _s: ("sbuf", [128, 512], B), "pr" + _s: ("sbuf", [128, 512], B),
-        "ab" + _s: ("sbuf", [128, 512], B), "mn" + _s: ("sbuf", [128, 512], B),
-        "X" + _s: ("sbuf", [128, 128], F), "nv" + _s: ("sbuf", [128, 256], B), "g1" + _s: ("sbuf", [128, 128], B),
-        "f" + _s: ("sbuf", [128, 640], F), "n" + _s: ("sbuf", [128, 128], I), "u" + _s: ("sbuf", [128, 160], U),
-        "land" + _s: ("sbuf", [128, RO * MW], F), "msg" + _s: ("sbuf", [128, RO * MW], F),
+        "ab" + _s: ("sbuf", [128, 4 * SEG], B), "mn" + _s: ("sbuf", [128, 4 * SEG], B),
+        "X" + _s: ("sbuf", [128, 64], F), "nv" + _s: ("sbuf", [128, 256], B), "g1" + _s: ("sbuf", [128, 64], B),
+        "Rm" + _s: ("sbuf", [128, 72], F), "O" + _s: ("sbuf", [128, 128], F),
+        "f" + _s: ("sbuf", [128, 512], F), "n" + _s: ("sbuf", [128, 128], I), "u" + _s: ("sbuf", [128, 160], U),
+        "land" + _s: ("sbuf", [128, RO * LW], F), "msg" + _s: ("sbuf", [128, RO * MW], F),
         "pa" + _s: ("psum", [128, 512], F), "pb" + _s: ("psum", [128, 512], F),
         "pc" + _s: ("psum", [128, 512], F), "pd" + _s: ("psum", [128, 512], F),
     })
-SEMAPHORES = (["act", "dve", "pe", "pool", "sent", "ldc", "fin"] + ["ld%s%d" % (k, s) for k in "ghv" for s in range(2)]
+SEMAPHORES = (["act", "dve", "pe", "pool", "sent", "ldc", "fin", "ldv", "ldz0", "ldz1"] + ["ldg%d_%d" % (s, q) for s in range(2) for q in range(4)]
               + ["arr%d_%d" % (t, s) for t in range(1, RO) for s in range(2)])
+QUEUES = ("act", "dve", "pe", "pool", "sp")
 
-HALF = 21.0
-ROUND = ("97c 180 76a 121 142c 1a 135 161d 86a 164d 166 168 170d 221 70b 194 372c 244d 339c 459a 156c 135c 106c 251b 130a 218b 232b 156 242b "
-         "153c 232 138d 279 282a 127b 266 278 376 267 233 65c 402 324d 294 445c 327 340d 354d 368 241 493 233a 179d 182d 245 268b 288d 396b "
-         "305a 346 351a 319 332b 330 303b 265a 337a 322d 339d 332b 334 375a 387b 336c 193 345c 353b 492b 395d 447d 364c 452 346d 369 519 358 "
-         "333c 381 367b 449b 308 369d 482c 228d 363d 433d 457d 431 386b 480a 350a 328b 451 398 473d 632c 451a 440 506d 328b 496b 559c 520 490 "
-         "526d 291c 484d 488d 513c 527 460 533a 523 565c 567a 696c 662b")
-DUE = {(p, q): (int(x.rstrip("abcd")) / 10.0, {"a": 0.1, "b": 0.2, "c": 0.4, "d": 0.8}.get(x[-1], 0.0))
-       for p in "abmy" for q, x in enumerate(ROUND.split())}
-SPREAD = [(1.25, 1.56, 3.8, .06, .08, 2.6), (1.25, 1.56, 3.8, .02, .15, 3.5), (1.1, 1.2, 5, .04, .1, 2.5), (1.4, 1.9, 2.5, .05, .06, 4.5),
-          (1.1, 1.9, 4.5, .03, .2, 3.0), (1.4, 1.2, 3, .0, .05, 2.0), (1.25, 1.56, 3.8, .045, .11, 3.3)]
-CYC = 0.00083 * 1.25
-COST = {"cyc": CYC, "gat": 1.56, "sca": 3.8, "fix": 0.06, "lat": 0.08, "rem": 2.6, "dma": 2.0, "bw": 200e3}
+SPREAD = [(1.0, 1.56, 3.8, .06, .1, 3.0), (1.05, 1.2, 5, .03, .2, 3.5), (1.4, 1.9, 2.5, .05, .08, 4.5),
+          (1.1, 1.9, 4.5, .03, .15, 3.0), (1.35, 1.2, 3, .06, .08, 2.5), (1.15, 1.56, 3.8, .05, .12, 3.3)]
+
+
+def cost(m):
+    return {"cyc": 0.00083 * m[0], "gat": m[1], "sca": m[2], "fix": m[3], "lat": m[4], "rem": m[5], "dma": 2.0, "bw": 200e3}
 
 
 def build(g, core, T, topo):
@@ -72,7 +73,7 @@ def build(g, core, T, topo):
     n = len(T.cores)
     dst = T.cores[(rank + STEP) % n]
     ops = []
-    ctx = {"pri": (0, 0, 0), "ts": None, "seen": [0], "all": [0]}
+    ctx = {"ts": None}
 
     def R(name, a=None, b=None, st=1, p0=0, p1=128):
         shp = SCRATCH[name][1]
@@ -86,14 +87,9 @@ def build(g, core, T, topo):
     def ps(v):
         return SCRATCH[v[1]][0] == "psum"
 
-    def op(eng, fn, rd, wr, kind, amt, sem=None, cnt=0, after=None):
+    def op(eng, fn, rd, wr, kind, amt, sem=None, cnt=0):
         ops.append({"e": eng, "fn": fn, "rd": [x[1:4] for x in rd], "wr": [x[1:4] for x in wr], "k": kind, "n": amt,
-                    "sem": sem, "cnt": cnt, "pri": ctx["pri"], "ts": ctx["ts"], "key": None, "i": len(ops)})
-        part = {None: "x", (0, 0): "a", (0, 1): "b", (RO - 1, 0): "y", (RO - 1, 1): "z"}.get(ctx["ts"], "m")
-        seen = ctx["all"] if part == "x" else ctx["seen"]
-        seen[0] += 1
-        ops[-1]["key"] = (part, seen[0] - 1)
-        return ops[-1]
+                    "sem": sem, "cnt": cnt, "ts": ctx["ts"], "i": len(ops)})
 
     def ind(win, off):
         return (win[0].indirect(off[0]), win[1], win[2], win[3], off[4] * 16, off)
@@ -142,9 +138,12 @@ def build(g, core, T, topo):
     def mset(o, v):
         op("dve", lambda: g.vector.memset(o[0], v), [], [o], "cyc", max(64, (0.5 if two(o) else 1) * o[4]))
 
-    def act(o, i, fn, bias=0.0, scale=1.0):
+    def act(o, i, fn, bias=0.0, scale=1.0, acc=None):
         k, c = vcost(o, i, 1)
-        op("act", lambda: g.scalar.activation(o[0], i[0], fn, bias=ap(bias), scale=scale), rds(i, bias), [o], k, c)
+        if acc is None:
+            op("act", lambda: g.scalar.activation(o[0], i[0], fn, bias=ap(bias), scale=scale), rds(i, bias), [o], k, c)
+        else:
+            op("act", lambda: g.scalar.activation(o[0], i[0], fn, bias=ap(bias), scale=scale, accum_out=acc[0]), rds(i, bias), [o, acc], k, c + 24)
 
     def mm(*terms, start=True, stop=True):
         def fn():
@@ -161,8 +160,14 @@ def build(g, core, T, topo):
         else:
             op("pool", lambda: g.iota(o[0], pat, base, cm, allow_small_or_imprecise_dtypes=True), [], [o], "cyc", 130 + 2 * o[4])
 
-    def perm(o, pat, base):
-        i = R("ones", 0, o[4])
+    def fill(o, v):
+        iota(o, [[0, o[4]]], v)
+
+    def keep(o, i):
+        op("pool", lambda: g.affine_select(o[0], i[0], [[0, o[4]]], ALU.is_ge, 0.0, 0, 0), [i], [o], "cyc", 170 + 2 * o[4])
+
+    def perm(o, pat, base, i=None):
+        i = i or R("ones", 0, o[4])
         op("pool", lambda: g.affine_select(o[0], i[0], [[-a, c] for a, c in pat], ALU.is_equal, 0.0, -base, 1), [i], [o], "cyc", 170 + 2 * o[4])
 
     def dmas(eng, pairs, rd, wr, sem, nbytes):
@@ -171,58 +176,66 @@ def build(g, core, T, topo):
         def fn():
             for o, i in pairs:
                 q.dma_start(o, i).then_inc(T.sem[sem], 16)
-        return op(eng, fn, rd, wr, "dma", (len(pairs), nbytes), sem=sem, cnt=16 * len(pairs))
+        op(eng, fn, rd, wr, "dma", (len(pairs), nbytes), sem=sem, cnt=16 * len(pairs))
+
+    chunks, at = [], 0
+    for grp in PAR["chs"]:
+        chunks.append([])
+        for cw in grp:
+            chunks[-1].append((sum(map(len, chunks)), at, cw))
+            at += cw
 
     dmas("sp", [(T.cin[:, 0:64], T.cla[:]), (T.cin[:, 64:128], T.par[:]), (T.cin[:, 128:136], T.lit[:])], [], [R("cin")], "ldc", 70e3)
+    for q in range(2):
+        dmas("act", [(T.z[0:64, 2048 * q:2048 * q + 2048], T.val[0:64, 2048 * q:2048 * q + 2048])], [], [R("z", 2048 * q, 2048 * q + 2048)], "ldz%d" % q, 1 << 18)
     for s in range(2):
         S = str(s)
         hv = [(32 * G + 16 * h, 64 * s + 16 * G) for G in range(4) for h in range(2)]
-        for q in range(2):
-            dmas("act" if s == 0 and q == 0 else "sp", [(T["G" + S][a:a + 16, 1024 * q:1024 * q + 1024], T.gen[b:b + 16, 1024 * q:1024 * q + 1024]) for a, b in hv],
-                 [], [R("G" + S, 1024 * q, 1024 * q + 1024)], "ld%s%d" % ("gh"[q], s), 1 << 19)
-        dmas("act" if s == 0 else "sp", [(T["V" + S][a:a + 16, 0:4096], T.val[b:b + 16, :]) for a, b in hv], [], [R("V" + S, 0, 4096)], "ldv" + S, 1 << 20)
+        for q, (c0, c1) in enumerate(PAR["gcut"][s]):
+            dmas("sp", [(T["G" + S][a:a + 16, c0:c1], T.gen[b:b + 16, c0:c1]) for a, b in hv],
+                 [], [R("G" + S, c0, c1)], "ldg%d_%d" % (s, q), 512 * (c1 - c0))
+    dmas("sp", [(T.V1[a:a + 16, V0:V0 + 4096], T.val[b:b + 16, :]) for a, b in hv], [], [R("V1", V0, V0 + 4096)], "ldv", 1 << 20)
 
-    ctx["pri"] = (0, -1, 0)
     mset(R("ones"), 1.0)
     iota(R("pidx", 0, 1), [[0, 1]], 0, 1)
     perm(R("In0"), [[16, 5], [-1000, 2], [1, 16]], 1000)
-    iota(R("rows", 0, 160), [[2, 5], [-BIG, 4], [0, 8]], 3 * BIG)
+    perm(R("In1"), [[16, 5], [-1000, 2], [1, 16]], 1064)
     perm(R("If"), [[1, 128]], 0)
-    fld = {"blk": (4, 7), "G": (5, 3), "p31": (0, 31), "r15": (0, 15), "ht": (4, 1), "y0": (0, 1), "k7": (0, 7), "b": (3, 1), "p3": (0, 3)}
+    perm(R("J"), [[1, 129], [-1000, 2]], 1000)
+    fld = {"blk": (4, 7), "G": (5, 3), "r15": (0, 15), "y": (1, 1), "b0": (0, 1), "b": (3, 1), "B10": (2, 3)}
     col = {}
     for q, (nm, (sh, ms)) in enumerate(fld.items()):
         ts(R("pidx", q + 1, q + 2), R("pidx", 0, 1), sh, ms, ALU.logical_shift_right, ALU.bitwise_and)
         col[nm] = R("pf", q + 1, q + 2)
-    copy(R("pf", 0, 10), R("pidx", 0, 10))
+    copy(R("pf", 0, 8), R("pidx", 0, 8))
     copy(R("cinf"), R("cin"))
-    for bt in range(2):
-        ts(R("S1%d" % bt), R("rows", 0, 160), float(bt), col["blk"], ALU.add, ALU.is_equal)
-    ts(R("nIf"), R("If"), -1.0, None, ALU.mult)
+    act(R("nIf"), R("If"), AF.Identity, 0.0, -1.0)
+    mset(R("cb", 256, 384), 1.0)
+    perm(R("Dup", p1=64), [[16, 4], [0, 2], [1, 16]], 0, R("cb", 256, 384, p1=64))
+    for q in range(8):
+        pu = R(("pa1", "pb1")[q % 2])
+        mm((pu, R("Dup", p1=64), R("z", 512 * q, 512 * q + 512, p1=64)))
+        act(R("V0", V0 + 512 * q, V0 + 512 * q + 512), pu, AF.Identity)
     for s in range(2):
-        mset(R("V%d" % s, 4096, 4352), 0.0)
-    ctx["pri"] = (0, 0, 5)
+        S = str(s)
+        mset(R("V" + S, 0, V0), 0.0)
+        mset(R("V" + S, V0 + 4096, VW), 0.0)
+        fill(R("O" + S, 56, 64), 0)
+        fill(R("Rm" + S, 64, 72), -1)
+        fill(R("ab" + S, 66, 2 * SEG), 64)
     perm(R("SW0"), [[32, 5], [-1000, 2], [1, 16]], 1000)
     perm(R("SW1"), [[32, 5], [1000, 2], [1, 16]], -16)
-    perm(R("In1"), [[16, 5], [-1000, 2], [1, 16]], 1064)
     mset(R("m8"), 1.0)
     mset(R("m8", 0, CW, 8), 0.0)
-    mset(R("zb"), 0.0)
-    def cut(chs):
-        out, at = [], 0
-        for grp in chs:
-            out.append([])
-            for cw in grp:
-                out[-1].append((sum(map(len, out)), at, cw, at + at // 16 + 16))
-                at += cw
-        return out
-    zeros = [x[3] - 1 for grp in cut(PAR["chs"]) for x in grp]
-    mset(R("Q", 15, 8192 + 512, 272), 0.0)
+    mset(R("Q", 0, 16), 0.0)
     turn = [0]
-    copy(R("Ib"), R("If"))
-    copy(R("nIb"), R("nIf"))
-    ctx["pri"] = (1, 0, 0)
+    act(R("Ib"), R("If"), AF.Identity)
+    act(R("nIb"), R("If"), AF.Identity, 0.0, -1.0)
     iota(R("rows", 160, 304), [[1, 9], [-BIG, 2], [0, 8]], BIG)
     ts(R("VB"), R("rows", 160, 304), col["blk"], 65536.0, ALU.is_equal, ALU.mult)
+    act(R("nVB"), R("VB"), AF.Identity, 0.0, -1.0)
+    mset(R("YC", 0, 32), 8.5 * 65536)
+    mset(R("YC", 32, 64), -8.5 * 65536)
     iota(R("CK", p1=64), [[0, 32], [-4096, 16]], 15 * 4096)
     mset(R("CK", p0=64), float(1 << 20))
     mset(R("o64"), 1.0 / 64)
@@ -232,174 +245,212 @@ def build(g, core, T, topo):
     ts(R("WW"), R("rows", 304, 448), col["blk"], None, ALU.is_equal)
     iota(R("rows", 704, 736), [[32, 32]], 30)
     ubase = R("sm", 0, 32)
-    ts(ubase, R("rows", 704, 736), col["b"], None, ALU.add)
-    ts(R("pf", 10, 11), col["k7"], -0.125, 0.875, ALU.mult, ALU.add)
-    ts(R("TB"), R("ones", 0, 32), R("pf", 10, 11), None, ALU.mult)
-    mset(R("m8s"), 1.0)
-    mset(R("m8s", 0, 32, 8), 0.0)
-    perm(R("Z0"), [[2, 65], [-1000, 2]], 1000)
-    perm(R("Z1"), [[2, 65], [1000, 2]], -1)
-    act(R("nBig"), R("If"), AF.Identity, 0.0, -8192.0)
-    act(R("pBig"), R("If"), AF.Identity, 0.0, 8192.0)
+    act(ubase, R("rows", 704, 736), AF.Identity, col["b"])
+    ts(R("pf", 10, 11), col["r15"], -0.125, 0.875, ALU.mult, ALU.add)
+    ts(R("pf", 11, 12), col["r15"], 15.0, OFF, ALU.is_equal, ALU.mult)
+    ts(R("pf", 12, 13), R("pf", 10, 11), 0.0, R("pf", 11, 12), ALU.max, ALU.add)
+    ts(R("TB"), R("ones", 0, 64), R("pf", 12, 13), None, ALU.mult)
+    fill(R("cb", 0, 128), -8192)
+    fill(R("cb", 128, 256), -2 ** 21)
+    for b in range(2):
+        perm(R("Nb", 128 * b, 128 * b + 128), [[16, 8], [1000, 2], [1, 8]], 8 * b, R("cb", 0, 128))
+        perm(R("Mp", 144 * b, 144 * b + 144), [[16, 9], [-1000, 2], [1, 8]], 1000 + 8 * b)
+        tt(R("Md", 128 * b, 128 * b + 128), R("Mp", 144 * b, 144 * b + 128), R("Mp", 144 * b + 1, 144 * b + 129), ALU.subtract)
+    fill(R("Md", 7, 256, 16), 0)
+    fill(R("m2"), 0)
+    fill(R("m2", 7, 64, 16), -2)
+    perm(R("Z0"), [[4, 33], [-1000, 2], [1, 2]], 1000)
+    perm(R("Z1"), [[4, 33], [1000, 2], [1, 2]], -2)
     iota(R("rows", 448, 576), [[1, 4], [0, 32]], 0)
-    ts(R("B32"), R("rows", 448, 576), col["G"], None, ALU.is_equal)
-    iota(R("rows", 576, 704), [[0, 4], [1, 32]], 0)
-    ts(R("dl"), R("rows", 576, 704), col["p31"], None, ALU.is_equal)
+    ts(R("Bn"), R("rows", 448, 576), col["G"], -8192.0, ALU.is_equal, ALU.mult)
+    fill(R("rows", 576, 704), -8192)
+    for x in range(2):
+        perm(R("Row", 128 * x, 128 * x + 128), [[32, 4], [0, 32]], 16 * x + 6, R("rows", 576, 704))
     for ht in range(2):
         perm(R("Hs", 128 * ht, 128 * ht + 128), [[32, 4], [0, 2], [1, 16]], 16 * ht)
-    mset(R("m128"), 0.0)
-    mset(R("m128", 0, 512, 128), float(1 << 23))
-    iota(R("rows", 736, 752), [[0, 4], [1, 2], [16, 2]], 0)
-    iota(R("rows", 752, 768), [[0, 4], [32, 2], [16, 2]], 0)
-    iota(R("rows", 768, 776), [[1, 4], [0, 2]], 0)
-    ts(R("pf", 11, 12), col["ht"], 64.0, col["r15"], ALU.mult, ALU.add)
-    ts(R("pf", 12, 13), col["y0"], 31.0, R("pf", 11, 12), ALU.mult, ALU.add)
-    lane = []
+        perm(R("Hb", 128 * ht, 128 * ht + 128), [[32, 4], [0, 2], [1, 16]], 16 * ht, R("cb", 128, 256))
+    fill(R("mseg"), 0)
+    fill(R("mseg", 0, 4 * SEG, SEG), 1 << 23)
+    act(R("pf", 13, 14), col["b0"], AF.Identity, 0.0, 16.0)
+    act(R("pf", 14, 15), col["B10"], AF.Identity, R("pf", 13, 14), 2.0)
     for par in range(2):
-        lane.append(R("sm", 32 + 32 * par, 48 + 32 * par))
-        ts(lane[par], R("rows", 736 + 16 * par, 752 + 16 * par), R("pf", 12 - par, 13 - par), 1.0 / 64, ALU.add, ALU.mult)
-    iota(R("rows", 776, 792), [[16, 16]], 4096)
-    dum = R("sm", 96, 112)
-    ts(dum, R("rows", 776, 792), col["r15"], None, ALU.add)
-    copy(R("Hb"), R("Hs"))
-    for c in range(2):
-        ts(R("su", c, c + 1), col["b"], 8.0, 16.0 * c + 7, ALU.mult, ALU.add)
-    ts(R("su", 2, 3), col["p3"], 128.0, 127.0, ALU.mult, ALU.add)
-    copy(R("su", 4, 12), R("rows", 768, 776))
+        wx, wy = ((1, 32), (32, 1))[par]
+        a = (SEG + 6) * par
+        iota(R("LR", a, a + 2), [[32767, 2]], 0)
+        for c in range(4):
+            iota(R("LR", a + 2 + 64 * (c // 2) + c % 2, a + 66 + 64 * (c // 2), 2), [[-64, 8], [-32 * wy, 2], [-512, 2]], -32 * (64 * (c // 2) + wx * (c % 2) + 1))
+        for w in range(2):
+            iota(R("rows", 16 * par + 8 * w, 16 * par + 8 * w + 8), [[64, 2], [wx, 2], [8, 2]], 1)
+        act(R("pf", 15 + par, 16 + par), col["y"], AF.Identity, R("pf", 14, 15), float(wy))
+        ts(R("LK", 16 * par, 16 * par + 16), R("rows", 16 * par, 16 * par + 16), R("pf", 15 + par, 16 + par), 8192.0, ALU.add, ALU.mult)
+    iota(R("rows", 776, 792), [[16, 16]], V0 + 4096)
+    dum = R("sm", 32, 48)
+    ts(dum, R("rows", 776, 792), col["r15"], -0.5, ALU.add, ALU.add)
+    iota(R("rows", 32, 36), [[16, 4]], 15)
+    act(R("pf", 17, 18), col["b"], AF.Identity, 0.0, 64.0)
+    ts(R("sm", 48, 52), R("rows", 32, 36), R("pf", 17, 18), 64.0, ALU.add, ALU.min)
+    keep(R("su", 0, 4), R("sm", 48, 52))
     for u in range(2):
         perm(R("Out", 64 * u, 64 * u + 64), [[32, 4], [1, 16]], 16 * u)
+        perm(R("Out", 128 + 64 * u, 192 + 64 * u), [[2, 64]], u)
 
-    def other(lv, lo, t1, t2):
-        ts(t1, lv, 2.0 - 2.0 ** -12, 2.0 ** 25, ALU.mult, ALU.add)
-        ts(t2, t1, -2.0 ** 25, 1.0, ALU.add, ALU.add)
-        tt(lo, t2, lv, ALU.subtract)
+    def swap(o, i, name):
+        for y in range(2):
+            mm(*[(R(o[0], o[1] + y, o[2], 2), R("SW%d" % y, 16 - 16 * (x - y), 144 - 16 * (x - y)), R(name, i[0] + x, i[1], 2)) for x in range(2)])
 
     def stream(s):
         S = str(s)
 
         def r(name, *a, **k):
             return R(name + S, *a, **k)
-        Vw = r("V")
-        ctx["pri"] = (0, 0, 0) if s == 0 else (1, 0, 8)
-        for q in range(4):
-            ev = r("P", 1024 * q, 1024 * q + 1024, 2)
-            ts(ev, r("G", 512 * q, 512 * q + 512), -0.5, None, ALU.add)
-            tm = r("tmp", 512 * (q % 2), 512 * (q % 2) + 512)
-            act(tm, ev, AF.Identity, 2.0 ** 25, 2.0)
-            pu = r("pb") if q % 2 else R("pa0") if s == 0 else r("pc")
-            act(pu, tm, AF.Identity, -2.0 ** 25)
-            tt(r("P", 1024 * q + 1, 1024 * q + 1024, 2), pu, ev, ALU.subtract)
-        ctx["pri"] = (0, 0, s)
+        Vw, Vm = r("V"), r("V", V0, V0 + 4096)
+
+        def clauses(src, bank, w, y):
+            tr(r("f", 128 + 32 * w, 160 + 32 * w), src)
+            for u in range(2):
+                for yb in range(4):
+                    mm((r(bank, 64 + 4 * u + yb, 128, 8, 0, 64), R("Out", 64 * u, 64 * u + 64), r("f", 128 + 32 * w + 8 * yb, 136 + 32 * w + 8 * yb)))
+            act(r("tmp", 64 * w, 64 * w + 64, 1, 0, 64), r(bank, 64, 128, 1, 0, 64), AF.Identity)
+            dmas("sp", [(y[64 * s:64 * s + 64, :], T["tmp" + S][0:64, 64 * w:64 * w + 64])], [r("tmp", 64 * w, 64 * w + 64)], [], "fin", 16e3)
+
+        def edits(a):
+            act(r("nv", 128, 256), ind(Vw, r("u", a + 8, a + 16)), AF.Relu, -32.0)
+            ts(r("nv", 0, 128), ind(Vw, r("u", a, a + 8)), 32.0, 255.0, ALU.add, ALU.min)
         for w in range(2):
             for yb in range(4):
                 mm(*[(r("pc", 32 * w + 8 * yb, 32 * w + 8 * yb + 8), R("In" + S, 16 - 16 * u, 144 - 16 * u),
                       R("cinf", 64 * w + 4 * u + yb, 64 * w + 64, 8)) for u in range(2)])
-        tr(r("land", 0, 64), r("pc", 0, 64))
-        mm(*[(r("pd", 0, 4), R("In" + S, 16 - 16 * u, 144 - 16 * u), R("cinf", 128 + 4 * u, 132 + 4 * u)) for u in range(2)])
-        copy(r("land", 64, 68), r("pd", 0, 4))
-        other(r("land", 64, 68), r("land", 68, 72), r("f", 400, 404), r("f", 408, 412))
+        tr(r("land", 40, 72), r("pc", 0, 32))
+        tr(r("land", 72, 104), r("pc", 32, 64))
+        for b in range(2):
+            mm((r("pb", 32, 36), R("J", 1 + 128 * s - b, 129 + 128 * s - b), R("cinf", 128 + b, 136, 2)), start=b == 0, stop=b == 1)
+        if s:
+            act(r("land", 32, 36), r("pb", 32, 36), AF.Identity, OFF)
+            act(r("f", 400, 404), r("land", 32, 36), AF.Identity, 2.0 ** 24)
+            act(r("f", 404, 408), r("f", 400, 404), AF.Identity, -2.0 ** 25, 2.0)
+        else:
+            ts(r("land", 32, 36), r("pb", 32, 36), OFF, None, ALU.add)
+            ts(r("f", 400, 404), r("land", 32, 36), 2.0 ** 24, -2.0 ** 24, ALU.add, ALU.add)
+            ts(r("f", 404, 408), r("f", 400, 404), 2.0, None, ALU.mult)
+        tt(r("land", 36, 40), r("f", 404, 408), r("land", 32, 36), ALU.subtract)
+        for q, (a, b) in enumerate(PAR["pcut"][s]):
+            ev = r("P", 2 * a, 2 * b, 2)
+            tm = r("tmp", 512 * (q % 2), 512 * (q % 2) + b - a)
+            pu = R(("pa0", "pd0")[q % 2] if s == 0 else "pd1", 0, b - a)
+            if s:
+                keep(ev, r("G", a, b))
+                act(tm, ev, AF.Identity, 2.0 ** 25, 2.0 - 2.0 ** -12)
+                ts(pu, tm, -2.0 ** 25, 1.0, ALU.add, ALU.add)
+            else:
+                ts(ev, r("G", a, b), -0.5, None, ALU.add)
+                if q % 2:
+                    act(tm, ev, AF.Identity, 2.0 ** 25, 2.0)
+                    act(pu, tm, AF.Identity, -2.0 ** 25)
+                else:
+                    ts(tm, r("G", a, b), -0.5, 2.0 ** 24, ALU.add, ALU.add)
+                    act(pu, tm, AF.Identity, -2.0 ** 25, 2.0)
+            tt(r("P", 2 * a + 1, 2 * b, 2), pu, ev, ALU.subtract)
         thr = r("f", 416, 417)
         mset(thr, float(((AT[0] - 1) * 32 + 16) * 4096))
 
         for t in range(RO):
             par = t % 2
-            chain = (0, t, s)
-            ctx["pri"] = chain
-            ctx["ts"], ctx["seen"] = (t, s), [0]
-            L0, M0 = t * MW, t * MW + 32
-            C, D = r("land", L0, L0 + 32), r("land", L0 + 32, L0 + 64)
-            copy(r("u", 0, 8), r("land", L0 + 64, L0 + 72))
-            mm((r("pc", 0, 32), R("If"), D), (r("pc", 0, 32), R("nIf"), C))
-            if PAR["g1"] == "act":
-                act(r("g1", 0, 64), ind(Vw, r("u", 4, 8)), AF.Identity)
-            else:
-                copy(r("g1", 0, 64), ind(Vw, r("u", 4, 8)))
-            tt(r("g2"), ind(Vw, r("u", 0, 4)), r("g1", 0, 64), ALU.is_lt)
-            for bt in range(2):
-                mm(*[(r("pc", 32 + 16 * bt, 48 + 16 * bt), R("S1%d" % bt, 24 - 8 * yb, 152 - 8 * yb),
-                      r("g2", 16 * yb, 16 + 16 * yb)) for yb in range(4)])
-            ts(r("f", 0, 32), r("pc", 32, 64), 8.5, None, ALU.is_ge)
-            tt(r("f", 32, 64), r("f", 0, 32), r("pc", 0, 32), ALU.mult)
-            tt(C, r("f", 32, 64), C, ALU.add)
+            ctx["ts"] = (t, s)
+            L0, M0 = t * LW, t * MW
+            swap(("pb" + S, 0 if t else 32, 40), (L0 if t else 32, L0 + 40), "land" + S)
+            ts(r("u", 0, 8), r("pb", 32, 40), 0.5, None, ALU.add)
+            if t:
+                act(r("land", L0 + 72, L0 + 104), r("pb", 0, 32), AF.Identity)
+                act(r("f", 96, 128), r("land", L0, L0 + 32), AF.Identity, thr)
+            mm((r("pc", 0, 64), R("Ib"), R("YC")), stop=False)
+            act(r("g1"), ind(Vw, r("u", 4, 8)), AF.Identity)
+            tt(r("g2"), ind(Vw, r("u", 0, 4)), r("g1"), ALU.is_lt)
+            mm(*[(r("pc", 32 * w, 32 * w + 32), R(("nVB", "VB")[w], 8 - 8 * b, 136 - 8 * b), r("g2", b, 64, 2)) for w in range(2) for b in range(2)], start=False)
+            tt(r("f", 0, 64), r("land", L0 + 40, L0 + 104), r("pc", 0, 64), ALU.min)
+            C = r("msg", M0, M0 + 32)
+            tt(C, r("f", 0, 32), r("f", 32, 64), ALU.max)
             copy(r("u", 16, 48), C)
-            for a, b in ((0, PAR["head"]), (PAR["head"], 512)):
-                act(r("img", a, b), ind(r("P"), r("u", 16 + a // 16, 16 + b // 16)), AF.Identity, 0.5)
+            cuts = PAR["turn"]
+            for a, b in (cuts[:2], (cuts[1], cuts[-1])):
+                act(r("img", a, b), ind(r("P"), r("u", 16 + a // 16, 16 + b // 16)), AF.Identity, 0.0 if s else 0.5)
                 tr(r("imT", a, b), r("img", a, b))
-                copy(r("of", a, b), r("imT", a, b))
-            ctx["pri"] = (1, t, s, -1)
-            for y in range(2):
-                mm(*[(r("pd", y, 64, 2), R("SW%d" % y, 16 - 16 * (x - y), 144 - 16 * (x - y)), r("land", L0 + x, L0 + 64, 2)) for x in range(2)])
-            act(r("f", 96, 128), r("pd", 32, 64), AF.Identity, thr)
-            act(r("msg", M0 + 32, M0 + 64), r("pd", 0, 32), AF.Identity)
-            chunks = cut(PAR["last"] if (t, s) == (RO - 1, 1) else PAR["chs"])
-            nch = sum(map(len, chunks))
-            for grp in chunks:
-                ctx["pri"] = (1, t, s, grp[0][0])
+            for a, b in zip(cuts, cuts[1:]):
+                (keep if a else copy)(r("of", a, b), r("imT", a, b))
+            if t == 0:
+                swap(("pd" + S, 32, 64), (72, 104), "land" + S)
+                act(r("f", 96, 128), r("pd", 32, 64), AF.Identity, thr)
+            if t + 1 == RO:
+                swap(("pd" + S, 32, 64), (M0, M0 + 32), "msg" + S)
+                clauses(r("pd", 32, 64), "pd", 1, T.yd)
+            mm((r("pc", 64, 128), R("Ib"), R("TB")), stop=False)
+            for q, grp in enumerate(chunks):
                 u0, u1 = grp[0][1] // 8, (grp[-1][1] + grp[-1][2]) // 8
-                pa = "pa%d" % (turn[0] % 2)
+                pa, kb = "pa%d" % (turn[0] % 2), ("pb", "pd")[q % 2]
                 turn[0] += 1
-                mm((R(pa, 0, u1 - u0), R("zb"), R("m16", 0, u1 - u0)), stop=False)
-                kv = r("pb", u0 // 2, u1 // 2)
-                mm((kv, R("If"), r("imT", u0 // 2, u1 // 2)), (kv, R("o64"), R("CK", u0 // 2, u1 // 2)), stop=False)
+                kv = r(kb, u0 // 2, u1 // 2)
+                for a in range(u0 // 2, u1 // 2, PAR["piece"]):
+                    b = min(a + PAR["piece"], u1 // 2)
+                    mm((r(kb, a, b), R("o64"), R("CK", a, b)), (r(kb, a, b), R("If"), r("imT", a, b)), start=a == u0 // 2, stop=False)
 
-                def second(c, a, cw, q):
-                    scan(R("z", a, a + cw), R("w", a, a + cw), R("Q", q - 1, q - 1 + cw), ALU.max, ALU.min)
+                def second(c, a, cw):
+                    scan(R("z", a, a + cw), R("w", a, a + cw), R("Q", a + 15, a + 15 + cw), ALU.max, ALU.min)
                     mm((R(pa, a // 8 - u0, (a + cw) // 8 - u0), R("nIb"), R("z", a + 7, a + cw, 8)), start=False, stop=c == grp[-1][0])
-                for q0, (c, a, cw, q) in enumerate(grp):
-                    ctx["pri"] = (1, t, s, c)
+                for q0, (c, a, cw) in enumerate(grp):
                     wv = R("w", a, a + cw)
-                    src = ind(Vw, r("of", a // 16, (a + cw) // 16))
-                    if (t, s, c) in PAR["dveg"]:
+                    src = ind(Vm, r("of", a // 16, (a + cw) // 16))
+                    if (t, s, c) in PAR["dveg"] or c in PAR["dve"]:
                         copy(wv, src)
                     else:
                         act(wv, src, AF.Identity)
-                    if c >= nch - PAR["hot"]:
-                        ctx["pri"] = chain
-                    if q - 1 not in zeros:
-                        iota(R("Q", q - 1, q), [[0, 1]], 0)
-                    scan(R("Q", q, q + cw), R("m8", 0, cw), wv, ALU.mult, ALU.max)
-                    top = R("Q", q + 7, q + cw, 8)
-                    mm((R(pa, a // 8 - u0, (a + cw) // 8 - u0), R("Ib"), top), start=False, stop=False)
-                    if c == nch - 1:
-                        mset(top, 0.0)
-                    else:
-                        iota(top, [[0, cw // 8]], 0)
+                    scan(R("Q", a + 16, a + 16 + cw), R("m8", 0, cw), wv, ALU.mult, ALU.max)
+                    top = R("Q", a + 23, a + 16 + cw, 8)
+                    mm((R(pa, a // 8 - u0, (a + cw) // 8 - u0), R("Ib"), top), start=q0 == 0, stop=False)
+                    fill(top, 0)
                     if q0:
                         second(*grp[q0 - 1])
                 second(*grp[-1])
                 act(r("usg", u0, u1), R(pa, 0, u1 - u0), AF.Sign, -MT[t] - 0.5)
                 mm(*[(kv, R("VB", 8 - 8 * b, 136 - 8 * b), r("usg", u0 + b, u1, 2)) for b in range(2)], start=False)
                 scan(r("ks", u0 // 2, u1 // 2), R("m16", u0 // 2, u1 // 2), kv, ALU.mult, ALU.max)
-            ctx["pri"] = chain
+            for v in range(2):
+                for u in range(2):
+                    mm((r("pd", v, 8, 2), R("Z%d" % v, 2 - 2 * (u - v), 130 - 2 * (u - v)), r("land", L0 + 32 + u, L0 + 40, 2)), start=u + v == 0, stop=False)
             km, nC = r("n", 0, 32), r("n", 32, 64)
-            tt(km, r("ks", 15, 512, 16), r("f", 96, 128), ALU.max)
+            best = r("ks", 15, 512, 16)
+            tt(km, best, r("f", 96, 128), ALU.max)
             ts(r("n", 96, 128), km, 11, 30, ALU.logical_shift_right, ALU.bitwise_and)
             ts(nC, km, 4095, None, ALU.bitwise_and)
             tt(r("n", 64, 96), ubase, r("n", 96, 128), ALU.subtract)
             copy(r("u", 48, 112), r("n", 32, 96))
+            stay, cnt = r("sg", 0, 32), r("f", 424, 425)
+            act(stay, best, AF.Sign, thr, -1.0, acc=cnt)
             act(r("um"), ind(r("usg"), r("u", 80, 112)), AF.Relu)
-            tt(r("pr"), ind(Vw, r("u", 48, 80)), r("um"), ALU.mult)
-            copy(r("msg", M0, M0 + 32), nC)
-            stay = r("msg", M0 - 32, M0)
-            ts(stay, km, -4096.0, thr, ALU.add, ALU.is_lt)
-            tr(r("f", 192, 256), r("msg", M0 - 32, M0 + 32))
-            st3 = r("f", 192, 224, 8)
-            mm((r("pc", 64, 96), R("Ib"), R("TB")), (r("pc", 64, 96), R("nBig"), stay), stop=False)
-            mm(*([(r("pd", 64, 68), R("pBig"), st3), (r("pd", 64, 68), R("nBig"), R("ones", 0, 4))]
-                 + [(r("pd", 64 + 2 * x, 66 + 2 * x), R("Z%d" % x, 1 - (y - x), 129 - (y - x)), r("land", L0 + 64 + 2 * y, L0 + 66 + 2 * y))
-                    for x in range(2) for y in range(2)]))
-            mm((r("pd", 72, 76), R("pBig"), st3), (r("pd", 72, 76), R("If"), R("sm", 32 + 32 * par, 36 + 32 * par)))
-            mm(*[(r("pc", 64, 96), R("WW", 15 - p, 143 - p), r("pr", p, 512, 16)) for p in range(16)], start=False)
-            tr(r("f", 256, 288), r("pc", 64, 96))
-            scan(r("f", 288, 320), R("m8s"), r("f", 256, 288), ALU.mult, ALU.max)
-            tt(r("f", 320, 352), ind(r("f", 288, 320), R("su", 0, 2)), r("f", 256, 288), ALU.is_equal)
-            tt(r("f", 352, 384), r("f", 320, 352), r("f", 224, 256), ALU.mult)
-            scan(r("f", 256, 288), R("m8s"), r("f", 352, 384), ALU.mult, ALU.add)
-            lv, lo, ll = r("msg", M0 + 64, M0 + 68), r("msg", M0 + 68, M0 + 72), r("msg", M0 + 64, M0 + 72)
-            tt(lv, r("f", 263, 288, 8), r("pd", 64, 68), ALU.max)
-            other(lv, lo, r("f", 400, 404), r("f", 408, 412))
+            tt(r("pr"), ind(Vm, r("u", 48, 80)), r("um"), ALU.mult)
+            new = r("msg", M0 + 40, M0 + 72)
+            keep(new, nC)
+            if t + 1 == RO:
+                clauses(new, ("pb", "pa")[s], 0, T.yc)
+            else:
+                mm((r("pb", 40, 41), R("Bn"), cnt))
+                act(r("sg", 32, 33), r("pb", 40, 41), AF.Identity, -319.75 * 2 ** 17, -1.0)
+                ts(thr, r("sg", 32, 33), 320.0 * 2 ** 17 + ((AT[t + 1] - 1) * 32 + 16) * 4096, r("pb", 40, 41), ALU.add, ALU.add)
+            mm(*[(r("pc", 64 + b, 128, 2), R("Nb", 128 * b, 128 * b + 128), stay) for b in range(2)], start=False, stop=False)
+            for b in range(2):
+                mm((r("pc", 64 + b, 128, 2), R("Md", 128 * b, 128 * b + 128), new), start=False, stop=False)
+            mm(*[(r("pc", 64, 128), R("WW", 15 - k, 143 - k), r("pr", k, 512, 8)) for k in range(8)], start=False)
+            tr(r("f", 256, 320), r("pc", 64, 128))
+            for o in (r("Rm", 0, 64), r("f", 192, 256)):
+                scan(o, R("m16", 0, 64), r("f", 256, 320), ALU.mult, ALU.max)
+            tt(r("f", 320, 384), ind(r("Rm"), R("su", 0, 4)), r("f", 192, 256), ALU.is_equal)
+            scan(r("O", 0, 56), r("f", 264, 320), r("f", 320, 376), ALU.add, ALU.mult)
+            ts(r("O", 6, 56, 16), r("O", 7, 56, 16), 2.0 ** 24, -2.0 ** 24, ALU.add, ALU.add)
+            tr(r("X"), r("O", 0, 64))
+            scan(r("O", 70, 120), R("m2", 6, 56), r("O", 6, 56), ALU.mult, ALU.subtract)
+            ll = r("O", 7, 120, 16)
+            mm(*[(r("pd", 4 * w, 4 * w + 4), R("nIf"), r("Rm", 7, 64, 16)) for w in range(2)], start=False)
+            tt(r("msg", M0 + 32, M0 + 40), ll, r("pd", 0, 8), ALU.max)
             if t + 1 < RO:
-                src, la = r("msg", M0, M0 + 72), r("land", L0 + MW, L0 + MW + 72)
+                src, la = r("msg", M0, M0 + MW), r("land", L0 + LW, L0 + LW + MW)
                 rid, pid, _ = topo.addr(dst)
                 en = topo.engines(core, dst)[:ENG]
                 mask = sum(1 << e for e in en)
@@ -408,57 +459,42 @@ def build(g, core, T, topo):
                 def send(src=src, la=la, sem=sem, mask=mask, rid=rid, pid=pid):
                     g.remote_dma(la[0], src[0], T.sem[sem], T.sem.sent, pid, rid, mask)
                 op("pool", send, [src], [la], "rem", len(en), sem=sem, cnt=len(en))
-            kk = r("f", 448, 452)
-            tt(kk, r("f", 408, 412), r("pd", 72, 76), ALU.add)
-            tt(r("X"), ind(kk, R("su", 4, 12)), R("dl"), ALU.mult)
-            mm((r("pc", 128, 256), R("B32"), r("X")))
+            a = (SEG + 6) * par
+            mm((r("pc", 128, 128 + SEG), R("Ib"), R("LR", a, a + SEG)), stop=False)
+            mm(*[(r("pc", 130 + x, 128 + SEG, 2), R("Row", 128 * x, 128 * x + 128), r("X")) for x in range(2)], start=False)
+            for c in (3, 2, 1, 0):
+                wd = 2 + 64 * (c // 2 + 1)
+                act(r("ab", SEG * c, SEG * c + wd), r("pc", 128, 128 + wd), AF.Abs, r("O", 6 + 16 * c, 7 + 16 * c), 1.0 / 8192)
+            end = (t, s) == (RO - 1, 1)
+            if end:
+                for ht in range(2):
+                    mm((r("pb", 48 + ht, 64, 2), R("Hs", 128 * ht, 128 * ht + 128), ll))
+                ts(r("u", 112, 128), r("pb", 48, 64), 0.5, None, ALU.add)
+                edits(112)
+            if t + 1 == RO:
+                for b in range(2):
+                    mm((r("pb", 192 + b, 200, 2, 0, 64), R("Out", 128 + 64 * b, 192 + 64 * b), r("msg", M0 + 32, M0 + 36)))
+                act(r("tmp", 128, 136, 1, 0, 64), r("pb", 192, 200, 1, 0, 64), AF.Identity, -OFF)
+                dmas("sp", [(T.yl[64 * s:64 * s + 64, :], T["tmp" + S][0:64, 128:136])], [r("tmp", 128, 136)], [], "fin", 2e3)
+            mm((r("pd", 16, 32), R("Ib"), R("LK", 16 * par, 16 * par + 16)), stop=False)
             for ht in range(2):
-                mm((r("pd", 80 + ht, 96, 2), R("Hs", 128 * ht, 128 * ht + 128), ll))
-            for c in range(4):
-                act(r("ab", 128 * c, 128 * c + 128), r("pc", 128, 256), AF.Abs, r("f", 408 + c, 409 + c), -1.0)
-            copy(r("u", 112, 128), r("pd", 80, 96))
-            if PAR["up"] == "dve" or (t, s) == (RO - 1, 1):
-                ts(r("nv", 0, 128), ind(Vw, r("u", 112, 120)), 32.0, 255.0, ALU.add, ALU.min)
-            else:
-                act(r("g1"), ind(Vw, r("u", 112, 120)), AF.Relu, 223.0, -1.0)
-                act(r("nv", 0, 128), r("g1"), AF.Identity, 255.0, -1.0)
-            act(r("nv", 128, 256), ind(Vw, r("u", 120, 128)), AF.Relu, -32.0)
-            scan(r("mn"), R("m128"), r("ab"), ALU.add, ALU.min)
-            tt(r("lo"), ind(r("mn"), R("su", 2, 3)), lane[par], ALU.not_equal)
-            for ht in range(2):
-                mm((r("pc", 256 + ht, 272, 2), R("Hb", 128 * ht, 128 * ht + 128), r("lo", 0, 8)))
-            tt(r("f", 472, 488), r("pc", 256, 272), dum, ALU.mult)
-            tt(r("f", 456, 472), r("f", 472, 488), r("pd", 80, 96), ALU.max)
-            copy(r("u", 128, 144), r("f", 456, 472))
+                mm((r("pd", 16 + ht, 32, 2), R("Hs", 128 * ht, 128 * ht + 128), ll), start=False, stop=False)
+            scan(r("mn"), R("mseg"), r("ab"), ALU.add, ALU.min)
+            mm(*[(r("pd", 16 + 8 * w + ht, 24 + 8 * w, 2), R("Hb", 128 * ht, 128 * ht + 128), r("mn", SEG - 1, 4 * SEG, SEG))
+                 for w in range(2) for ht in range(2)], start=False)
+            tt(r("f", 456, 472), r("pd", 16, 32), dum, ALU.min)
+            ts(r("u", 128, 144), r("f", 456, 472), 0.5, None, ALU.add)
+            if not end:
+                edits(128)
             copy(ind(Vw, r("u", 128, 144)), r("nv"))
+            ctx["ts"] = None
             if t + 1 < RO:
-                ctx["pri"] = (1, t + 1, s, -2)
-                mm(*[(r("pd", 112, 113), R("B32"), r("f", 192 + 8 * c, 193 + 8 * c)) for c in range(4)])
-                copy(r("n", 96, 97), r("pd", 112, 113))
-                ts(r("n", 100, 101), r("n", 96, 97), 1, None, ALU.bitwise_and)
-                ts(thr, r("n", 100, 101), 2.0 ** 17, float(((AT[t + 1] - 1) * 32 + 16) * 4096), ALU.mult, ALU.add)
-                ctx["ts"] = None
                 yield
-        ctx["ts"] = None
-        ctx["pri"] = (0, RO, s)
-        M0 = (RO - 1) * MW + 32
-        tr(r("f", 496, 560), r("msg", M0, M0 + 64))
-        for w in range(2):
-            for u in range(2):
-                for yb in range(4):
-                    mm((r("pb", 64 * w + 4 * u + yb, 64 * w + 64, 8, 0, 64), R("Out", 64 * u, 64 * u + 64),
-                        r("f", 496 + 32 * w + 8 * yb, 504 + 32 * w + 8 * yb)))
-        for u in range(2):
-            mm((r("pb", 128 + 4 * u, 132 + 4 * u, 1, 0, 64), R("Out", 64 * u, 64 * u + 64), r("msg", M0 + 64, M0 + 68)))
-        act(r("ks", 0, 136, 1, 0, 64), r("pb", 0, 136, 1, 0, 64), AF.Identity)
-        ks = T["ks" + S]
-        dmas("sp", [(T.yc[64 * s:64 * s + 64, :], ks[0:64, 0:64]), (T.yd[64 * s:64 * s + 64, :], ks[0:64, 64:128]),
-                    (T.yl[64 * s:64 * s + 64, :], ks[0:64, 128:136])], [r("ks", 0, 136)], [], "fin", 35e3)
         V = T["V" + S]
         for h in range(2):
             dmas("sp" if h == 0 else "act",
                  [(T.yv[64 * s + 16 * G:64 * s + 16 * G + 16, 2048 * h:2048 * h + 2048],
-                   V[32 * G + 16 * h:32 * G + 16 * h + 16, 2048 * h:2048 * h + 2048]) for G in range(4)], [Vw], [], "fin", 1 << 18)
+                   V[32 * G + 16 * h:32 * G + 16 * h + 16, V0 + 2048 * h:V0 + 2048 * h + 2048]) for G in range(4)], [Vw], [], "fin", 1 << 18)
 
     both = [stream(0), stream(1)]
     for t in range(RO):
@@ -472,85 +508,78 @@ def build(g, core, T, topo):
             bank = SCRATCH[nm][0] == "psum"
             if bank:
                 a, b = 0, 512
-            for a2, b2, w2, j in last.get(nm, []):
-                if (w or w2 or (bank and ops[j]["e"] != o["e"])) and a < b2 and a2 < b and j != o["i"]:
+            wrote, read = last.setdefault(nm, ([], []))
+            for a2, b2, j in wrote + (read if w or bank else []):
+                if a < b2 and a2 < b and j != o["i"] and (w or (a2, b2, j) in wrote or ops[j]["e"] != o["e"]):
                     dep.add(j)
         for (nm, a, b), w in acc:
             if SCRATCH[nm][0] == "psum":
                 a, b = 0, 512
-            lst = last.setdefault(nm, [])
             if w:
-                lst[:] = [e for e in lst if not (a <= e[0] and e[1] <= b)]
-            lst.append((a, b, w, o["i"]))
+                for lst in last[nm]:
+                    lst[:] = [e for e in lst if not (a <= e[0] and e[1] <= b)]
+            last[nm][0 if w else 1].append((a, b, o["i"]))
         o["dep"] = sorted(dep)
+        o["after"] = []
+    for e, names in (("act", "w"), ("dve", "Qz")):
+        line = [o for o in ops if o["e"] == e and o["ts"] and o["wr"][0][0] in names]
+        for a, b in zip(line, line[1:]):
+            b["after"].append(a["i"])
     return ops
 
 
-def times(o, start, c, st):
-    k, a = o["k"], o["n"]
-    if k == "dma":
-        free = start + 0.06 * a[0]
-        st["dma"] = max(st["dma"], start + c["dma"]) + a[1] / c["bw"]
-        return free, st["dma"]
-    if k == "rem":
-        return start + 0.5, start + c["rem"]
-    if k == "pe":
-        d = a * c["cyc"]
-        return start + d, start + d + c["fix"]
-    d = c["fix"] + a * c["cyc"] * (c[k] if k != "cyc" else 1)
-    return start + d, start + d
-
-
-def dues(ops, c):
-    out = [None] * len(ops)
+def table(ops, c):
+    out = []
     for o in ops:
-        if o["key"][0] == "z":
-            out[o["i"]] = (HALF * (2 * RO - 1) + 10 + 0.3 * o["key"][1], 0.0)
-        elif o["key"] in DUE:
-            d, w = DUE[o["key"]]
-            out[o["i"]] = (d + (HALF * (2 * o["ts"][0] + o["ts"][1]) if o["ts"] else 0.0), w)
-    need = [1e9] * len(ops)
-    for o in reversed(ops):
-        i = o["i"]
-        if out[i] is None and need[i] < 1e9:
-            out[i] = (need[i] - times(o, 0.0, c, {"dma": 0.0})[1] - 0.3, 0.0)
-        if out[i] is not None:
-            for j in o["dep"]:
-                need[j] = min(need[j], out[i][0])
-    for o in ops:
-        if out[o["i"]] is None:
-            out[o["i"]] = (max([out[j][0] for j in o["dep"]] + [-100.0]) + 0.1, 0.0)
-        if o["k"] == "dma" and not o["dep"]:
-            out[o["i"]] = (-1000.0 + o["i"], 0.0)
+        k, a = o["k"], o["n"]
+        dep = [(j, -c["fix"] if o["e"] == "pe" and ops[j]["e"] == "pe" else c["lat"]) for j in o["dep"]] + [(j, 0.0) for j in o["after"]]
+        if k == "dma":
+            out.append((o["e"], 0.06 * a[0], c["dma"], a[1] / c["bw"], dep))
+        elif k == "rem":
+            out.append((o["e"], 0.5, c["rem"], 0.0, dep))
+        elif k == "pe":
+            out.append((o["e"], a * c["cyc"], a * c["cyc"] + c["fix"], 0.0, dep))
+        else:
+            d = c["fix"] + a * c["cyc"] * (c[k] if k != "cyc" else 1)
+            out.append((o["e"], d, d, 0.0, dep))
     return out
 
 
-def plan(ops, c=COST):
-    due = dues(ops, c)
-    free = {e: 0.0 for e in ("act", "dve", "pe", "pool", "sp")}
-    st = {"dma": 0.0}
+def plan(ops, tab, look):
+    n = len(ops)
     users = [[] for o in ops]
-    left = [len(o["dep"]) for o in ops]
-    for o in ops:
-        for j in o["dep"]:
-            users[j].append(o["i"])
-    rdy = {o["i"]: 0.0 for o in ops if not o["dep"]}
-    at = [0.0] * len(ops)
-    order = []
+    for i in range(n):
+        for j, l in tab[i][4]:
+            users[j].append((i, l))
+    rest = [0.0] * n
+    for i in range(n - 1, -1, -1):
+        rest[i] = tab[i][2] + tab[i][3] + max([0.0] + [l + rest[j] for j, l in users[i]])
+    left = [len(x[4]) for x in tab]
+    head = [min(i for i in range(n) if ops[i]["wr"] and ops[i]["wr"][0][0] == "w")]
+    for i in head:
+        rest[i] += 50.0
+        head.extend(j for j, l in tab[i][4] if j not in head)
+    for i in range(n):
+        if tab[i][3] and not left[i]:
+            rest[i] = 1e6 - i
+    free, dma, at, order, start = {}, 0.0, [0.0] * n, [], [0.0] * n
+    rdy = {i: 0.0 for i in range(n) if not left[i]}
     while rdy:
-        est = {i: max(v, free[ops[i]["e"]]) for i, v in rdy.items()}
-        i0 = min(est, key=est.get)
-        e = ops[i0]["e"]
-        i = min((i for i in est if ops[i]["e"] == e and est[i] <= est[i0] + due[i][1]), key=lambda i: (due[i][0], i))
-        free[e], done = times(ops[i], est[i], c, st)
+        est = {i: max(v, free.get(tab[i][0], 0.0)) for i, v in rdy.items()}
+        i0 = min(est, key=lambda i: (est[i], -rest[i]))
+        e = tab[i0][0]
+        i = max((i for i in est if tab[i][0] == e and est[i] <= est[i0] + look), key=lambda i: (rest[i], -i))
+        start[i], free[e], done = est[i], est[i] + tab[i][1], est[i] + tab[i][2]
+        if tab[i][3]:
+            dma = done = max(dma, done) + tab[i][3]
         del rdy[i]
         order.append(i)
-        for j in users[i]:
-            at[j] = max(at[j], done + (0 if e == "pe" and ops[j]["e"] == "pe" else c["lat"]))
+        for j, l in users[i]:
+            at[j] = max(at[j], done + l)
             left[j] -= 1
             if left[j] == 0:
                 rdy[j] = at[j]
-    return order
+    return order, start, order.index(head[0])
 
 
 def in_order(order, pre):
@@ -570,33 +599,50 @@ def in_order(order, pre):
     return out
 
 
-def table(ops, c):
-    out = []
-    for o in ops:
-        dep = [(j, 0.0 if o["e"] == "pe" and ops[j]["e"] == "pe" else c["lat"]) for j in o["dep"]]
-        if o["k"] == "dma":
-            out.append((o["e"], 0.06 * o["n"][0], c["dma"], o["n"][1] / c["bw"], dep))
-        else:
-            out.append((o["e"],) + times(o, 0.0, c, None) + (0.0, dep))
-    return out
-
-
-def run_through(tab, order):
-    free, done, start, dma = {}, [0.0] * len(tab), [0.0] * len(tab), 0.0
-    for i in order:
+def walk(tab, order, at=0, old=None, prev=None, pos=None):
+    n = len(tab)
+    if old:
+        done, why, free, prev = list(old[1]), list(old[2]), list(old[3]), dict(prev)
+        dma = max([0.0] + [done[i] for i in old[4] if pos[i] < at])
+    else:
+        done, why, free, prev, dma = [0.0] * n, [0] * n, [0.0] * (n + 1), dict.fromkeys(QUEUES, n), 0.0
+    for i in order[at:]:
         e, hold, rdy, wire, dep = tab[i]
-        t = free.get(e, 0.0)
+        w = prev[e]
+        t, w = free[w], -1 - w
+        for j, l in dep:
+            if done[j] + l >= t:
+                t, w = done[j] + l, j
+        why[i], free[i], prev[e] = w, t + hold, i
+        if wire:
+            dma = done[i] = max(dma, t + rdy) + wire
+        else:
+            done[i] = t + rdy
+    return max(done), done, why, free, old[4] if old else [i for i in range(n) if tab[i][3]]
+
+
+def probe(tab, order, at, old, prev, pos):
+    was, done, free, prev = old[1], list(old[1]), list(old[3]), dict(prev)
+    shift, run, dma = 1e9, 0, max([0.0] + [was[i] for i in old[4] if pos[i] < at])
+    for i in order[at:]:
+        e, hold, rdy, wire, dep = tab[i]
+        t = free[prev[e]]
         for j, l in dep:
             if done[j] + l > t:
                 t = done[j] + l
-        start[i] = t
-        free[e] = t + hold
+        free[i], prev[e] = t + hold, i
         if wire:
-            dma = max(dma, t + rdy) + wire
-            done[i] = dma
+            dma = done[i] = max(dma, t + rdy) + wire
+            continue
+        done[i] = t = t + rdy
+        t -= was[i]
+        if -1e-9 < t - shift < 1e-9:
+            run += 1
+            if run == 60:
+                return old[0] + shift
         else:
-            done[i] = t + rdy
-    return start, max(done)
+            shift, run = t, 0
+    return max(done)
 
 
 def place(line, t, h):
@@ -616,10 +662,9 @@ def place(line, t, h):
     return t
 
 
-def tighten(ops, order):
+def tighten(ops, tabs, tab, look, seed):
     n = len(ops)
-    tabs = [table(ops, dict(COST, cyc=0.00083 * m[0], gat=m[1], sca=m[2], fix=m[3], lat=m[4], rem=m[5])) for m in SPREAD]
-    tab = tabs.pop()
+    order, start, cut = plan(ops, tab, look)
     res = ["dma" if x[3] else x[0] for x in tab]
     hold = [x[3] or x[1] for x in tab]
     lead = [x[2] if x[3] else 0.0 for x in tab]
@@ -630,15 +675,17 @@ def tighten(ops, order):
         for j, d in pre[i]:
             suc[j].append((i, d))
     pre0, suc0 = [[j for j, d in p] for p in pre], [[j for j, d in p] for p in suc]
-    loads = sum(o["k"] == "dma" and not o["dep"] for o in ops)
-    seed = [PAR["seed"]]
+    head = [n] * n
+    for q, i in enumerate(order[:cut]):
+        head[i] = q
+    seed = [seed]
 
     def draw():
         seed[0] = (seed[0] * 1103515245 + 12345) % 2147483648
         return seed[0] / 2147483648.0
-    best = sum(run_through(x, order)[1] for x in tabs) / len(tabs)
-    start, span = run_through(tab, order)
-    for step in range(PAR["steps"]):
+    norm = [walk(x, order)[0] * len(tabs) for x in tabs]
+    best, span = 1.0, max(start)
+    for step in range(PAR["steps"][0]):
         a, w, j = draw() * (span + 10) - 10, (3, 8, 20)[int(draw() * 3)], (0.2, 0.6, 1.6)[int(draw() * 3)]
         st = [x + j * (draw() + draw() + draw() - 1.5) if a < x < a + w else x for x in start]
         back, lines = [0.0] * n, {}
@@ -646,13 +693,94 @@ def tighten(ops, order):
             t = max([0.0, done[i] - hold[i]] + [back[k] + hold[k] + d - hold[i] for k, d in suc[i]])
             back[i] = place(lines.setdefault(res[i], ([], [])), t, hold[i])
         lines = {}
-        for i in in_order(sorted(range(n), key=lambda i: (i >= loads, -(back[i] + hold[i]) if i >= loads else 0, i)), pre0):
+        for i in in_order(sorted(range(n), key=lambda i: (head[i], -(back[i] + hold[i]), i)), pre0):
             st[i] = place(lines.setdefault(res[i], ([], [])), max([lead[i]] + [st[j] + d for j, d in pre[i]]), hold[i])
-        new = in_order(sorted(range(n), key=lambda i: (i >= loads, st[i] - lead[i] if i >= loads else 0, i)), pre0)
-        v = sum(run_through(x, new)[1] for x in tabs) / len(tabs)
-        if v <= best + 0.05:
+        new = in_order(sorted(range(n), key=lambda i: (head[i], st[i] - lead[i], i)), pre0)
+        v = sum(walk(x, new)[0] / m for x, m in zip(tabs, norm))
+        if v <= best + 0.0002:
             best, start, order = v, st, new
     return order
+
+
+def chain(res):
+    end, done, why = res[:3]
+    i, pairs = done.index(end), []
+    while why[i] != -1 - len(done):
+        if why[i] < 0:
+            pairs.append((-1 - why[i], i))
+        i = why[i] if why[i] >= 0 else -1 - why[i]
+    return pairs
+
+
+def move(order, pos, pre, a, b, ahead):
+    ia, ib = pos[a], pos[b]
+    if ia > ib or ib - ia > 150:
+        return False
+    seg = order[ia:ib + 1]
+    if ahead:
+        grp, need = {b}, set(pre[b])
+        for x in reversed(seg[:-1]):
+            if x in need:
+                grp.add(x)
+                need |= pre[x]
+        new = [x for x in seg if x in grp] + [x for x in seg if x not in grp]
+    else:
+        grp = {a}
+        for x in seg[1:]:
+            if pre[x] & grp:
+                grp.add(x)
+        new = [x for x in seg if x not in grp] + [x for x in seg if x in grp]
+    if a in grp and b in grp:
+        return False
+    order[ia:ib + 1] = new
+    for q, x in enumerate(new):
+        pos[x] = ia + q
+    return True
+
+
+def anneal(tabs, order, fixed, steps, heat, seed):
+    n = len(order)
+    pre = [set(j for j, l in x[4]) for x in tabs[0]]
+    res = [walk(x, order) for x in tabs]
+    norm = [x[0] * len(tabs) for x in res]
+    now, low, best = 1.0, 1.0, order
+    spot, links = [0] * n, [chain(x) for x in res]
+    for q, x in enumerate(order):
+        spot[x] = q
+    for step in range(steps):
+        seed = (seed * 1103515245 + 12345) % 2147483648
+        pairs = links[(seed >> 8) % len(tabs)]
+        seed = (seed * 1103515245 + 12345) % 2147483648
+        a, b = pairs[(seed >> 8) % len(pairs)]
+        if a in pre[b] or a < fixed:
+            continue
+        new, pos, first = list(order), list(spot), spot[a]
+        if not move(new, pos, pre, a, b, seed >> 29 & 1):
+            continue
+        seed = (seed * 1103515245 + 12345) % 2147483648
+        bound = now - heat * (1 - step / steps) * math.log((seed + 1) / 2147483648.0)
+        prev = dict.fromkeys(QUEUES, n)
+        for i in new[:first]:
+            prev[tabs[0][i][0]] = i
+        if sum(probe(x, new, first, y, prev, pos) / m for x, y, m in zip(tabs, res, norm)) > bound:
+            continue
+        r = [walk(x, new, first, y, prev, pos) for x, y in zip(tabs, res)]
+        v = sum(x[0] / m for x, m in zip(r, norm))
+        if v <= bound:
+            now, order, res, spot, links = v, new, r, pos, [chain(x) for x in r]
+            if v < low:
+                low, best = v, new
+    return best
+
+
+def arrange(ops):
+    tabs = [table(ops, cost(m)) for m in SPREAD]
+    tab = tabs.pop()
+    loads = sum(o["k"] == "dma" and not o["dep"] for o in ops)
+    starts = [anneal(tabs, tighten(ops, tabs, tab, look, seed), loads, PAR["steps"][1], PAR["heat"], seed) for look, seed in PAR["starts"]]
+    norm = [walk(x, starts[0])[0] for x in tabs]
+    order = min(starts, key=lambda o: sum(walk(x, o)[0] / m for x, m in zip(tabs, norm)))
+    return anneal(tabs, order, loads, PAR["steps"][2], PAR["heat"], 1)
 
 
 ORDER = []
@@ -663,27 +791,31 @@ def rank_program(g, core, T, topo):
         return
     ops = build(g, core, T, topo)
     if not ORDER:
-        ORDER.extend(tighten(ops, plan(ops)))
-    order = ORDER
+        ORDER.extend(arrange(ops))
     queue = {"act": g.scalar, "dve": g.vector, "pe": g.tensor, "pool": g, "sp": g.sync}
     need = set()
     for o in ops:
         for j in o["dep"]:
             if not (o["e"] == "pe" and ops[j]["e"] == "pe"):
                 need.add(j)
-    mark, count, seen, total = {}, {}, {}, {"fin": 0, "sent": 0}
-    for i in order:
+    mark, count, total, knew, when = {}, {}, {"fin": 0, "sent": 0}, {}, {}
+    seen = {e: {} for e in queue}
+    for i in ORDER:
         o = ops[i]
         e = o["e"]
         want = {}
         for j in o["dep"]:
             if not (e == "pe" and ops[j]["e"] == "pe"):
                 sem, v = mark[j]
-                want[sem] = max(want.get(sem, 0), v)
-        for sem, v in want.items():
-            if seen.get((e, sem), 0) < v:
+                want[sem] = max(want.get(sem, (0, 0)), (v, j))
+        for sem, (v, j) in sorted(want.items(), key=lambda x: -when[x[1][1]]):
+            if seen[e].get(sem, 0) < v:
                 queue[e].wait_ge(T.sem[sem], v)
-                seen[(e, sem)] = v
+                seen[e][sem] = v
+                for sem, v in knew[j].items():
+                    seen[e][sem] = max(seen[e].get(sem, 0), v)
+        knew[i] = dict(seen[e]) if o["k"] != "rem" else {}
+        when[i] = len(when)
         ins = o["fn"]()
         if o["sem"] is not None:
             mark[i] = (o["sem"], o["cnt"])

@@ -5,16 +5,25 @@ RO, STEP = 6, 2
 MT = [32, 24, 40, 28, 48, 20]
 AT = [8, 10, 7, 9, 6, 11]
 PAR = {
-    "chs": [[1024, 512, 1024, 1024], [1024, 1024, 1024, 512], [512, 512]],
-    "dve": (1,),
-    "dveg": ((5, 1, 4),),
-    "turn": (0, 96, 224, 352, 512),
-    "piece": 64,
+    "subs": {"all": [3584, 3584, 1024], "last": [3584, 3584, 1024]},
+    "sums": {"all": [512], "last": [256, 256]},
+    "main": {"all": ([1024, -512, 1024, 1024, 1024, 1024, 1024, 512, 512, 512], [1024, 512, 1024, 1024, 1024, 1024, 1024, 512, 512, 512],
+                     [1024, 512, 1024, 1024, 1024, 1024, 1024, 512, 512, 512]),
+             "last": ([1024, -512, 1024, 1024, -512, 512, 1024, 1024, 512, 512, 512], [1024, 512, 1024, 1024, 1024, 1024, 1024, 512, 512, 512],
+                      [1024, 512, 1024, 1024, 1024, 1024, 1024, 512, 512, 512])},
+    "turn": (0, 128, 512),
+    "lits": (0, 128, 256, 384, 512),
+    "vec": ("sg", "d", "f96"),
+    "gaps": 4096,
+    "piece": 112,
     "gcut": [[(0, 512), (512, 1024), (1024, 1536), (1536, 2048)], [(0, 1024), (1024, 2048)]],
     "pcut": [[(0, 512), (512, 1024), (1024, 1536), (1536, 1792), (1792, 2048)], [(0, 512), (512, 1024), (1024, 1536), (1536, 2048)]],
-    "starts": ((0.2, 2), (0.25, 6), (0.17, 4), (0.22, 3)),
-    "steps": (100, 1200, 20000),
-    "heat": 0.0001,
+    "look": 0.22,
+    "seed": 4,
+    "shakes": 50,
+    "middle": ((2, 6000, 0.004), (1, 10000, 0.002), (1, 14000, 0.001)),
+    "start": ((1, 8000, 0.001), (1, 12000, 0.0005)),
+    "end": ((1, 6000, 0.0015), (1, 12000, 0.0007)),
 }
 CW = 1024
 ENG = 16
@@ -27,17 +36,17 @@ OFF = V0 - 0.5
 
 SCRATCH = {
     "cin": ("sbuf", [128, 136], I), "cinf": ("sbuf", [128, 136], F),
-    "pidx": ("sbuf", [128, 16], I), "pf": ("sbuf", [128, 24], F),
-    "ones": ("sbuf", [128, 264], F), "If": ("sbuf", [128, 128], F), "nIf": ("sbuf", [128, 128], F),
+    "pidx": ("sbuf", [128, 16], I), "pf": ("sbuf", [128, 32], F),
+    "ones": ("sbuf", [128, 264], F), "If": ("sbuf", [128, 128], F),
     "Ib": ("sbuf", [128, 128], B), "nIb": ("sbuf", [128, 128], B),
     "SW0": ("sbuf", [128, 160], F), "SW1": ("sbuf", [128, 160], F), "Z0": ("sbuf", [128, 132], F), "Z1": ("sbuf", [128, 132], F),
-    "In0": ("sbuf", [128, 160], F), "In1": ("sbuf", [128, 160], F), "Out": ("sbuf", [128, 256], F), "Hs": ("sbuf", [128, 256], F),
+    "In0": ("sbuf", [128, 128], F), "In1": ("sbuf", [128, 128], F), "Out": ("sbuf", [128, 256], F), "Hs": ("sbuf", [128, 256], F),
     "J": ("sbuf", [128, 258], F), "Mp": ("sbuf", [128, 288], F), "Md": ("sbuf", [128, 256], F), "Nb": ("sbuf", [128, 256], B),
     "rows": ("sbuf", [128, 800], F), "WW": ("sbuf", [128, 144], B), "VB": ("sbuf", [128, 144], B), "nVB": ("sbuf", [128, 144], B),
-    "Bn": ("sbuf", [128, 128], F), "Row": ("sbuf", [128, 256], F), "cb": ("sbuf", [128, 384], B), "Dup": ("sbuf", [128, 128], B),
+    "Bn": ("sbuf", [128, 128], F), "Row": ("sbuf", [128, 256], F), "cb": ("sbuf", [128, 458], B), "Dup": ("sbuf", [128, 128], B),
     "o64": ("sbuf", [128, 128], B), "CK": ("sbuf", [128, 512], B), "TB": ("sbuf", [128, 64], B), "YC": ("sbuf", [128, 64], B),
     "m8": ("sbuf", [128, CW], B), "m2": ("sbuf", [128, 64], B),
-    "m16": ("sbuf", [128, 512], B), "mseg": ("sbuf", [128, 4 * SEG], B), "LR": ("sbuf", [128, 2 * SEG + 12], B), "LK": ("sbuf", [128, 32], B),
+    "m16": ("sbuf", [128, 64], B), "mseg": ("sbuf", [128, 4 * SEG], B), "LR": ("sbuf", [128, 2 * SEG + 12], B), "LK": ("sbuf", [128, 32], B),
     "sm": ("sbuf", [128, 64], F), "su": ("sbuf", [128, 16], U), "Hb": ("sbuf", [128, 256], B),
     "w": ("sbuf", [128, 8192], B), "Q": ("sbuf", [128, 8192 + 16], B), "z": ("sbuf", [128, 8192], B),
 }
@@ -45,7 +54,7 @@ for _s in "01":
     SCRATCH.update({
         "V" + _s: ("sbuf", [128, VW], B), "G" + _s: ("sbuf", [128, 2048], I), "P" + _s: ("sbuf", [128, 4096], F),
         "tmp" + _s: ("sbuf", [128, 1024], F), "g2" + _s: ("sbuf", [128, 64], B), "sg" + _s: ("sbuf", [128, 48], B),
-        "usg" + _s: ("sbuf", [128, 1024], B), "img" + _s: ("sbuf", [128, 512], F), "imT" + _s: ("sbuf", [128, 512], F),
+        "usg" + _s: ("sbuf", [128, 1024], B), "img" + _s: ("sbuf", [128, 512], U), "imT" + _s: ("sbuf", [128, 512], F),
         "of" + _s: ("sbuf", [128, 512], U), "ks" + _s: ("sbuf", [128, 512], F),
         "um" + _s: ("sbuf", [128, 512], B), "pr" + _s: ("sbuf", [128, 512], B),
         "ab" + _s: ("sbuf", [128, 4 * SEG], B), "mn" + _s: ("sbuf", [128, 4 * SEG], B),
@@ -60,12 +69,13 @@ SEMAPHORES = (["act", "dve", "pe", "pool", "sent", "ldc", "fin", "ldv", "ldz0", 
               + ["arr%d_%d" % (t, s) for t in range(1, RO) for s in range(2)])
 QUEUES = ("act", "dve", "pe", "pool", "sp")
 
-SPREAD = [(1.0, 1.56, 3.8, .06, .1, 3.0), (1.05, 1.2, 5, .03, .2, 3.5), (1.4, 1.9, 2.5, .05, .08, 4.5),
-          (1.1, 1.9, 4.5, .03, .15, 3.0), (1.35, 1.2, 3, .06, .08, 2.5), (1.15, 1.56, 3.8, .05, .12, 3.3)]
+SPREAD = [(1.0, 1.56, 3.8, .05, .1, 3.0, 1.0, 1.5, .05, .02), (1.15, 1.25, 5, .03, .18, 3.5, 2.0, 2.0, .12, .04),
+          (1.4, 1.85, 2.5, .05, .08, 3.5, 1.5, 1.2, .03, .05), (1.15, 1.56, 3.8, .05, .12, 3.3, 1.2, 1.6, .05, .03)]
 
 
 def cost(m):
-    return {"cyc": 0.00083 * m[0], "gat": m[1], "sca": m[2], "fix": m[3], "lat": m[4], "rem": m[5], "dma": 2.0, "bw": 200e3}
+    return {"cyc": 0.00083 * m[0], "gat": m[1], "sca": m[2], "fix": m[3], "lat": m[4], "rem": m[5], "hold": m[6], "dma": m[7], "bw": 200e3,
+            "act": m[8], "mm": m[9]}
 
 
 def build(g, core, T, topo):
@@ -133,7 +143,7 @@ def build(g, core, T, topo):
            max(64, (0.5 if two(o, d0, d1) else 1) * o[4]))
 
     def tr(o, i):
-        op("dve", lambda: g.vector.transpose(o[0], i[0]), [i], [o], "cyc", max(64, i[4]))
+        op("dve", lambda: g.vector.transpose(o[0], i[0]), [i], [o], "cyc", max(64, (0.5 if two(o, i) else 1) * i[4]))
 
     def mset(o, v):
         op("dve", lambda: g.vector.memset(o[0], v), [], [o], "cyc", max(64, (0.5 if two(o) else 1) * o[4]))
@@ -152,7 +162,7 @@ def build(g, core, T, topo):
                 last = g.tensor.matmul(o[0], l[0], r[0], start and q == 0, stop and q == len(terms) - 1)
             return last
         c = sum(max(64, r[4]) * (1 if two(l) else 4) for o, l, r in terms)
-        op("pe", fn, [x for t in terms for x in t[1:]], [t[0] for t in terms], "pe", c)
+        op("pe", fn, [x for t in terms for x in t[1:]], [t[0] for t in terms], "pe", (c, len(terms)))
 
     def iota(o, pat, base, cm=0):
         if SCRATCH[o[1]][2] == I:
@@ -178,12 +188,12 @@ def build(g, core, T, topo):
                 q.dma_start(o, i).then_inc(T.sem[sem], 16)
         op(eng, fn, rd, wr, "dma", (len(pairs), nbytes), sem=sem, cnt=16 * len(pairs))
 
-    chunks, at = [], 0
-    for grp in PAR["chs"]:
-        chunks.append([])
-        for cw in grp:
-            chunks[-1].append((sum(map(len, chunks)), at, cw))
-            at += cw
+    def cut(sizes):
+        out, at = [], 0
+        for cw in sizes:
+            out.append((at, abs(cw), cw < 0))
+            at += abs(cw)
+        return out
 
     dmas("sp", [(T.cin[:, 0:64], T.cla[:]), (T.cin[:, 64:128], T.par[:]), (T.cin[:, 128:136], T.lit[:])], [], [R("cin")], "ldc", 70e3)
     for q in range(2):
@@ -198,18 +208,27 @@ def build(g, core, T, topo):
 
     mset(R("ones"), 1.0)
     iota(R("pidx", 0, 1), [[0, 1]], 0, 1)
-    perm(R("In0"), [[16, 5], [-1000, 2], [1, 16]], 1000)
-    perm(R("In1"), [[16, 5], [-1000, 2], [1, 16]], 1064)
-    perm(R("If"), [[1, 128]], 0)
     perm(R("J"), [[1, 129], [-1000, 2]], 1000)
-    fld = {"blk": (4, 7), "G": (5, 3), "r15": (0, 15), "y": (1, 1), "b0": (0, 1), "b": (3, 1), "B10": (2, 3)}
+    for s in range(2):
+        perm(R("In%d" % s), [[16, 4], [0, 2], [1, 16]], 64 * s)
+    perm(R("If"), [[1, 128]], 0)
+    fld = {"blk": (4, 7), "G": (5, 3), "r15": (0, 15), "y": (1, 1), "b0": (0, 1), "b": (3, 1), "B10": (2, 3), "h": (4, 1), "r3": (0, 3), "b2": (2, 1)}
     col = {}
     for q, (nm, (sh, ms)) in enumerate(fld.items()):
         ts(R("pidx", q + 1, q + 2), R("pidx", 0, 1), sh, ms, ALU.logical_shift_right, ALU.bitwise_and)
-        col[nm] = R("pf", q + 1, q + 2)
-    copy(R("pf", 0, 8), R("pidx", 0, 8))
+        col[nm] = R("pf", q + 21, q + 22)
+    copy(R("pf", 20, 31), R("pidx", 0, 11))
     copy(R("cinf"), R("cin"))
-    act(R("nIf"), R("If"), AF.Identity, 0.0, -1.0)
+    ts(R("pf", 0, 1), col["b"], -63.0, None, ALU.mult)
+    ts(R("pf", 1, 2), col["r15"], 8.0, R("pf", 0, 1), ALU.mult, ALU.add)
+    ts(R("pf", 2, 3), col["h"], 4.0, R("pf", 1, 2), ALU.mult, ALU.add)
+    iota(R("rows", 40, 44), [[64, 2], [2, 2]], 0)
+    ts(R("su", 4, 8), R("rows", 40, 44), R("pf", 2, 3), None, ALU.add)
+    ts(R("pf", 3, 4), col["b2"], col["h"], 100.0, ALU.not_equal, ALU.mult)
+    ts(R("pf", 4, 5), col["r3"], 8.0, col["b"], ALU.mult, ALU.add)
+    iota(R("rows", 44, 48), [[2, 4]], 0)
+    ts(R("rows", 48, 52), R("rows", 44, 48), R("pf", 3, 4), R("pf", 4, 5), ALU.add, ALU.add)
+    ts(R("su", 8, 12), R("rows", 48, 52), 32.0, None, ALU.min)
     mset(R("cb", 256, 384), 1.0)
     perm(R("Dup", p1=64), [[16, 4], [0, 2], [1, 16]], 0, R("cb", 256, 384, p1=64))
     for q in range(8):
@@ -236,11 +255,11 @@ def build(g, core, T, topo):
     act(R("nVB"), R("VB"), AF.Identity, 0.0, -1.0)
     mset(R("YC", 0, 32), 8.5 * 65536)
     mset(R("YC", 32, 64), -8.5 * 65536)
-    iota(R("CK", p1=64), [[0, 32], [-4096, 16]], 15 * 4096)
-    mset(R("CK", p0=64), float(1 << 20))
-    mset(R("o64"), 1.0 / 64)
-    mset(R("m16"), 1.0)
-    mset(R("m16", 0, 512, 16), 0.0)
+    mset(R("CK"), 4096.0)
+    mset(R("CK", 0, 512, 16), -2.0 ** 26)
+    act(R("o64"), R("ones", 0, 128), AF.Identity, 0.0, 1.0 / 64)
+    fill(R("m16"), 1)
+    fill(R("m16", 0, 64, 16), 0)
     iota(R("rows", 304, 448), [[1, 9], [-BIG, 16]], 15 * BIG)
     ts(R("WW"), R("rows", 304, 448), col["blk"], None, ALU.is_equal)
     iota(R("rows", 704, 736), [[32, 32]], 30)
@@ -249,11 +268,14 @@ def build(g, core, T, topo):
     ts(R("pf", 10, 11), col["r15"], -0.125, 0.875, ALU.mult, ALU.add)
     ts(R("pf", 11, 12), col["r15"], 15.0, OFF, ALU.is_equal, ALU.mult)
     ts(R("pf", 12, 13), R("pf", 10, 11), 0.0, R("pf", 11, 12), ALU.max, ALU.add)
-    ts(R("TB"), R("ones", 0, 64), R("pf", 12, 13), None, ALU.mult)
+    act(R("TB"), R("ones", 0, 64), AF.Identity, R("pf", 12, 13), 0.0)
     fill(R("cb", 0, 128), -8192)
     fill(R("cb", 128, 256), -2 ** 21)
+    fill(R("cb", 384, 448), 2 ** 15)
+    fill(R("cb", 448, 456), 2 ** 19)
     for b in range(2):
         perm(R("Nb", 128 * b, 128 * b + 128), [[16, 8], [1000, 2], [1, 8]], 8 * b, R("cb", 0, 128))
+        perm(R("Nb", 128 * b + 15, 128 * b + 128, 16), [[16, 8]], 8 * b, R("cb", 448, 456))
         perm(R("Mp", 144 * b, 144 * b + 144), [[16, 9], [-1000, 2], [1, 8]], 1000 + 8 * b)
         tt(R("Md", 128 * b, 128 * b + 128), R("Mp", 144 * b, 144 * b + 128), R("Mp", 144 * b + 1, 144 * b + 129), ALU.subtract)
     fill(R("Md", 7, 256, 16), 0)
@@ -271,8 +293,8 @@ def build(g, core, T, topo):
         perm(R("Hb", 128 * ht, 128 * ht + 128), [[32, 4], [0, 2], [1, 16]], 16 * ht, R("cb", 128, 256))
     fill(R("mseg"), 0)
     fill(R("mseg", 0, 4 * SEG, SEG), 1 << 23)
-    act(R("pf", 13, 14), col["b0"], AF.Identity, 0.0, 16.0)
-    act(R("pf", 14, 15), col["B10"], AF.Identity, R("pf", 13, 14), 2.0)
+    act(R("pf", 13, 14), col["b0"], AF.Identity, 0.0, 16.0 * 8192)
+    act(R("pf", 14, 15), col["B10"], AF.Identity, R("pf", 13, 14), 2.0 * 8192)
     for par in range(2):
         wx, wy = ((1, 32), (32, 1))[par]
         a = (SEG + 6) * par
@@ -281,12 +303,12 @@ def build(g, core, T, topo):
             iota(R("LR", a + 2 + 64 * (c // 2) + c % 2, a + 66 + 64 * (c // 2), 2), [[-64, 8], [-32 * wy, 2], [-512, 2]], -32 * (64 * (c // 2) + wx * (c % 2) + 1))
         for w in range(2):
             iota(R("rows", 16 * par + 8 * w, 16 * par + 8 * w + 8), [[64, 2], [wx, 2], [8, 2]], 1)
-        act(R("pf", 15 + par, 16 + par), col["y"], AF.Identity, R("pf", 14, 15), float(wy))
-        ts(R("LK", 16 * par, 16 * par + 16), R("rows", 16 * par, 16 * par + 16), R("pf", 15 + par, 16 + par), 8192.0, ALU.add, ALU.mult)
+        act(R("pf", 15 + par, 16 + par), col["y"], AF.Identity, R("pf", 14, 15), 8192.0 * wy)
+        act(R("LK", 16 * par, 16 * par + 16), R("rows", 16 * par, 16 * par + 16), AF.Identity, R("pf", 15 + par, 16 + par), 8192.0)
     iota(R("rows", 776, 792), [[16, 16]], V0 + 4096)
     dum = R("sm", 32, 48)
-    ts(dum, R("rows", 776, 792), col["r15"], -0.5, ALU.add, ALU.add)
-    iota(R("rows", 32, 36), [[16, 4]], 15)
+    act(dum, R("rows", 776, 792), AF.Identity, col["r15"])
+    iota(R("rows", 32, 36), [[16, 4]], 7)
     act(R("pf", 17, 18), col["b"], AF.Identity, 0.0, 64.0)
     ts(R("sm", 48, 52), R("rows", 32, 36), R("pf", 17, 18), 64.0, ALU.add, ALU.min)
     keep(R("su", 0, 4), R("sm", 48, 52))
@@ -306,22 +328,20 @@ def build(g, core, T, topo):
         Vw, Vm = r("V"), r("V", V0, V0 + 4096)
 
         def clauses(src, bank, w, y):
-            tr(r("f", 128 + 32 * w, 160 + 32 * w), src)
-            for u in range(2):
-                for yb in range(4):
-                    mm((r(bank, 64 + 4 * u + yb, 128, 8, 0, 64), R("Out", 64 * u, 64 * u + 64), r("f", 128 + 32 * w + 8 * yb, 136 + 32 * w + 8 * yb)))
+            tr(r("f", 432 + 40 * w, 464 + 40 * w), src)
+            act(r("f", 128 + 64 * w, 192 + 64 * w), ind(r("f", 432 + 40 * w, 465 + 40 * w), R("su", 8, 12)), AF.Identity)
+            mm(*[(r(bank, 64, 128, 1, 0, 64), R("Out", 64 * u, 64 * u + 64), r("f", 128 + 64 * w, 192 + 64 * w)) for u in range(2)])
             act(r("tmp", 64 * w, 64 * w + 64, 1, 0, 64), r(bank, 64, 128, 1, 0, 64), AF.Identity)
             dmas("sp", [(y[64 * s:64 * s + 64, :], T["tmp" + S][0:64, 64 * w:64 * w + 64])], [r("tmp", 64 * w, 64 * w + 64)], [], "fin", 16e3)
 
         def edits(a):
             act(r("nv", 128, 256), ind(Vw, r("u", a + 8, a + 16)), AF.Relu, -32.0)
             ts(r("nv", 0, 128), ind(Vw, r("u", a, a + 8)), 32.0, 255.0, ALU.add, ALU.min)
-        for w in range(2):
-            for yb in range(4):
-                mm(*[(r("pc", 32 * w + 8 * yb, 32 * w + 8 * yb + 8), R("In" + S, 16 - 16 * u, 144 - 16 * u),
-                      R("cinf", 64 * w + 4 * u + yb, 64 * w + 64, 8)) for u in range(2)])
-        tr(r("land", 40, 72), r("pc", 0, 32))
-        tr(r("land", 72, 104), r("pc", 32, 64))
+        mm((r("pc", 0, 128), R("In" + S), R("cinf", 0, 128)))
+        act(r("f", 128, 256), r("pc", 0, 128), AF.Identity)
+        copy(r("f", 256, 320), ind(r("f", 128, 256), R("su", 4, 8)))
+        tr(r("land", 40, 104), r("f", 256, 320))
+        fill(r("f", 464, 512, 40), 0)
         for b in range(2):
             mm((r("pb", 32, 36), R("J", 1 + 128 * s - b, 129 + 128 * s - b), R("cinf", 128 + b, 136, 2)), start=b == 0, stop=b == 1)
         if s:
@@ -351,7 +371,7 @@ def build(g, core, T, topo):
                     act(pu, tm, AF.Identity, -2.0 ** 25, 2.0)
             tt(r("P", 2 * a + 1, 2 * b, 2), pu, ev, ALU.subtract)
         thr = r("f", 416, 417)
-        mset(thr, float(((AT[0] - 1) * 32 + 16) * 4096))
+        fill(thr, (2 * AT[0] - 17) * 2 ** 16)
 
         for t in range(RO):
             par = t % 2
@@ -360,58 +380,73 @@ def build(g, core, T, topo):
             swap(("pb" + S, 0 if t else 32, 40), (L0 if t else 32, L0 + 40), "land" + S)
             ts(r("u", 0, 8), r("pb", 32, 40), 0.5, None, ALU.add)
             if t:
-                act(r("land", L0 + 72, L0 + 104), r("pb", 0, 32), AF.Identity)
-                act(r("f", 96, 128), r("land", L0, L0 + 32), AF.Identity, thr)
+                if "d" in PAR["vec"]:
+                    copy(r("land", L0 + 72, L0 + 104), r("pb", 0, 32))
+                else:
+                    act(r("land", L0 + 72, L0 + 104), r("pb", 0, 32), AF.Identity)
+                if "f96" in PAR["vec"]:
+                    ts(r("f", 96, 128), r("land", L0, L0 + 32), thr, None, ALU.add)
+                else:
+                    act(r("f", 96, 128), r("land", L0, L0 + 32), AF.Identity, thr)
             mm((r("pc", 0, 64), R("Ib"), R("YC")), stop=False)
             act(r("g1"), ind(Vw, r("u", 4, 8)), AF.Identity)
             tt(r("g2"), ind(Vw, r("u", 0, 4)), r("g1"), ALU.is_lt)
             mm(*[(r("pc", 32 * w, 32 * w + 32), R(("nVB", "VB")[w], 8 - 8 * b, 136 - 8 * b), r("g2", b, 64, 2)) for w in range(2) for b in range(2)], start=False)
             tt(r("f", 0, 64), r("land", L0 + 40, L0 + 104), r("pc", 0, 64), ALU.min)
             C = r("msg", M0, M0 + 32)
-            tt(C, r("f", 0, 32), r("f", 32, 64), ALU.max)
-            copy(r("u", 16, 48), C)
+            tt(r("u", 16, 48), r("f", 0, 32), r("f", 32, 64), ALU.max)
+            keep(C, r("u", 16, 48))
             cuts = PAR["turn"]
-            for a, b in (cuts[:2], (cuts[1], cuts[-1])):
-                act(r("img", a, b), ind(r("P"), r("u", 16 + a // 16, 16 + b // 16)), AF.Identity, 0.0 if s else 0.5)
-                tr(r("imT", a, b), r("img", a, b))
             for a, b in zip(cuts, cuts[1:]):
-                (keep if a else copy)(r("of", a, b), r("imT", a, b))
+                ts(r("img", a, b), ind(r("P"), r("u", 16 + a // 16, 16 + b // 16)), 0.0 if s else 0.5, None, ALU.add)
+                tr(r("of", a, b), r("img", a, b))
+            for a, b in zip(PAR["lits"], PAR["lits"][1:]):
+                keep(r("imT", a, b), r("of", a, b))
             if t == 0:
                 swap(("pd" + S, 32, 64), (72, 104), "land" + S)
                 act(r("f", 96, 128), r("pd", 32, 64), AF.Identity, thr)
             if t + 1 == RO:
                 swap(("pd" + S, 32, 64), (M0, M0 + 32), "msg" + S)
                 clauses(r("pd", 32, 64), "pd", 1, T.yd)
-            mm((r("pc", 64, 128), R("Ib"), R("TB")), stop=False)
-            for q, grp in enumerate(chunks):
-                u0, u1 = grp[0][1] // 8, (grp[-1][1] + grp[-1][2]) // 8
+            mm((r("pc", 64, 128), R("Ib"), R("TB")), (r("pc", 64, 128), R("WW", 0, 128), R("cb", 384, 448)), stop=False)
+            kind = "last" if (t, s) == (RO - 1, 1) else "all"
+            gs, qs, zs = [cut(x) for x in PAR["main"][kind]]
+            for q, (a0, aw, _) in enumerate(cut(PAR["subs"][kind])):
+                u0, u1 = a0 // 8, (a0 + aw) // 8
                 pa, kb = "pa%d" % (turn[0] % 2), ("pb", "pd")[q % 2]
                 turn[0] += 1
                 kv = r(kb, u0 // 2, u1 // 2)
                 for a in range(u0 // 2, u1 // 2, PAR["piece"]):
                     b = min(a + PAR["piece"], u1 // 2)
-                    mm((r(kb, a, b), R("o64"), R("CK", a, b)), (r(kb, a, b), R("If"), r("imT", a, b)), start=a == u0 // 2, stop=False)
+                    mm((r(kb, a, b), R("If"), r("imT", a, b)), start=a == u0 // 2, stop=False)
 
-                def second(c, a, cw):
-                    scan(R("z", a, a + cw), R("w", a, a + cw), R("Q", a + 15, a + 15 + cw), ALU.max, ALU.min)
-                    mm((R(pa, a // 8 - u0, (a + cw) // 8 - u0), R("nIb"), R("z", a + 7, a + cw, 8)), start=False, stop=c == grp[-1][0])
-                for q0, (c, a, cw) in enumerate(grp):
-                    wv = R("w", a, a + cw)
-                    src = ind(Vm, r("of", a // 16, (a + cw) // 16))
-                    if (t, s, c) in PAR["dveg"] or c in PAR["dve"]:
-                        copy(wv, src)
-                    else:
-                        act(wv, src, AF.Identity)
-                    scan(R("Q", a + 16, a + 16 + cw), R("m8", 0, cw), wv, ALU.mult, ALU.max)
+                low = [a0]
+
+                def seconds(upto):
+                    while zs and zs[0][0] + zs[0][1] <= upto:
+                        a, cw, _ = zs.pop(0)
+                        scan(R("z", a, a + cw), R("w", a, a + cw), R("Q", a + 15, a + 15 + cw), ALU.max, ALU.min)
+                        if a + cw - low[0] >= PAR["gaps"] or a + cw == a0 + aw or zs[0][0] + zs[0][1] == a0 + aw:
+                            mm((R(pa, low[0] // 8 - u0, (a + cw) // 8 - u0), R("nIb"), R("z", low[0] + 7, a + cw, 8)), start=False, stop=a + cw == a0 + aw)
+                            low[0] = a + cw
+                while qs and qs[0][0] < a0 + aw:
+                    a, cw, _ = qs.pop(0)
+                    while gs and gs[0][0] < a + cw:
+                        b, gw, vec = gs.pop(0)
+                        src = ind(Vm, r("of", b // 16, (b + gw) // 16))
+                        if vec:
+                            copy(R("w", b, b + gw), src)
+                        else:
+                            act(R("w", b, b + gw), src, AF.Identity)
+                    scan(R("Q", a + 16, a + 16 + cw), R("m8", 0, cw), R("w", a, a + cw), ALU.mult, ALU.max)
                     top = R("Q", a + 23, a + 16 + cw, 8)
-                    mm((R(pa, a // 8 - u0, (a + cw) // 8 - u0), R("Ib"), top), start=q0 == 0, stop=False)
+                    mm((R(pa, a // 8 - u0, (a + cw) // 8 - u0), R("Ib"), top), start=a == a0, stop=False)
                     fill(top, 0)
-                    if q0:
-                        second(*grp[q0 - 1])
-                second(*grp[-1])
+                    seconds(a)
+                seconds(a0 + aw)
                 act(r("usg", u0, u1), R(pa, 0, u1 - u0), AF.Sign, -MT[t] - 0.5)
                 mm(*[(kv, R("VB", 8 - 8 * b, 136 - 8 * b), r("usg", u0 + b, u1, 2)) for b in range(2)], start=False)
-                scan(r("ks", u0 // 2, u1 // 2), R("m16", u0 // 2, u1 // 2), kv, ALU.mult, ALU.max)
+                scan(r("ks", u0 // 2, u1 // 2), R("CK", u0 // 2, u1 // 2), kv, ALU.add, ALU.max)
             for v in range(2):
                 for u in range(2):
                     mm((r("pd", v, 8, 2), R("Z%d" % v, 2 - 2 * (u - v), 130 - 2 * (u - v)), r("land", L0 + 32 + u, L0 + 40, 2)), start=u + v == 0, stop=False)
@@ -420,35 +455,38 @@ def build(g, core, T, topo):
             tt(km, best, r("f", 96, 128), ALU.max)
             ts(r("n", 96, 128), km, 11, 30, ALU.logical_shift_right, ALU.bitwise_and)
             ts(nC, km, 4095, None, ALU.bitwise_and)
-            tt(r("n", 64, 96), ubase, r("n", 96, 128), ALU.subtract)
-            copy(r("u", 48, 112), r("n", 32, 96))
+            tt(r("u", 80, 112), ubase, r("n", 96, 128), ALU.subtract)
+            keep(r("u", 48, 80), nC)
             stay, cnt = r("sg", 0, 32), r("f", 424, 425)
             act(stay, best, AF.Sign, thr, -1.0, acc=cnt)
-            act(r("um"), ind(r("usg"), r("u", 80, 112)), AF.Relu)
-            tt(r("pr"), ind(Vm, r("u", 48, 80)), r("um"), ALU.mult)
+            for a, b, _ in cut(PAR["sums"][kind]):
+                act(r("um", a, a + b), ind(r("usg"), r("u", 80 + a // 16, 80 + (a + b) // 16)), AF.Relu)
+                tt(r("pr", a, a + b), ind(Vm, r("u", 48 + a // 16, 48 + (a + b) // 16)), r("um", a, a + b), ALU.mult)
             new = r("msg", M0 + 40, M0 + 72)
             keep(new, nC)
             if t + 1 == RO:
                 clauses(new, ("pb", "pa")[s], 0, T.yc)
             else:
                 mm((r("pb", 40, 41), R("Bn"), cnt))
-                act(r("sg", 32, 33), r("pb", 40, 41), AF.Identity, -319.75 * 2 ** 17, -1.0)
-                ts(thr, r("sg", 32, 33), 320.0 * 2 ** 17 + ((AT[t + 1] - 1) * 32 + 16) * 4096, r("pb", 40, 41), ALU.add, ALU.add)
+                if "sg" in PAR["vec"]:
+                    ts(r("sg", 32, 33), r("pb", 40, 41), -1.0, -319.75 * 2 ** 17, ALU.mult, ALU.add)
+                else:
+                    act(r("sg", 32, 33), r("pb", 40, 41), AF.Identity, -319.75 * 2 ** 17, -1.0)
+                ts(thr, r("sg", 32, 33), 320.0 * 2 ** 17 + (2 * AT[t + 1] - 17) * 2 ** 16, r("pb", 40, 41), ALU.add, ALU.add)
             mm(*[(r("pc", 64 + b, 128, 2), R("Nb", 128 * b, 128 * b + 128), stay) for b in range(2)], start=False, stop=False)
             for b in range(2):
                 mm((r("pc", 64 + b, 128, 2), R("Md", 128 * b, 128 * b + 128), new), start=False, stop=False)
             mm(*[(r("pc", 64, 128), R("WW", 15 - k, 143 - k), r("pr", k, 512, 8)) for k in range(8)], start=False)
             tr(r("f", 256, 320), r("pc", 64, 128))
-            for o in (r("Rm", 0, 64), r("f", 192, 256)):
-                scan(o, R("m16", 0, 64), r("f", 256, 320), ALU.mult, ALU.max)
-            tt(r("f", 320, 384), ind(r("Rm"), R("su", 0, 4)), r("f", 192, 256), ALU.is_equal)
-            scan(r("O", 0, 56), r("f", 264, 320), r("f", 320, 376), ALU.add, ALU.mult)
+            scan(r("Rm", 0, 64), R("m16", 0, 64), r("f", 256, 320), ALU.mult, ALU.max)
+            tt(r("f", 320, 384), ind(r("Rm"), R("su", 0, 4)), r("f", 256, 320), ALU.not_equal)
+            scan(r("O", 0, 56), r("f", 320, 376), r("f", 264, 320), ALU.mult, ALU.add)
             ts(r("O", 6, 56, 16), r("O", 7, 56, 16), 2.0 ** 24, -2.0 ** 24, ALU.add, ALU.add)
             tr(r("X"), r("O", 0, 64))
             scan(r("O", 70, 120), R("m2", 6, 56), r("O", 6, 56), ALU.mult, ALU.subtract)
             ll = r("O", 7, 120, 16)
-            mm(*[(r("pd", 4 * w, 4 * w + 4), R("nIf"), r("Rm", 7, 64, 16)) for w in range(2)], start=False)
-            tt(r("msg", M0 + 32, M0 + 40), ll, r("pd", 0, 8), ALU.max)
+            mm(*[(r("pd", 4 * w, 4 * w + 4), R("If"), r("Rm", 7, 64, 16)) for w in range(2)], start=False)
+            tt(r("msg", M0 + 32, M0 + 40), ll, r("pd", 0, 8), ALU.min)
             if t + 1 < RO:
                 src, la = r("msg", M0, M0 + MW), r("land", L0 + LW, L0 + LW + MW)
                 rid, pid, _ = topo.addr(dst)
@@ -469,21 +507,20 @@ def build(g, core, T, topo):
             if end:
                 for ht in range(2):
                     mm((r("pb", 48 + ht, 64, 2), R("Hs", 128 * ht, 128 * ht + 128), ll))
-                ts(r("u", 112, 128), r("pb", 48, 64), 0.5, None, ALU.add)
+                ts(r("u", 112, 128), r("pb", 48, 64), 0.5, float(VW - 1), ALU.add, ALU.min)
                 edits(112)
             if t + 1 == RO:
                 for b in range(2):
                     mm((r("pb", 192 + b, 200, 2, 0, 64), R("Out", 128 + 64 * b, 192 + 64 * b), r("msg", M0 + 32, M0 + 36)))
                 act(r("tmp", 128, 136, 1, 0, 64), r("pb", 192, 200, 1, 0, 64), AF.Identity, -OFF)
                 dmas("sp", [(T.yl[64 * s:64 * s + 64, :], T["tmp" + S][0:64, 128:136])], [r("tmp", 128, 136)], [], "fin", 2e3)
-            mm((r("pd", 16, 32), R("Ib"), R("LK", 16 * par, 16 * par + 16)), stop=False)
+            mm((r("pd", 16, 32), R("Ib"), R("LK", 16 * par, 16 * par + 16)), (r("pd", 16, 32), R("o64", p1=32), R("cb", 256, 272, p1=32)), stop=False)
             for ht in range(2):
                 mm((r("pd", 16 + ht, 32, 2), R("Hs", 128 * ht, 128 * ht + 128), ll), start=False, stop=False)
             scan(r("mn"), R("mseg"), r("ab"), ALU.add, ALU.min)
             mm(*[(r("pd", 16 + 8 * w + ht, 24 + 8 * w, 2), R("Hb", 128 * ht, 128 * ht + 128), r("mn", SEG - 1, 4 * SEG, SEG))
                  for w in range(2) for ht in range(2)], start=False)
-            tt(r("f", 456, 472), r("pd", 16, 32), dum, ALU.min)
-            ts(r("u", 128, 144), r("f", 456, 472), 0.5, None, ALU.add)
+            tt(r("u", 128, 144), r("pd", 16, 32), dum, ALU.min)
             if not end:
                 edits(128)
             copy(ind(Vw, r("u", 128, 144)), r("nv"))
@@ -536,11 +573,12 @@ def table(ops, c):
         if k == "dma":
             out.append((o["e"], 0.06 * a[0], c["dma"], a[1] / c["bw"], dep))
         elif k == "rem":
-            out.append((o["e"], 0.5, c["rem"], 0.0, dep))
+            out.append((o["e"], c["hold"], c["rem"], 0.0, dep))
         elif k == "pe":
-            out.append((o["e"], a * c["cyc"], a * c["cyc"] + c["fix"], 0.0, dep))
+            d = a[0] * c["cyc"] + a[1] * c["mm"]
+            out.append((o["e"], d, d + c["fix"], 0.0, dep))
         else:
-            d = c["fix"] + a * c["cyc"] * (c[k] if k != "cyc" else 1)
+            d = c["fix"] + c["act"] * (o["e"] == "act") + a * c["cyc"] * (c[k] if k != "cyc" else 1)
             out.append((o["e"], d, d, 0.0, dep))
     return out
 
@@ -599,14 +637,10 @@ def in_order(order, pre):
     return out
 
 
-def walk(tab, order, at=0, old=None, prev=None, pos=None):
+def walk(tab, order):
     n = len(tab)
-    if old:
-        done, why, free, prev = list(old[1]), list(old[2]), list(old[3]), dict(prev)
-        dma = max([0.0] + [done[i] for i in old[4] if pos[i] < at])
-    else:
-        done, why, free, prev, dma = [0.0] * n, [0] * n, [0.0] * (n + 1), dict.fromkeys(QUEUES, n), 0.0
-    for i in order[at:]:
+    done, why, free, prev, dma = [0.0] * n, [0] * n, [0.0] * (n + 1), dict.fromkeys(QUEUES, n), 0.0
+    for i in order:
         e, hold, rdy, wire, dep = tab[i]
         w = prev[e]
         t, w = free[w], -1 - w
@@ -618,31 +652,7 @@ def walk(tab, order, at=0, old=None, prev=None, pos=None):
             dma = done[i] = max(dma, t + rdy) + wire
         else:
             done[i] = t + rdy
-    return max(done), done, why, free, old[4] if old else [i for i in range(n) if tab[i][3]]
-
-
-def probe(tab, order, at, old, prev, pos):
-    was, done, free, prev = old[1], list(old[1]), list(old[3]), dict(prev)
-    shift, run, dma = 1e9, 0, max([0.0] + [was[i] for i in old[4] if pos[i] < at])
-    for i in order[at:]:
-        e, hold, rdy, wire, dep = tab[i]
-        t = free[prev[e]]
-        for j, l in dep:
-            if done[j] + l > t:
-                t = done[j] + l
-        free[i], prev[e] = t + hold, i
-        if wire:
-            dma = done[i] = max(dma, t + rdy) + wire
-            continue
-        done[i] = t = t + rdy
-        t -= was[i]
-        if -1e-9 < t - shift < 1e-9:
-            run += 1
-            if run == 60:
-                return old[0] + shift
-        else:
-            shift, run = t, 0
-    return max(done)
+    return max(done), done, why
 
 
 def place(line, t, h):
@@ -685,7 +695,7 @@ def tighten(ops, tabs, tab, look, seed):
         return seed[0] / 2147483648.0
     norm = [walk(x, order)[0] * len(tabs) for x in tabs]
     best, span = 1.0, max(start)
-    for step in range(PAR["steps"][0]):
+    for step in range(PAR["shakes"]):
         a, w, j = draw() * (span + 10) - 10, (3, 8, 20)[int(draw() * 3)], (0.2, 0.6, 1.6)[int(draw() * 3)]
         st = [x + j * (draw() + draw() + draw() - 1.5) if a < x < a + w else x for x in start]
         back, lines = [0.0] * n, {}
@@ -702,85 +712,228 @@ def tighten(ops, tabs, tab, look, seed):
     return order
 
 
-def chain(res):
-    end, done, why = res[:3]
-    i, pairs = done.index(end), []
-    while why[i] != -1 - len(done):
-        if why[i] < 0:
-            pairs.append((-1 - why[i], i))
-        i = why[i] if why[i] >= 0 else -1 - why[i]
+def part(tabs, ids):
+    new = {i: q for q, i in enumerate(ids)}
+    above, direct = [0] * len(ids), [None] * len(ids)
+    for q in sorted(range(len(ids)), key=lambda q: ids[q]):
+        dep = [new[j] for j, l in tabs[0][ids[q]][4] if j in new]
+        far = 0
+        for j in dep:
+            far |= above[j]
+        direct[q] = set(j for j in dep if not far >> j & 1)
+        for j in dep:
+            far |= 1 << j
+        above[q] = far
+    out = []
+    for tab in tabs:
+        rows = []
+        for q, i in enumerate(ids):
+            e, hold, rdy, wire, dep = tab[i]
+            lat = {}
+            for j, l in dep:
+                if j in new and new[j] in direct[q]:
+                    lat[new[j]] = max(l, lat.get(new[j], -1.0))
+            rows.append((QUEUES.index(e), hold, rdy, wire, tuple(lat.items())))
+        out.append(rows)
+    return out
+
+
+def run(tab, order, at, old, goal):
+    done, begin, free = old[1][:], old[2][:], [-1.0] * 5
+    q, left, dma = at, 4, max([0.0] + [done[i] for i in old[3] if old[4][i] < at])
+    while q and left:
+        q -= 1
+        i = order[q]
+        e = tab[i][0]
+        if free[e] < 0:
+            free[e] = begin[i] + tab[i][1]
+            left -= e < 4
+    free = [max(x, 0.0) for x in free]
+    for i in order[at:]:
+        e, hold, rdy, wire, dep = tab[i]
+        t = free[e]
+        for j, l in dep:
+            j = done[j] + l
+            if j > t:
+                t = j
+        begin[i] = t
+        free[e] = t + hold
+        if wire:
+            dma = done[i] = max(dma, t + rdy) + wire
+        else:
+            done[i] = t + rdy
+        if i == goal:
+            return t + rdy, done, begin, old[3], old[4]
+    return max(done), done, begin, old[3], old[4]
+
+
+def chain(tab, order, res, goal, lo, hi):
+    end, done, begin, wires, spot = res
+    i, pairs = goal if goal is not None else done.index(end), []
+    while spot[i] > lo:
+        t = begin[i] - 1e-9
+        for j, l in tab[i][4]:
+            if done[j] + l >= t:
+                break
+        else:
+            q, e = spot[i] - 1, tab[i][0]
+            while q >= 0 and tab[order[q]][0] != e:
+                q -= 1
+            if q < lo:
+                break
+            j = order[q]
+            if q < hi:
+                pairs.append((j, i))
+        i = j
     return pairs
 
 
-def move(order, pos, pre, a, b, ahead):
-    ia, ib = pos[a], pos[b]
-    if ia > ib or ib - ia > 150:
-        return False
-    seg = order[ia:ib + 1]
-    if ahead:
-        grp, need = {b}, set(pre[b])
-        for x in reversed(seg[:-1]):
-            if x in need:
-                grp.add(x)
-                need |= pre[x]
-        new = [x for x in seg if x in grp] + [x for x in seg if x not in grp]
-    else:
-        grp = {a}
-        for x in seg[1:]:
-            if pre[x] & grp:
-                grp.add(x)
-        new = [x for x in seg if x not in grp] + [x for x in seg if x in grp]
-    if a in grp and b in grp:
-        return False
-    order[ia:ib + 1] = new
-    for q, x in enumerate(new):
-        pos[x] = ia + q
-    return True
-
-
-def anneal(tabs, order, fixed, steps, heat, seed):
-    n = len(order)
+def settle(tabs, order, goal, steps, heat, seed, lo=0, hi=1 << 30, key=None):
+    n, m = len(order), len(tabs)
     pre = [set(j for j, l in x[4]) for x in tabs[0]]
-    res = [walk(x, order) for x in tabs]
-    norm = [x[0] * len(tabs) for x in res]
-    now, low, best = 1.0, 1.0, order
-    spot, links = [0] * n, [chain(x) for x in res]
+    spot = [0] * n
     for q, x in enumerate(order):
         spot[x] = q
+    zero = (0.0, [0.0] * n, [0.0] * n, [i for i in range(n) if tabs[0][i][3]], spot)
+    res = [run(x, order, 0, zero, goal) for x in tabs]
+    norm = [x[0] * m for x in res]
+    now, low, best, ends = 1.0, 1.0, key or order, [x[0] for x in res]
+    per = len(key) if key else 0
+    if per:
+        lo = sum(key[q % per] + q - q % per < max(key) - per + 30 for q in range(n))
+    links = [None] * m
     for step in range(steps):
         seed = (seed * 1103515245 + 12345) % 2147483648
-        pairs = links[(seed >> 8) % len(tabs)]
-        seed = (seed * 1103515245 + 12345) % 2147483648
-        a, b = pairs[(seed >> 8) % len(pairs)]
-        if a in pre[b] or a < fixed:
-            continue
-        new, pos, first = list(order), list(spot), spot[a]
-        if not move(new, pos, pre, a, b, seed >> 29 & 1):
+        q = (seed >> 8) % m
+        if links[q] is None:
+            links[q] = chain(tabs[q], order, res[q], goal, lo, hi)
+        if not links[q]:
             continue
         seed = (seed * 1103515245 + 12345) % 2147483648
-        bound = now - heat * (1 - step / steps) * math.log((seed + 1) / 2147483648.0)
-        prev = dict.fromkeys(QUEUES, n)
-        for i in new[:first]:
-            prev[tabs[0][i][0]] = i
-        if sum(probe(x, new, first, y, prev, pos) / m for x, y, m in zip(tabs, res, norm)) > bound:
+        a, b = links[q][(seed >> 8) % len(links[q])]
+        ia, ib, how = spot[a], spot[b], seed >> 28
+        if how < 2 and not per:
+            b, ib, ia = a, ia, max([lo] + [spot[j] + 1 for j in pre[a]])
+            a = order[ia]
+        elif a in pre[b] or ib - ia > 150:
             continue
-        r = [walk(x, new, first, y, prev, pos) for x, y in zip(tabs, res)]
-        v = sum(x[0] / m for x, m in zip(r, norm))
-        if v <= bound:
-            now, order, res, spot, links = v, new, r, pos, [chain(x) for x in r]
-            if v < low:
-                low, best = v, new
-    return best
+        seg = order[ia:ib + 1]
+        if how < 5 - (per > 0):
+            grp, need = {b}, set(pre[b])
+            for x in reversed(seg[:-1]):
+                if x in need:
+                    grp.add(x)
+                    need |= pre[x]
+            turned = [x for x in seg if x in grp] + [x for x in seg if x not in grp]
+        else:
+            grp = {a}
+            for x in seg[1:]:
+                if pre[x] & grp:
+                    grp.add(x)
+            turned = [x for x in seg if x not in grp] + [x for x in seg if x in grp]
+        if a in grp and b in grp:
+            continue
+        new, changed = order[:], []
+        for d in range(-n + per, n, per) if per else (0,):
+            here = [spot[x + d] for x in seg if 0 <= x + d < n]
+            changed += here
+            for q, y in zip(here, [y + d for y in turned if 0 <= y + d < n]):
+                new[q] = y
+        seed = (seed * 1103515245 + 12345) % 2147483648
+        room = -heat * (1 - step / steps) * math.log((seed + 1) / 2147483648.0)
+        v, got, ia = 0.0, [], min(changed)
+        for q in range(m):
+            got.append(run(tabs[q], new, ia, res[q], goal))
+            v += (got[q][0] - res[q][0]) / norm[q]
+            if v > room + 0.002 * (m - 1 - q) / m:
+                break
+        else:
+            now, order, res, links = now + v, new, got, [None] * m
+            if per:
+                old, key = key, key[:]
+                for x, y in zip(seg, turned):
+                    key[y % per] = old[x % per] + x - x % per - y + y % per
+            for q in changed:
+                spot[order[q]] = q
+            if now < low:
+                low, best, ends = now, key if per else new, [x[0] for x in res]
+    return best, ends
+
+
+def fittest(tries, stages, step):
+    for keepers, steps, heat in stages:
+        got = [step(x, steps, heat, PAR["seed"] + q) for q, x in enumerate(tries)]
+        tries = [x[0] for x in sorted(got, key=lambda x: sum(a / b for a, b in zip(x[1], got[0][1])))[:keepers]]
+    return tries[0]
+
+
+def middle(ops, tabs, start, first):
+    ids = [o["i"] for o in ops if o["ts"] and 1 <= o["ts"][0] <= 3]
+    per = len(ids) // 3
+    sub = part(tabs, ids)
+    tries = []
+    for t in range(1, RO - 1):
+        span = start[first[t + 1, 0]] - start[first[t, 0]]
+        at = [(start[ids[k] + (t - 1) * per] - start[first[t, 0]]) / span for k in range(per)]
+        again = True
+        while again:
+            again = False
+            for q in range(per, 2 * per):
+                for j, l in sub[0][q][4]:
+                    if j // per + at[j % per] >= 1 + at[q % per]:
+                        at[q % per], again = j // per + at[j % per] - 1 + 1e-7, True
+        key = [0] * per
+        for q, k in enumerate(sorted(range(per), key=lambda k: (at[k] % 1, k))):
+            key[k] = q + per * math.floor(at[k])
+        tries.append(key)
+
+    def step(key, steps, heat, seed):
+        return settle(sub, sorted(range(3 * per), key=lambda q: key[q % per] + q - q % per), ids.index(first[3, 0]), steps, heat, seed, key=key)
+    return ids, fittest(tries, PAR["middle"], step)
 
 
 def arrange(ops):
     tabs = [table(ops, cost(m)) for m in SPREAD]
     tab = tabs.pop()
+    n = len(ops)
+    order = tighten(ops, tabs, tab, PAR["look"], PAR["seed"])
+    done = walk(tab, order)[1]
+    start = [done[i] - tab[i][2] - tab[i][3] for i in range(n)]
+    first, seen, like = {}, {}, {}
+    for o in ops:
+        if o["ts"]:
+            v = (o["ts"][1], o["e"], o["k"], o["n"]) + tuple((x[0], x[1] % {"land": LW, "msg": MW}.get(x[0][:-1], 1 << 20)) for x in o["wr"])
+            seen[o["ts"], v] = seen.get((o["ts"], v), 0) + 1
+            like[o["i"]] = v + (seen[o["ts"], v],)
+            if o["wr"] and o["wr"][0][0] == "w":
+                first.setdefault(o["ts"], o["i"])
+    ids, key = middle(ops, tabs, start, first)
+    per = len(key)
+    spot = {like[ids[k]]: key[k] for k in range(per)}
+    zero, span = spot[like[first[1, 0]]], start[first[3, 0]] - start[first[2, 0]]
     loads = sum(o["k"] == "dma" and not o["dep"] for o in ops)
-    starts = [anneal(tabs, tighten(ops, tabs, tab, look, seed), loads, PAR["steps"][1], PAR["heat"], seed) for look, seed in PAR["starts"]]
-    norm = [walk(x, starts[0])[0] for x in tabs]
-    order = min(starts, key=lambda o: sum(walk(x, o)[0] / m for x, m in zip(tabs, norm)))
-    return anneal(tabs, order, loads, PAR["steps"][2], PAR["heat"], 1)
+    at, last, soon = [0.0] * n, {}, plan(ops, tab, PAR["look"])[1]
+    for o in ops:
+        i = o["i"]
+        if i < loads:
+            at[i] = i - 1e9
+        elif i < first[0, 0] or not o["ts"]:
+            at[i] = zero + (soon[i] - soon[first[0, 0]]) / span * per if soon[i] < soon[first[2, 0]] else 1e9
+        elif like[i] in spot:
+            last[o["ts"]] = at[i] = spot[like[i]] + per * o["ts"][0]
+        else:
+            at[i] = last.get(o["ts"], min(key) + per * o["ts"][0]) + 0.5
+    full = in_order(sorted(range(n), key=lambda i: (at[i], i)), [[j for j, l in x[4]] for x in tab])
+    was = {i: q for q, i in enumerate(order)}
+    b, c, hi = full.index(first[2, 1]) + 1, full.index(first[1, 0]), full.index(first[1, 1])
+    sub = part(tabs, full[:b])
+    tries = [list(range(b)), sorted(range(c), key=lambda q: was[full[q]]) + list(range(c, b))]
+    full[:b] = [full[q] for q in fittest(tries, PAR["start"], lambda x, steps, heat, seed: settle(sub, x, b - 1, steps, heat, seed, loads, hi))]
+    a, c, lo = full.index(first[RO - 3, 1]), full.index(first[RO - 1, 0]), full.index(first[RO - 2, 1])
+    sub = part(tabs, full[a:])
+    tries = [list(range(n - a)), list(range(c - a)) + sorted(range(c - a, n - a), key=lambda q: was[full[a + q]])]
+    full[a:] = [full[a + q] for q in fittest(tries, PAR["end"], lambda x, steps, heat, seed: settle(sub, x, None, steps, heat, seed, lo - a))]
+    return full
 
 
 ORDER = []

import math
from concourse.mybir import AluOpType as ALU, ActivationFunctionType as AF

RO, STEP = 6, 2
MT = [32, 24, 40, 28, 48, 20]
AT = [8, 10, 7, 9, 6, 11]
PAR = {
    "subs": {"all": [3584, 3584, 1024], "last": [3584, 3584, 1024]},
    "sums": {"all": [512], "last": [256, 256]},
    "main": {"all": ([1024, -512, 1024, 1024, 1024, 1024, 1024, 512, 512, 512], [1024, 512, 1024, 1024, 1024, 1024, 1024, 512, 512, 512],
                     [1024, 512, 1024, 1024, 1024, 1024, 1024, 512, 512, 512]),
             "last": ([1024, -512, 1024, 1024, -512, 512, 1024, 1024, 512, 512, 512], [1024, 512, 1024, 1024, 1024, 1024, 1024, 512, 512, 512],
                      [1024, 512, 1024, 1024, 1024, 1024, 1024, 512, 512, 512])},
    "turn": (0, 128, 512),
    "lits": (0, 128, 256, 384, 512),
    "vec": ("sg", "d", "f96"),
    "gaps": 4096,
    "piece": 112,
    "gcut": [[(0, 512), (512, 1024), (1024, 1536), (1536, 2048)], [(0, 1024), (1024, 2048)]],
    "pcut": [[(0, 512), (512, 1024), (1024, 1536), (1536, 1792), (1792, 2048)], [(0, 512), (512, 1024), (1024, 1536), (1536, 2048)]],
    "look": 0.22,
    "seed": 4,
    "shakes": 50,
    "middle": ((2, 6000, 0.004), (1, 10000, 0.002), (1, 14000, 0.001)),
    "start": ((1, 8000, 0.001), (1, 12000, 0.0005)),
    "end": ((1, 6000, 0.0015), (1, 12000, 0.0007)),
}
CW = 1024
ENG = 16
BIG = 100
F, B, I, U = "float32", "bfloat16", "int32", "uint16"
MW, LW = 72, 104
V0, VW = 16, 4368
SEG = 130
OFF = V0 - 0.5

SCRATCH = {
    "cin": ("sbuf", [128, 136], I), "cinf": ("sbuf", [128, 136], F),
    "pidx": ("sbuf", [128, 16], I), "pf": ("sbuf", [128, 32], F),
    "ones": ("sbuf", [128, 264], F), "If": ("sbuf", [128, 128], F),
    "Ib": ("sbuf", [128, 128], B), "nIb": ("sbuf", [128, 128], B),
    "SW0": ("sbuf", [128, 160], F), "SW1": ("sbuf", [128, 160], F), "Z0": ("sbuf", [128, 132], F), "Z1": ("sbuf", [128, 132], F),
    "In0": ("sbuf", [128, 128], F), "In1": ("sbuf", [128, 128], F), "Out": ("sbuf", [128, 256], F), "Hs": ("sbuf", [128, 256], F),
    "J": ("sbuf", [128, 258], F), "Mp": ("sbuf", [128, 288], F), "Md": ("sbuf", [128, 256], F), "Nb": ("sbuf", [128, 256], B),
    "rows": ("sbuf", [128, 800], F), "WW": ("sbuf", [128, 144], B), "VB": ("sbuf", [128, 144], B), "nVB": ("sbuf", [128, 144], B),
    "Bn": ("sbuf", [128, 128], F), "Row": ("sbuf", [128, 256], F), "cb": ("sbuf", [128, 458], B), "Dup": ("sbuf", [128, 128], B),
    "o64": ("sbuf", [128, 128], B), "CK": ("sbuf", [128, 512], B), "TB": ("sbuf", [128, 64], B), "YC": ("sbuf", [128, 64], B),
    "m8": ("sbuf", [128, CW], B), "m2": ("sbuf", [128, 64], B),
    "m16": ("sbuf", [128, 64], B), "mseg": ("sbuf", [128, 4 * SEG], B), "LR": ("sbuf", [128, 2 * SEG + 12], B), "LK": ("sbuf", [128, 32], B),
    "sm": ("sbuf", [128, 64], F), "su": ("sbuf", [128, 16], U), "Hb": ("sbuf", [128, 256], B),
    "w": ("sbuf", [128, 8192], B), "Q": ("sbuf", [128, 8192 + 16], B), "z": ("sbuf", [128, 8192], B),
}
for _s in "01":
    SCRATCH.update({
        "V" + _s: ("sbuf", [128, VW], B), "G" + _s: ("sbuf", [128, 2048], I), "P" + _s: ("sbuf", [128, 4096], F),
        "tmp" + _s: ("sbuf", [128, 1024], F), "g2" + _s: ("sbuf", [128, 64], B), "sg" + _s: ("sbuf", [128, 48], B),
        "usg" + _s: ("sbuf", [128, 1024], B), "img" + _s: ("sbuf", [128, 512], U), "imT" + _s: ("sbuf", [128, 512], F),
        "of" + _s: ("sbuf", [128, 512], U), "ks" + _s: ("sbuf", [128, 512], F),
        "um" + _s: ("sbuf", [128, 512], B), "pr" + _s: ("sbuf", [128, 512], B),
        "ab" + _s: ("sbuf", [128, 4 * SEG], B), "mn" + _s: ("sbuf", [128, 4 * SEG], B),
        "X" + _s: ("sbuf", [128, 64], F), "nv" + _s: ("sbuf", [128, 256], B), "g1" + _s: ("sbuf", [128, 64], B),
        "Rm" + _s: ("sbuf", [128, 72], F), "O" + _s: ("sbuf", [128, 128], F),
        "f" + _s: ("sbuf", [128, 512], F), "n" + _s: ("sbuf", [128, 128], I), "u" + _s: ("sbuf", [128, 160], U),
        "land" + _s: ("sbuf", [128, RO * LW], F), "msg" + _s: ("sbuf", [128, RO * MW], F),
        "pa" + _s: ("psum", [128, 512], F), "pb" + _s: ("psum", [128, 512], F),
        "pc" + _s: ("psum", [128, 512], F), "pd" + _s: ("psum", [128, 512], F),
    })
SEMAPHORES = (["act", "dve", "pe", "pool", "sent", "ldc", "fin", "ldv", "ldz0", "ldz1"] + ["ldg%d_%d" % (s, q) for s in range(2) for q in range(4)]
              + ["arr%d_%d" % (t, s) for t in range(1, RO) for s in range(2)])
QUEUES = ("act", "dve", "pe", "pool", "sp")

SPREAD = [(1.0, 1.56, 3.8, .05, .1, 3.0, 1.0, 1.5, .05, .02), (1.15, 1.25, 5, .03, .18, 3.5, 2.0, 2.0, .12, .04),
          (1.4, 1.85, 2.5, .05, .08, 3.5, 1.5, 1.2, .03, .05), (1.15, 1.56, 3.8, .05, .12, 3.3, 1.2, 1.6, .05, .03)]


def cost(m):
    return {"cyc": 0.00083 * m[0], "gat": m[1], "sca": m[2], "fix": m[3], "lat": m[4], "rem": m[5], "hold": m[6], "dma": m[7], "bw": 200e3,
            "act": m[8], "mm": m[9]}


def build(g, core, T, topo):
    rank = T.rank_of(core)
    n = len(T.cores)
    dst = T.cores[(rank + STEP) % n]
    ops = []
    ctx = {"ts": None}

    def R(name, a=None, b=None, st=1, p0=0, p1=128):
        shp = SCRATCH[name][1]
        if a is None:
            a, b = 0, shp[1]
        return (T[name][p0:p1, a:b:st] if st != 1 else T[name][p0:p1, a:b], name, a, b, (b - a + st - 1) // st)

    def two(*v):
        return all(SCRATCH[x[1]][2] in (B, U) for x in v)

    def ps(v):
        return SCRATCH[v[1]][0] == "psum"

    def op(eng, fn, rd, wr, kind, amt, sem=None, cnt=0):
        ops.append({"e": eng, "fn": fn, "rd": [x[1:4] for x in rd], "wr": [x[1:4] for x in wr], "k": kind, "n": amt,
                    "sem": sem, "cnt": cnt, "ts": ctx["ts"], "i": len(ops)})

    def ind(win, off):
        return (win[0].indirect(off[0]), win[1], win[2], win[3], off[4] * 16, off)

    def rds(*v):
        out = []
        for x in v:
            if isinstance(x, tuple):
                out.append(x)
                if len(x) > 5:
                    out.append(x[5])
        return out

    def ap(x):
        return x[0] if isinstance(x, tuple) else x

    def vcost(o, i, rate):
        if len(i) > 5:
            return "gat", i[4]
        if len(o) > 5:
            return "sca", o[4]
        return "cyc", max(64, rate * i[4])

    def copy(o, i):
        k, a = vcost(o, i, 0.5 if two(o, i) else 1)
        op("dve", lambda: g.vector.tensor_copy(o[0], i[0]), rds(i) + rds(o)[1:], [o], k, a)

    def tt(o, a, b, alu):
        k, c = vcost(o, a, 1 if ps(a) or ps(b) else 2)
        op("dve", lambda: g.vector.tensor_tensor(o[0], a[0], b[0], alu), rds(a, b), [o], k, c)

    def ts(o, a, s1, s2, o0, o1=None):
        k, c = vcost(o, a, 0.5 if two(o, a) else 1)
        if o1 is None:
            op("dve", lambda: g.vector.tensor_scalar(o[0], a[0], ap(s1), None, o0), rds(a, s1), [o], k, c)
        else:
            op("dve", lambda: g.vector.tensor_scalar(o[0], a[0], ap(s1), ap(s2), o0, o1), rds(a, s1, s2), [o], k, c)

    def scan(o, d0, d1, o0, o1):
        op("dve", lambda: g.vector.tensor_tensor_scan(o[0], d0[0], d1[0], 0.0, o0, o1), rds(d0, d1), [o], "cyc",
           max(64, (0.5 if two(o, d0, d1) else 1) * o[4]))

    def tr(o, i):
        op("dve", lambda: g.vector.transpose(o[0], i[0]), [i], [o], "cyc", max(64, (0.5 if two(o, i) else 1) * i[4]))

    def mset(o, v):
        op("dve", lambda: g.vector.memset(o[0], v), [], [o], "cyc", max(64, (0.5 if two(o) else 1) * o[4]))

    def act(o, i, fn, bias=0.0, scale=1.0, acc=None):
        k, c = vcost(o, i, 1)
        if acc is None:
            op("act", lambda: g.scalar.activation(o[0], i[0], fn, bias=ap(bias), scale=scale), rds(i, bias), [o], k, c)
        else:
            op("act", lambda: g.scalar.activation(o[0], i[0], fn, bias=ap(bias), scale=scale, accum_out=acc[0]), rds(i, bias), [o, acc], k, c + 24)

    def mm(*terms, start=True, stop=True):
        def fn():
            last = None
            for q, (o, l, r) in enumerate(terms):
                last = g.tensor.matmul(o[0], l[0], r[0], start and q == 0, stop and q == len(terms) - 1)
            return last
        c = sum(max(64, r[4]) * (1 if two(l) else 4) for o, l, r in terms)
        op("pe", fn, [x for t in terms for x in t[1:]], [t[0] for t in terms], "pe", (c, len(terms)))

    def iota(o, pat, base, cm=0):
        if SCRATCH[o[1]][2] == I:
            op("pool", lambda: g.iota(o[0], pat, base, cm), [], [o], "cyc", 130 + 2 * o[4])
        else:
            op("pool", lambda: g.iota(o[0], pat, base, cm, allow_small_or_imprecise_dtypes=True), [], [o], "cyc", 130 + 2 * o[4])

    def fill(o, v):
        iota(o, [[0, o[4]]], v)

    def keep(o, i):
        op("pool", lambda: g.affine_select(o[0], i[0], [[0, o[4]]], ALU.is_ge, 0.0, 0, 0), [i], [o], "cyc", 170 + 2 * o[4])

    def perm(o, pat, base, i=None):
        i = i or R("ones", 0, o[4])
        op("pool", lambda: g.affine_select(o[0], i[0], [[-a, c] for a, c in pat], ALU.is_equal, 0.0, -base, 1), [i], [o], "cyc", 170 + 2 * o[4])

    def dmas(eng, pairs, rd, wr, sem, nbytes):
        q = {"sp": g.sync, "act": g.scalar}[eng]

        def fn():
            for o, i in pairs:
                q.dma_start(o, i).then_inc(T.sem[sem], 16)
        op(eng, fn, rd, wr, "dma", (len(pairs), nbytes), sem=sem, cnt=16 * len(pairs))

    def cut(sizes):
        out, at = [], 0
        for cw in sizes:
            out.append((at, abs(cw), cw < 0))
            at += abs(cw)
        return out

    dmas("sp", [(T.cin[:, 0:64], T.cla[:]), (T.cin[:, 64:128], T.par[:]), (T.cin[:, 128:136], T.lit[:])], [], [R("cin")], "ldc", 70e3)
    for q in range(2):
        dmas("act", [(T.z[0:64, 2048 * q:2048 * q + 2048], T.val[0:64, 2048 * q:2048 * q + 2048])], [], [R("z", 2048 * q, 2048 * q + 2048)], "ldz%d" % q, 1 << 18)
    for s in range(2):
        S = str(s)
        hv = [(32 * G + 16 * h, 64 * s + 16 * G) for G in range(4) for h in range(2)]
        for q, (c0, c1) in enumerate(PAR["gcut"][s]):
            dmas("sp", [(T["G" + S][a:a + 16, c0:c1], T.gen[b:b + 16, c0:c1]) for a, b in hv],
                 [], [R("G" + S, c0, c1)], "ldg%d_%d" % (s, q), 512 * (c1 - c0))
    dmas("sp", [(T.V1[a:a + 16, V0:V0 + 4096], T.val[b:b + 16, :]) for a, b in hv], [], [R("V1", V0, V0 + 4096)], "ldv", 1 << 20)

    mset(R("ones"), 1.0)
    iota(R("pidx", 0, 1), [[0, 1]], 0, 1)
    perm(R("J"), [[1, 129], [-1000, 2]], 1000)
    for s in range(2):
        perm(R("In%d" % s), [[16, 4], [0, 2], [1, 16]], 64 * s)
    perm(R("If"), [[1, 128]], 0)
    fld = {"blk": (4, 7), "G": (5, 3), "r15": (0, 15), "y": (1, 1), "b0": (0, 1), "b": (3, 1), "B10": (2, 3), "h": (4, 1), "r3": (0, 3), "b2": (2, 1)}
    col = {}
    for q, (nm, (sh, ms)) in enumerate(fld.items()):
        ts(R("pidx", q + 1, q + 2), R("pidx", 0, 1), sh, ms, ALU.logical_shift_right, ALU.bitwise_and)
        col[nm] = R("pf", q + 21, q + 22)
    copy(R("pf", 20, 31), R("pidx", 0, 11))
    copy(R("cinf"), R("cin"))
    ts(R("pf", 0, 1), col["b"], -63.0, None, ALU.mult)
    ts(R("pf", 1, 2), col["r15"], 8.0, R("pf", 0, 1), ALU.mult, ALU.add)
    ts(R("pf", 2, 3), col["h"], 4.0, R("pf", 1, 2), ALU.mult, ALU.add)
    iota(R("rows", 40, 44), [[64, 2], [2, 2]], 0)
    ts(R("su", 4, 8), R("rows", 40, 44), R("pf", 2, 3), None, ALU.add)
    ts(R("pf", 3, 4), col["b2"], col["h"], 100.0, ALU.not_equal, ALU.mult)
    ts(R("pf", 4, 5), col["r3"], 8.0, col["b"], ALU.mult, ALU.add)
    iota(R("rows", 44, 48), [[2, 4]], 0)
    ts(R("rows", 48, 52), R("rows", 44, 48), R("pf", 3, 4), R("pf", 4, 5), ALU.add, ALU.add)
    ts(R("su", 8, 12), R("rows", 48, 52), 32.0, None, ALU.min)
    mset(R("cb", 256, 384), 1.0)
    perm(R("Dup", p1=64), [[16, 4], [0, 2], [1, 16]], 0, R("cb", 256, 384, p1=64))
    for q in range(8):
        pu = R(("pa1", "pb1")[q % 2])
        mm((pu, R("Dup", p1=64), R("z", 512 * q, 512 * q + 512, p1=64)))
        act(R("V0", V0 + 512 * q, V0 + 512 * q + 512), pu, AF.Identity)
    for s in range(2):
        S = str(s)
        mset(R("V" + S, 0, V0), 0.0)
        mset(R("V" + S, V0 + 4096, VW), 0.0)
        fill(R("O" + S, 56, 64), 0)
        fill(R("Rm" + S, 64, 72), -1)
        fill(R("ab" + S, 66, 2 * SEG), 64)
    perm(R("SW0"), [[32, 5], [-1000, 2], [1, 16]], 1000)
    perm(R("SW1"), [[32, 5], [1000, 2], [1, 16]], -16)
    mset(R("m8"), 1.0)
    mset(R("m8", 0, CW, 8), 0.0)
    mset(R("Q", 0, 16), 0.0)
    turn = [0]
    act(R("Ib"), R("If"), AF.Identity)
    act(R("nIb"), R("If"), AF.Identity, 0.0, -1.0)
    iota(R("rows", 160, 304), [[1, 9], [-BIG, 2], [0, 8]], BIG)
    ts(R("VB"), R("rows", 160, 304), col["blk"], 65536.0, ALU.is_equal, ALU.mult)
    act(R("nVB"), R("VB"), AF.Identity, 0.0, -1.0)
    mset(R("YC", 0, 32), 8.5 * 65536)
    mset(R("YC", 32, 64), -8.5 * 65536)
    mset(R("CK"), 4096.0)
    mset(R("CK", 0, 512, 16), -2.0 ** 26)
    act(R("o64"), R("ones", 0, 128), AF.Identity, 0.0, 1.0 / 64)
    fill(R("m16"), 1)
    fill(R("m16", 0, 64, 16), 0)
    iota(R("rows", 304, 448), [[1, 9], [-BIG, 16]], 15 * BIG)
    ts(R("WW"), R("rows", 304, 448), col["blk"], None, ALU.is_equal)
    iota(R("rows", 704, 736), [[32, 32]], 30)
    ubase = R("sm", 0, 32)
    act(ubase, R("rows", 704, 736), AF.Identity, col["b"])
    ts(R("pf", 10, 11), col["r15"], -0.125, 0.875, ALU.mult, ALU.add)
    ts(R("pf", 11, 12), col["r15"], 15.0, OFF, ALU.is_equal, ALU.mult)
    ts(R("pf", 12, 13), R("pf", 10, 11), 0.0, R("pf", 11, 12), ALU.max, ALU.add)
    act(R("TB"), R("ones", 0, 64), AF.Identity, R("pf", 12, 13), 0.0)
    fill(R("cb", 0, 128), -8192)
    fill(R("cb", 128, 256), -2 ** 21)
    fill(R("cb", 384, 448), 2 ** 15)
    fill(R("cb", 448, 456), 2 ** 19)
    for b in range(2):
        perm(R("Nb", 128 * b, 128 * b + 128), [[16, 8], [1000, 2], [1, 8]], 8 * b, R("cb", 0, 128))
        perm(R("Nb", 128 * b + 15, 128 * b + 128, 16), [[16, 8]], 8 * b, R("cb", 448, 456))
        perm(R("Mp", 144 * b, 144 * b + 144), [[16, 9], [-1000, 2], [1, 8]], 1000 + 8 * b)
        tt(R("Md", 128 * b, 128 * b + 128), R("Mp", 144 * b, 144 * b + 128), R("Mp", 144 * b + 1, 144 * b + 129), ALU.subtract)
    fill(R("Md", 7, 256, 16), 0)
    fill(R("m2"), 0)
    fill(R("m2", 7, 64, 16), -2)
    perm(R("Z0"), [[4, 33], [-1000, 2], [1, 2]], 1000)
    perm(R("Z1"), [[4, 33], [1000, 2], [1, 2]], -2)
    iota(R("rows", 448, 576), [[1, 4], [0, 32]], 0)
    ts(R("Bn"), R("rows", 448, 576), col["G"], -8192.0, ALU.is_equal, ALU.mult)
    fill(R("rows", 576, 704), -8192)
    for x in range(2):
        perm(R("Row", 128 * x, 128 * x + 128), [[32, 4], [0, 32]], 16 * x + 6, R("rows", 576, 704))
    for ht in range(2):
        perm(R("Hs", 128 * ht, 128 * ht + 128), [[32, 4], [0, 2], [1, 16]], 16 * ht)
        perm(R("Hb", 128 * ht, 128 * ht + 128), [[32, 4], [0, 2], [1, 16]], 16 * ht, R("cb", 128, 256))
    fill(R("mseg"), 0)
    fill(R("mseg", 0, 4 * SEG, SEG), 1 << 23)
    act(R("pf", 13, 14), col["b0"], AF.Identity, 0.0, 16.0 * 8192)
    act(R("pf", 14, 15), col["B10"], AF.Identity, R("pf", 13, 14), 2.0 * 8192)
    for par in range(2):
        wx, wy = ((1, 32), (32, 1))[par]
        a = (SEG + 6) * par
        iota(R("LR", a, a + 2), [[32767, 2]], 0)
        for c in range(4):
            iota(R("LR", a + 2 + 64 * (c // 2) + c % 2, a + 66 + 64 * (c // 2), 2), [[-64, 8], [-32 * wy, 2], [-512, 2]], -32 * (64 * (c // 2) + wx * (c % 2) + 1))
        for w in range(2):
            iota(R("rows", 16 * par + 8 * w, 16 * par + 8 * w + 8), [[64, 2], [wx, 2], [8, 2]], 1)
        act(R("pf", 15 + par, 16 + par), col["y"], AF.Identity, R("pf", 14, 15), 8192.0 * wy)
        act(R("LK", 16 * par, 16 * par + 16), R("rows", 16 * par, 16 * par + 16), AF.Identity, R("pf", 15 + par, 16 + par), 8192.0)
    iota(R("rows", 776, 792), [[16, 16]], V0 + 4096)
    dum = R("sm", 32, 48)
    act(dum, R("rows", 776, 792), AF.Identity, col["r15"])
    iota(R("rows", 32, 36), [[16, 4]], 7)
    act(R("pf", 17, 18), col["b"], AF.Identity, 0.0, 64.0)
    ts(R("sm", 48, 52), R("rows", 32, 36), R("pf", 17, 18), 64.0, ALU.add, ALU.min)
    keep(R("su", 0, 4), R("sm", 48, 52))
    for u in range(2):
        perm(R("Out", 64 * u, 64 * u + 64), [[32, 4], [1, 16]], 16 * u)
        perm(R("Out", 128 + 64 * u, 192 + 64 * u), [[2, 64]], u)

    def swap(o, i, name):
        for y in range(2):
            mm(*[(R(o[0], o[1] + y, o[2], 2), R("SW%d" % y, 16 - 16 * (x - y), 144 - 16 * (x - y)), R(name, i[0] + x, i[1], 2)) for x in range(2)])

    def stream(s):
        S = str(s)

        def r(name, *a, **k):
            return R(name + S, *a, **k)
        Vw, Vm = r("V"), r("V", V0, V0 + 4096)

        def clauses(src, bank, w, y):
            tr(r("f", 432 + 40 * w, 464 + 40 * w), src)
            act(r("f", 128 + 64 * w, 192 + 64 * w), ind(r("f", 432 + 40 * w, 465 + 40 * w), R("su", 8, 12)), AF.Identity)
            mm(*[(r(bank, 64, 128, 1, 0, 64), R("Out", 64 * u, 64 * u + 64), r("f", 128 + 64 * w, 192 + 64 * w)) for u in range(2)])
            act(r("tmp", 64 * w, 64 * w + 64, 1, 0, 64), r(bank, 64, 128, 1, 0, 64), AF.Identity)
            dmas("sp", [(y[64 * s:64 * s + 64, :], T["tmp" + S][0:64, 64 * w:64 * w + 64])], [r("tmp", 64 * w, 64 * w + 64)], [], "fin", 16e3)

        def edits(a):
            act(r("nv", 128, 256), ind(Vw, r("u", a + 8, a + 16)), AF.Relu, -32.0)
            ts(r("nv", 0, 128), ind(Vw, r("u", a, a + 8)), 32.0, 255.0, ALU.add, ALU.min)
        mm((r("pc", 0, 128), R("In" + S), R("cinf", 0, 128)))
        act(r("f", 128, 256), r("pc", 0, 128), AF.Identity)
        copy(r("f", 256, 320), ind(r("f", 128, 256), R("su", 4, 8)))
        tr(r("land", 40, 104), r("f", 256, 320))
        fill(r("f", 464, 512, 40), 0)
        for b in range(2):
            mm((r("pb", 32, 36), R("J", 1 + 128 * s - b, 129 + 128 * s - b), R("cinf", 128 + b, 136, 2)), start=b == 0, stop=b == 1)
        if s:
            act(r("land", 32, 36), r("pb", 32, 36), AF.Identity, OFF)
            act(r("f", 400, 404), r("land", 32, 36), AF.Identity, 2.0 ** 24)
            act(r("f", 404, 408), r("f", 400, 404), AF.Identity, -2.0 ** 25, 2.0)
        else:
            ts(r("land", 32, 36), r("pb", 32, 36), OFF, None, ALU.add)
            ts(r("f", 400, 404), r("land", 32, 36), 2.0 ** 24, -2.0 ** 24, ALU.add, ALU.add)
            ts(r("f", 404, 408), r("f", 400, 404), 2.0, None, ALU.mult)
        tt(r("land", 36, 40), r("f", 404, 408), r("land", 32, 36), ALU.subtract)
        for q, (a, b) in enumerate(PAR["pcut"][s]):
            ev = r("P", 2 * a, 2 * b, 2)
            tm = r("tmp", 512 * (q % 2), 512 * (q % 2) + b - a)
            pu = R(("pa0", "pd0")[q % 2] if s == 0 else "pd1", 0, b - a)
            if s:
                keep(ev, r("G", a, b))
                act(tm, ev, AF.Identity, 2.0 ** 25, 2.0 - 2.0 ** -12)
                ts(pu, tm, -2.0 ** 25, 1.0, ALU.add, ALU.add)
            else:
                ts(ev, r("G", a, b), -0.5, None, ALU.add)
                if q % 2:
                    act(tm, ev, AF.Identity, 2.0 ** 25, 2.0)
                    act(pu, tm, AF.Identity, -2.0 ** 25)
                else:
                    ts(tm, r("G", a, b), -0.5, 2.0 ** 24, ALU.add, ALU.add)
                    act(pu, tm, AF.Identity, -2.0 ** 25, 2.0)
            tt(r("P", 2 * a + 1, 2 * b, 2), pu, ev, ALU.subtract)
        thr = r("f", 416, 417)
        fill(thr, (2 * AT[0] - 17) * 2 ** 16)

        for t in range(RO):
            par = t % 2
            ctx["ts"] = (t, s)
            L0, M0 = t * LW, t * MW
            swap(("pb" + S, 0 if t else 32, 40), (L0 if t else 32, L0 + 40), "land" + S)
            ts(r("u", 0, 8), r("pb", 32, 40), 0.5, None, ALU.add)
            if t:
                if "d" in PAR["vec"]:
                    copy(r("land", L0 + 72, L0 + 104), r("pb", 0, 32))
                else:
                    act(r("land", L0 + 72, L0 + 104), r("pb", 0, 32), AF.Identity)
                if "f96" in PAR["vec"]:
                    ts(r("f", 96, 128), r("land", L0, L0 + 32), thr, None, ALU.add)
                else:
                    act(r("f", 96, 128), r("land", L0, L0 + 32), AF.Identity, thr)
            mm((r("pc", 0, 64), R("Ib"), R("YC")), stop=False)
            act(r("g1"), ind(Vw, r("u", 4, 8)), AF.Identity)
            tt(r("g2"), ind(Vw, r("u", 0, 4)), r("g1"), ALU.is_lt)
            mm(*[(r("pc", 32 * w, 32 * w + 32), R(("nVB", "VB")[w], 8 - 8 * b, 136 - 8 * b), r("g2", b, 64, 2)) for w in range(2) for b in range(2)], start=False)
            tt(r("f", 0, 64), r("land", L0 + 40, L0 + 104), r("pc", 0, 64), ALU.min)
            C = r("msg", M0, M0 + 32)
            tt(r("u", 16, 48), r("f", 0, 32), r("f", 32, 64), ALU.max)
            keep(C, r("u", 16, 48))
            cuts = PAR["turn"]
            for a, b in zip(cuts, cuts[1:]):
                ts(r("img", a, b), ind(r("P"), r("u", 16 + a // 16, 16 + b // 16)), 0.0 if s else 0.5, None, ALU.add)
                tr(r("of", a, b), r("img", a, b))
            for a, b in zip(PAR["lits"], PAR["lits"][1:]):
                keep(r("imT", a, b), r("of", a, b))
            if t == 0:
                swap(("pd" + S, 32, 64), (72, 104), "land" + S)
                act(r("f", 96, 128), r("pd", 32, 64), AF.Identity, thr)
            if t + 1 == RO:
                swap(("pd" + S, 32, 64), (M0, M0 + 32), "msg" + S)
                clauses(r("pd", 32, 64), "pd", 1, T.yd)
            mm((r("pc", 64, 128), R("Ib"), R("TB")), (r("pc", 64, 128), R("WW", 0, 128), R("cb", 384, 448)), stop=False)
            kind = "last" if (t, s) == (RO - 1, 1) else "all"
            gs, qs, zs = [cut(x) for x in PAR["main"][kind]]
            for q, (a0, aw, _) in enumerate(cut(PAR["subs"][kind])):
                u0, u1 = a0 // 8, (a0 + aw) // 8
                pa, kb = "pa%d" % (turn[0] % 2), ("pb", "pd")[q % 2]
                turn[0] += 1
                kv = r(kb, u0 // 2, u1 // 2)
                for a in range(u0 // 2, u1 // 2, PAR["piece"]):
                    b = min(a + PAR["piece"], u1 // 2)
                    mm((r(kb, a, b), R("If"), r("imT", a, b)), start=a == u0 // 2, stop=False)

                low = [a0]

                def seconds(upto):
                    while zs and zs[0][0] + zs[0][1] <= upto:
                        a, cw, _ = zs.pop(0)
                        scan(R("z", a, a + cw), R("w", a, a + cw), R("Q", a + 15, a + 15 + cw), ALU.max, ALU.min)
                        if a + cw - low[0] >= PAR["gaps"] or a + cw == a0 + aw or zs[0][0] + zs[0][1] == a0 + aw:
                            mm((R(pa, low[0] // 8 - u0, (a + cw) // 8 - u0), R("nIb"), R("z", low[0] + 7, a + cw, 8)), start=False, stop=a + cw == a0 + aw)
                            low[0] = a + cw
                while qs and qs[0][0] < a0 + aw:
                    a, cw, _ = qs.pop(0)
                    while gs and gs[0][0] < a + cw:
                        b, gw, vec = gs.pop(0)
                        src = ind(Vm, r("of", b // 16, (b + gw) // 16))
                        if vec:
                            copy(R("w", b, b + gw), src)
                        else:
                            act(R("w", b, b + gw), src, AF.Identity)
                    scan(R("Q", a + 16, a + 16 + cw), R("m8", 0, cw), R("w", a, a + cw), ALU.mult, ALU.max)
                    top = R("Q", a + 23, a + 16 + cw, 8)
                    mm((R(pa, a // 8 - u0, (a + cw) // 8 - u0), R("Ib"), top), start=a == a0, stop=False)
                    fill(top, 0)
                    seconds(a)
                seconds(a0 + aw)
                act(r("usg", u0, u1), R(pa, 0, u1 - u0), AF.Sign, -MT[t] - 0.5)
                mm(*[(kv, R("VB", 8 - 8 * b, 136 - 8 * b), r("usg", u0 + b, u1, 2)) for b in range(2)], start=False)
                scan(r("ks", u0 // 2, u1 // 2), R("CK", u0 // 2, u1 // 2), kv, ALU.add, ALU.max)
            for v in range(2):
                for u in range(2):
                    mm((r("pd", v, 8, 2), R("Z%d" % v, 2 - 2 * (u - v), 130 - 2 * (u - v)), r("land", L0 + 32 + u, L0 + 40, 2)), start=u + v == 0, stop=False)
            km, nC = r("n", 0, 32), r("n", 32, 64)
            best = r("ks", 15, 512, 16)
            tt(km, best, r("f", 96, 128), ALU.max)
            ts(r("n", 96, 128), km, 11, 30, ALU.logical_shift_right, ALU.bitwise_and)
            ts(nC, km, 4095, None, ALU.bitwise_and)
            tt(r("u", 80, 112), ubase, r("n", 96, 128), ALU.subtract)
            keep(r("u", 48, 80), nC)
            stay, cnt = r("sg", 0, 32), r("f", 424, 425)
            act(stay, best, AF.Sign, thr, -1.0, acc=cnt)
            for a, b, _ in cut(PAR["sums"][kind]):
                act(r("um", a, a + b), ind(r("usg"), r("u", 80 + a // 16, 80 + (a + b) // 16)), AF.Relu)
                tt(r("pr", a, a + b), ind(Vm, r("u", 48 + a // 16, 48 + (a + b) // 16)), r("um", a, a + b), ALU.mult)
            new = r("msg", M0 + 40, M0 + 72)
            keep(new, nC)
            if t + 1 == RO:
                clauses(new, ("pb", "pa")[s], 0, T.yc)
            else:
                mm((r("pb", 40, 41), R("Bn"), cnt))
                if "sg" in PAR["vec"]:
                    ts(r("sg", 32, 33), r("pb", 40, 41), -1.0, -319.75 * 2 ** 17, ALU.mult, ALU.add)
                else:
                    act(r("sg", 32, 33), r("pb", 40, 41), AF.Identity, -319.75 * 2 ** 17, -1.0)
                ts(thr, r("sg", 32, 33), 320.0 * 2 ** 17 + (2 * AT[t + 1] - 17) * 2 ** 16, r("pb", 40, 41), ALU.add, ALU.add)
            mm(*[(r("pc", 64 + b, 128, 2), R("Nb", 128 * b, 128 * b + 128), stay) for b in range(2)], start=False, stop=False)
            for b in range(2):
                mm((r("pc", 64 + b, 128, 2), R("Md", 128 * b, 128 * b + 128), new), start=False, stop=False)
            mm(*[(r("pc", 64, 128), R("WW", 15 - k, 143 - k), r("pr", k, 512, 8)) for k in range(8)], start=False)
            tr(r("f", 256, 320), r("pc", 64, 128))
            scan(r("Rm", 0, 64), R("m16", 0, 64), r("f", 256, 320), ALU.mult, ALU.max)
            tt(r("f", 320, 384), ind(r("Rm"), R("su", 0, 4)), r("f", 256, 320), ALU.not_equal)
            scan(r("O", 0, 56), r("f", 320, 376), r("f", 264, 320), ALU.mult, ALU.add)
            ts(r("O", 6, 56, 16), r("O", 7, 56, 16), 2.0 ** 24, -2.0 ** 24, ALU.add, ALU.add)
            tr(r("X"), r("O", 0, 64))
            scan(r("O", 70, 120), R("m2", 6, 56), r("O", 6, 56), ALU.mult, ALU.subtract)
            ll = r("O", 7, 120, 16)
            mm(*[(r("pd", 4 * w, 4 * w + 4), R("If"), r("Rm", 7, 64, 16)) for w in range(2)], start=False)
            tt(r("msg", M0 + 32, M0 + 40), ll, r("pd", 0, 8), ALU.min)
            if t + 1 < RO:
                src, la = r("msg", M0, M0 + MW), r("land", L0 + LW, L0 + LW + MW)
                rid, pid, _ = topo.addr(dst)
                en = topo.engines(core, dst)[:ENG]
                mask = sum(1 << e for e in en)
                sem = "arr%d_%d" % (t + 1, s)

                def send(src=src, la=la, sem=sem, mask=mask, rid=rid, pid=pid):
                    g.remote_dma(la[0], src[0], T.sem[sem], T.sem.sent, pid, rid, mask)
                op("pool", send, [src], [la], "rem", len(en), sem=sem, cnt=len(en))
            a = (SEG + 6) * par
            mm((r("pc", 128, 128 + SEG), R("Ib"), R("LR", a, a + SEG)), stop=False)
            mm(*[(r("pc", 130 + x, 128 + SEG, 2), R("Row", 128 * x, 128 * x + 128), r("X")) for x in range(2)], start=False)
            for c in (3, 2, 1, 0):
                wd = 2 + 64 * (c // 2 + 1)
                act(r("ab", SEG * c, SEG * c + wd), r("pc", 128, 128 + wd), AF.Abs, r("O", 6 + 16 * c, 7 + 16 * c), 1.0 / 8192)
            end = (t, s) == (RO - 1, 1)
            if end:
                for ht in range(2):
                    mm((r("pb", 48 + ht, 64, 2), R("Hs", 128 * ht, 128 * ht + 128), ll))
                ts(r("u", 112, 128), r("pb", 48, 64), 0.5, float(VW - 1), ALU.add, ALU.min)
                edits(112)
            if t + 1 == RO:
                for b in range(2):
                    mm((r("pb", 192 + b, 200, 2, 0, 64), R("Out", 128 + 64 * b, 192 + 64 * b), r("msg", M0 + 32, M0 + 36)))
                act(r("tmp", 128, 136, 1, 0, 64), r("pb", 192, 200, 1, 0, 64), AF.Identity, -OFF)
                dmas("sp", [(T.yl[64 * s:64 * s + 64, :], T["tmp" + S][0:64, 128:136])], [r("tmp", 128, 136)], [], "fin", 2e3)
            mm((r("pd", 16, 32), R("Ib"), R("LK", 16 * par, 16 * par + 16)), (r("pd", 16, 32), R("o64", p1=32), R("cb", 256, 272, p1=32)), stop=False)
            for ht in range(2):
                mm((r("pd", 16 + ht, 32, 2), R("Hs", 128 * ht, 128 * ht + 128), ll), start=False, stop=False)
            scan(r("mn"), R("mseg"), r("ab"), ALU.add, ALU.min)
            mm(*[(r("pd", 16 + 8 * w + ht, 24 + 8 * w, 2), R("Hb", 128 * ht, 128 * ht + 128), r("mn", SEG - 1, 4 * SEG, SEG))
                 for w in range(2) for ht in range(2)], start=False)
            tt(r("u", 128, 144), r("pd", 16, 32), dum, ALU.min)
            if not end:
                edits(128)
            copy(ind(Vw, r("u", 128, 144)), r("nv"))
            ctx["ts"] = None
            if t + 1 < RO:
                yield
        V = T["V" + S]
        for h in range(2):
            dmas("sp" if h == 0 else "act",
                 [(T.yv[64 * s + 16 * G:64 * s + 16 * G + 16, 2048 * h:2048 * h + 2048],
                   V[32 * G + 16 * h:32 * G + 16 * h + 16, V0 + 2048 * h:V0 + 2048 * h + 2048]) for G in range(4)], [Vw], [], "fin", 1 << 18)

    both = [stream(0), stream(1)]
    for t in range(RO):
        for s in range(2):
            next(both[s], None)
    last = {}
    for o in ops:
        dep = set()
        acc = [(x, False) for x in o["rd"]] + [(x, True) for x in o["wr"]]
        for (nm, a, b), w in acc:
            bank = SCRATCH[nm][0] == "psum"
            if bank:
                a, b = 0, 512
            wrote, read = last.setdefault(nm, ([], []))
            for a2, b2, j in wrote + (read if w or bank else []):
                if a < b2 and a2 < b and j != o["i"] and (w or (a2, b2, j) in wrote or ops[j]["e"] != o["e"]):
                    dep.add(j)
        for (nm, a, b), w in acc:
            if SCRATCH[nm][0] == "psum":
                a, b = 0, 512
            if w:
                for lst in last[nm]:
                    lst[:] = [e for e in lst if not (a <= e[0] and e[1] <= b)]
            last[nm][0 if w else 1].append((a, b, o["i"]))
        o["dep"] = sorted(dep)
        o["after"] = []
    for e, names in (("act", "w"), ("dve", "Qz")):
        line = [o for o in ops if o["e"] == e and o["ts"] and o["wr"][0][0] in names]
        for a, b in zip(line, line[1:]):
            b["after"].append(a["i"])
    return ops


def table(ops, c):
    out = []
    for o in ops:
        k, a = o["k"], o["n"]
        dep = [(j, -c["fix"] if o["e"] == "pe" and ops[j]["e"] == "pe" else c["lat"]) for j in o["dep"]] + [(j, 0.0) for j in o["after"]]
        if k == "dma":
            out.append((o["e"], 0.06 * a[0], c["dma"], a[1] / c["bw"], dep))
        elif k == "rem":
            out.append((o["e"], c["hold"], c["rem"], 0.0, dep))
        elif k == "pe":
            d = a[0] * c["cyc"] + a[1] * c["mm"]
            out.append((o["e"], d, d + c["fix"], 0.0, dep))
        else:
            d = c["fix"] + c["act"] * (o["e"] == "act") + a * c["cyc"] * (c[k] if k != "cyc" else 1)
            out.append((o["e"], d, d, 0.0, dep))
    return out


def plan(ops, tab, look):
    n = len(ops)
    users = [[] for o in ops]
    for i in range(n):
        for j, l in tab[i][4]:
            users[j].append((i, l))
    rest = [0.0] * n
    for i in range(n - 1, -1, -1):
        rest[i] = tab[i][2] + tab[i][3] + max([0.0] + [l + rest[j] for j, l in users[i]])
    left = [len(x[4]) for x in tab]
    head = [min(i for i in range(n) if ops[i]["wr"] and ops[i]["wr"][0][0] == "w")]
    for i in head:
        rest[i] += 50.0
        head.extend(j for j, l in tab[i][4] if j not in head)
    for i in range(n):
        if tab[i][3] and not left[i]:
            rest[i] = 1e6 - i
    free, dma, at, order, start = {}, 0.0, [0.0] * n, [], [0.0] * n
    rdy = {i: 0.0 for i in range(n) if not left[i]}
    while rdy:
        est = {i: max(v, free.get(tab[i][0], 0.0)) for i, v in rdy.items()}
        i0 = min(est, key=lambda i: (est[i], -rest[i]))
        e = tab[i0][0]
        i = max((i for i in est if tab[i][0] == e and est[i] <= est[i0] + look), key=lambda i: (rest[i], -i))
        start[i], free[e], done = est[i], est[i] + tab[i][1], est[i] + tab[i][2]
        if tab[i][3]:
            dma = done = max(dma, done) + tab[i][3]
        del rdy[i]
        order.append(i)
        for j, l in users[i]:
            at[j] = max(at[j], done + l)
            left[j] -= 1
            if left[j] == 0:
                rdy[j] = at[j]
    return order, start, order.index(head[0])


def in_order(order, pre):
    seen, out = [False] * len(order), []
    for i in order:
        st = [i]
        while st:
            x = st[-1]
            m = [j for j in pre[x] if not seen[j]]
            if m:
                st.extend(m)
            else:
                st.pop()
                if not seen[x]:
                    seen[x] = True
                    out.append(x)
    return out


def walk(tab, order):
    n = len(tab)
    done, why, free, prev, dma = [0.0] * n, [0] * n, [0.0] * (n + 1), dict.fromkeys(QUEUES, n), 0.0
    for i in order:
        e, hold, rdy, wire, dep = tab[i]
        w = prev[e]
        t, w = free[w], -1 - w
        for j, l in dep:
            if done[j] + l >= t:
                t, w = done[j] + l, j
        why[i], free[i], prev[e] = w, t + hold, i
        if wire:
            dma = done[i] = max(dma, t + rdy) + wire
        else:
            done[i] = t + rdy
    return max(done), done, why


def place(line, t, h):
    a, b = line
    lo, hi = 0, len(b)
    while lo < hi:
        mid = (lo + hi) // 2
        if b[mid] <= t:
            lo = mid + 1
        else:
            hi = mid
    while lo < len(a) and a[lo] < t + h - 1e-9:
        t = max(t, b[lo])
        lo += 1
    a.insert(lo, t)
    b.insert(lo, t + h)
    return t


def tighten(ops, tabs, tab, look, seed):
    n = len(ops)
    order, start, cut = plan(ops, tab, look)
    res = ["dma" if x[3] else x[0] for x in tab]
    hold = [x[3] or x[1] for x in tab]
    lead = [x[2] if x[3] else 0.0 for x in tab]
    done = [x[3] or x[2] for x in tab]
    pre = [[(j, done[j] + lead[i] + l) for j, l in tab[i][4]] for i in range(n)]
    suc = [[] for i in range(n)]
    for i in range(n):
        for j, d in pre[i]:
            suc[j].append((i, d))
    pre0, suc0 = [[j for j, d in p] for p in pre], [[j for j, d in p] for p in suc]
    head = [n] * n
    for q, i in enumerate(order[:cut]):
        head[i] = q
    seed = [seed]

    def draw():
        seed[0] = (seed[0] * 1103515245 + 12345) % 2147483648
        return seed[0] / 2147483648.0
    norm = [walk(x, order)[0] * len(tabs) for x in tabs]
    best, span = 1.0, max(start)
    for step in range(PAR["shakes"]):
        a, w, j = draw() * (span + 10) - 10, (3, 8, 20)[int(draw() * 3)], (0.2, 0.6, 1.6)[int(draw() * 3)]
        st = [x + j * (draw() + draw() + draw() - 1.5) if a < x < a + w else x for x in start]
        back, lines = [0.0] * n, {}
        for i in in_order(sorted(range(n), key=lambda i: (-(st[i] + hold[i]), -i)), suc0):
            t = max([0.0, done[i] - hold[i]] + [back[k] + hold[k] + d - hold[i] for k, d in suc[i]])
            back[i] = place(lines.setdefault(res[i], ([], [])), t, hold[i])
        lines = {}
        for i in in_order(sorted(range(n), key=lambda i: (head[i], -(back[i] + hold[i]), i)), pre0):
            st[i] = place(lines.setdefault(res[i], ([], [])), max([lead[i]] + [st[j] + d for j, d in pre[i]]), hold[i])
        new = in_order(sorted(range(n), key=lambda i: (head[i], st[i] - lead[i], i)), pre0)
        v = sum(walk(x, new)[0] / m for x, m in zip(tabs, norm))
        if v <= best + 0.0002:
            best, start, order = v, st, new
    return order


def part(tabs, ids):
    new = {i: q for q, i in enumerate(ids)}
    above, direct = [0] * len(ids), [None] * len(ids)
    for q in sorted(range(len(ids)), key=lambda q: ids[q]):
        dep = [new[j] for j, l in tabs[0][ids[q]][4] if j in new]
        far = 0
        for j in dep:
            far |= above[j]
        direct[q] = set(j for j in dep if not far >> j & 1)
        for j in dep:
            far |= 1 << j
        above[q] = far
    out = []
    for tab in tabs:
        rows = []
        for q, i in enumerate(ids):
            e, hold, rdy, wire, dep = tab[i]
            lat = {}
            for j, l in dep:
                if j in new and new[j] in direct[q]:
                    lat[new[j]] = max(l, lat.get(new[j], -1.0))
            rows.append((QUEUES.index(e), hold, rdy, wire, tuple(lat.items())))
        out.append(rows)
    return out


def run(tab, order, at, old, goal):
    done, begin, free = old[1][:], old[2][:], [-1.0] * 5
    q, left, dma = at, 4, max([0.0] + [done[i] for i in old[3] if old[4][i] < at])
    while q and left:
        q -= 1
        i = order[q]
        e = tab[i][0]
        if free[e] < 0:
            free[e] = begin[i] + tab[i][1]
            left -= e < 4
    free = [max(x, 0.0) for x in free]
    for i in order[at:]:
        e, hold, rdy, wire, dep = tab[i]
        t = free[e]
        for j, l in dep:
            j = done[j] + l
            if j > t:
                t = j
        begin[i] = t
        free[e] = t + hold
        if wire:
            dma = done[i] = max(dma, t + rdy) + wire
        else:
            done[i] = t + rdy
        if i == goal:
            return t + rdy, done, begin, old[3], old[4]
    return max(done), done, begin, old[3], old[4]


def chain(tab, order, res, goal, lo, hi):
    end, done, begin, wires, spot = res
    i, pairs = goal if goal is not None else done.index(end), []
    while spot[i] > lo:
        t = begin[i] - 1e-9
        for j, l in tab[i][4]:
            if done[j] + l >= t:
                break
        else:
            q, e = spot[i] - 1, tab[i][0]
            while q >= 0 and tab[order[q]][0] != e:
                q -= 1
            if q < lo:
                break
            j = order[q]
            if q < hi:
                pairs.append((j, i))
        i = j
    return pairs


def settle(tabs, order, goal, steps, heat, seed, lo=0, hi=1 << 30, key=None):
    n, m = len(order), len(tabs)
    pre = [set(j for j, l in x[4]) for x in tabs[0]]
    spot = [0] * n
    for q, x in enumerate(order):
        spot[x] = q
    zero = (0.0, [0.0] * n, [0.0] * n, [i for i in range(n) if tabs[0][i][3]], spot)
    res = [run(x, order, 0, zero, goal) for x in tabs]
    norm = [x[0] * m for x in res]
    now, low, best, ends = 1.0, 1.0, key or order, [x[0] for x in res]
    per = len(key) if key else 0
    if per:
        lo = sum(key[q % per] + q - q % per < max(key) - per + 30 for q in range(n))
    links = [None] * m
    for step in range(steps):
        seed = (seed * 1103515245 + 12345) % 2147483648
        q = (seed >> 8) % m
        if links[q] is None:
            links[q] = chain(tabs[q], order, res[q], goal, lo, hi)
        if not links[q]:
            continue
        seed = (seed * 1103515245 + 12345) % 2147483648
        a, b = links[q][(seed >> 8) % len(links[q])]
        ia, ib, how = spot[a], spot[b], seed >> 28
        if how < 2 and not per:
            b, ib, ia = a, ia, max([lo] + [spot[j] + 1 for j in pre[a]])
            a = order[ia]
        elif a in pre[b] or ib - ia > 150:
            continue
        seg = order[ia:ib + 1]
        if how < 5 - (per > 0):
            grp, need = {b}, set(pre[b])
            for x in reversed(seg[:-1]):
                if x in need:
                    grp.add(x)
                    need |= pre[x]
            turned = [x for x in seg if x in grp] + [x for x in seg if x not in grp]
        else:
            grp = {a}
            for x in seg[1:]:
                if pre[x] & grp:
                    grp.add(x)
            turned = [x for x in seg if x not in grp] + [x for x in seg if x in grp]
        if a in grp and b in grp:
            continue
        new, changed = order[:], []
        for d in range(-n + per, n, per) if per else (0,):
            here = [spot[x + d] for x in seg if 0 <= x + d < n]
            changed += here
            for q, y in zip(here, [y + d for y in turned if 0 <= y + d < n]):
                new[q] = y
        seed = (seed * 1103515245 + 12345) % 2147483648
        room = -heat * (1 - step / steps) * math.log((seed + 1) / 2147483648.0)
        v, got, ia = 0.0, [], min(changed)
        for q in range(m):
            got.append(run(tabs[q], new, ia, res[q], goal))
            v += (got[q][0] - res[q][0]) / norm[q]
            if v > room + 0.002 * (m - 1 - q) / m:
                break
        else:
            now, order, res, links = now + v, new, got, [None] * m
            if per:
                old, key = key, key[:]
                for x, y in zip(seg, turned):
                    key[y % per] = old[x % per] + x - x % per - y + y % per
            for q in changed:
                spot[order[q]] = q
            if now < low:
                low, best, ends = now, key if per else new, [x[0] for x in res]
    return best, ends


def fittest(tries, stages, step):
    for keepers, steps, heat in stages:
        got = [step(x, steps, heat, PAR["seed"] + q) for q, x in enumerate(tries)]
        tries = [x[0] for x in sorted(got, key=lambda x: sum(a / b for a, b in zip(x[1], got[0][1])))[:keepers]]
    return tries[0]


def middle(ops, tabs, start, first):
    ids = [o["i"] for o in ops if o["ts"] and 1 <= o["ts"][0] <= 3]
    per = len(ids) // 3
    sub = part(tabs, ids)
    tries = []
    for t in range(1, RO - 1):
        span = start[first[t + 1, 0]] - start[first[t, 0]]
        at = [(start[ids[k] + (t - 1) * per] - start[first[t, 0]]) / span for k in range(per)]
        again = True
        while again:
            again = False
            for q in range(per, 2 * per):
                for j, l in sub[0][q][4]:
                    if j // per + at[j % per] >= 1 + at[q % per]:
                        at[q % per], again = j // per + at[j % per] - 1 + 1e-7, True
        key = [0] * per
        for q, k in enumerate(sorted(range(per), key=lambda k: (at[k] % 1, k))):
            key[k] = q + per * math.floor(at[k])
        tries.append(key)

    def step(key, steps, heat, seed):
        return settle(sub, sorted(range(3 * per), key=lambda q: key[q % per] + q - q % per), ids.index(first[3, 0]), steps, heat, seed, key=key)
    return ids, fittest(tries, PAR["middle"], step)


def arrange(ops):
    tabs = [table(ops, cost(m)) for m in SPREAD]
    tab = tabs.pop()
    n = len(ops)
    order = tighten(ops, tabs, tab, PAR["look"], PAR["seed"])
    done = walk(tab, order)[1]
    start = [done[i] - tab[i][2] - tab[i][3] for i in range(n)]
    first, seen, like = {}, {}, {}
    for o in ops:
        if o["ts"]:
            v = (o["ts"][1], o["e"], o["k"], o["n"]) + tuple((x[0], x[1] % {"land": LW, "msg": MW}.get(x[0][:-1], 1 << 20)) for x in o["wr"])
            seen[o["ts"], v] = seen.get((o["ts"], v), 0) + 1
            like[o["i"]] = v + (seen[o["ts"], v],)
            if o["wr"] and o["wr"][0][0] == "w":
                first.setdefault(o["ts"], o["i"])
    ids, key = middle(ops, tabs, start, first)
    per = len(key)
    spot = {like[ids[k]]: key[k] for k in range(per)}
    zero, span = spot[like[first[1, 0]]], start[first[3, 0]] - start[first[2, 0]]
    loads = sum(o["k"] == "dma" and not o["dep"] for o in ops)
    at, last, soon = [0.0] * n, {}, plan(ops, tab, PAR["look"])[1]
    for o in ops:
        i = o["i"]
        if i < loads:
            at[i] = i - 1e9
        elif i < first[0, 0] or not o["ts"]:
            at[i] = zero + (soon[i] - soon[first[0, 0]]) / span * per if soon[i] < soon[first[2, 0]] else 1e9
        elif like[i] in spot:
            last[o["ts"]] = at[i] = spot[like[i]] + per * o["ts"][0]
        else:
            at[i] = last.get(o["ts"], min(key) + per * o["ts"][0]) + 0.5
    full = in_order(sorted(range(n), key=lambda i: (at[i], i)), [[j for j, l in x[4]] for x in tab])
    was = {i: q for q, i in enumerate(order)}
    b, c, hi = full.index(first[2, 1]) + 1, full.index(first[1, 0]), full.index(first[1, 1])
    sub = part(tabs, full[:b])
    tries = [list(range(b)), sorted(range(c), key=lambda q: was[full[q]]) + list(range(c, b))]
    full[:b] = [full[q] for q in fittest(tries, PAR["start"], lambda x, steps, heat, seed: settle(sub, x, b - 1, steps, heat, seed, loads, hi))]
    a, c, lo = full.index(first[RO - 3, 1]), full.index(first[RO - 1, 0]), full.index(first[RO - 2, 1])
    sub = part(tabs, full[a:])
    tries = [list(range(n - a)), list(range(c - a)) + sorted(range(c - a, n - a), key=lambda q: was[full[a + q]])]
    full[a:] = [full[a + q] for q in fittest(tries, PAR["end"], lambda x, steps, heat, seed: settle(sub, x, None, steps, heat, seed, lo - a))]
    return full


ORDER = []


def rank_program(g, core, T, topo):
    if T.rank_of(core) is None:
        return
    ops = build(g, core, T, topo)
    if not ORDER:
        ORDER.extend(arrange(ops))
    queue = {"act": g.scalar, "dve": g.vector, "pe": g.tensor, "pool": g, "sp": g.sync}
    need = set()
    for o in ops:
        for j in o["dep"]:
            if not (o["e"] == "pe" and ops[j]["e"] == "pe"):
                need.add(j)
    mark, count, total, knew, when = {}, {}, {"fin": 0, "sent": 0}, {}, {}
    seen = {e: {} for e in queue}
    for i in ORDER:
        o = ops[i]
        e = o["e"]
        want = {}
        for j in o["dep"]:
            if not (e == "pe" and ops[j]["e"] == "pe"):
                sem, v = mark[j]
                want[sem] = max(want.get(sem, (0, 0)), (v, j))
        for sem, (v, j) in sorted(want.items(), key=lambda x: -when[x[1][1]]):
            if seen[e].get(sem, 0) < v:
                queue[e].wait_ge(T.sem[sem], v)
                seen[e][sem] = v
                for sem, v in knew[j].items():
                    seen[e][sem] = max(seen[e].get(sem, 0), v)
        knew[i] = dict(seen[e]) if o["k"] != "rem" else {}
        when[i] = len(when)
        ins = o["fn"]()
        if o["sem"] is not None:
            mark[i] = (o["sem"], o["cnt"])
            if o["k"] == "rem":
                total["sent"] += o["cnt"]
            elif o["sem"] == "fin":
                total["fin"] += o["cnt"]
        elif i in need:
            count[e] = count.get(e, 0) + 1
            ins.then_inc(T.sem[e], 1)
            mark[i] = (e, count[e])
    g.wait_ge(T.sem.sent, total["sent"])
    g.sync.wait_ge(T.sem.fin, total["fin"])
